import numpy as np, ml_dtypes
CORES = [66,74,82,90,194,202,210,218]
N = 8
BF = ml_dtypes.bfloat16
W, K, LP, CAP, PR = 2048, 4096, 2, 256, 8
XS = (4, 3)
MP = K >> LP
def coefs(rng, lo, hi):
    o = np.argsort(rng.random((8, 16, 16)), axis=1)
    v = rng.integers(1, 4, (8, 16, 16)) * np.where(o == 0, 1, np.where(o == 1, -1, 2 * rng.integers(0, 2, (8, 16, 16)) - 1))
    return np.where(o < rng.integers(lo, hi + 1, (8, 1, 16)), v, 0)
def rays(rng, top, dens):
    v = np.floor(rng.random((N, 8, 16, W)) * (np.reshape(top, (1, 8, 1, 1)) + 1.0))
    return (v * (rng.random((N, 8, 16, W)) < dens)).astype(np.int64)
def plant(rng, nn, pz, order, full=False, odd=()):
    c = coefs(rng, 6, 10); x = rng.integers(0, 16, (N, 8, 16, W))
    P = np.argsort(rng.random((8, 16)), axis=1); M = rng.integers(0, 16, 8)
    if full: x[:, 1::2] = np.floor(np.exp2(7.9 * rng.random((N, 4, 16, W)))).astype(np.int64)
    for g in range(8):
        m = M[g]; a, b, e = P[g, :3]; w = int(rng.integers(1, 4))
        if full or g in odd:
            c[g] = 2 * np.sign(c[g]); c[g, e] = rng.choice(np.array([-3, -1, 1, 3]), 16); x[:, g, e] |= 1
        c[g, :, m] = 0; c[g, a, m] = w; c[g, b, m] = -w
        for r in range(N):
            sg = np.zeros(W, np.int64); sg[:int(nn[r, g])] = -1; sg[W - int(pz[r, g]):] = 1
            if order[g] == 0: sg = rng.permutation(sg)
            if order[g] == 2: sg = sg[::-1]
            lo = rng.integers(0, 8, W); d = rng.integers(1, 8, W)
            if full: d = np.where(sg > 0, 7, 1)
            x[r, g, a] = lo + np.where(sg > 0, d, 0); x[r, g, b] = lo + np.where(sg < 0, d, 0)
    return x, c, P, M
def pack(x, c):
    return {"x": np.ascontiguousarray(x.reshape(N, 128, W)).astype(np.float32).astype(BF), "q": np.stack([c.reshape(128, 16)] * N).astype(np.int32)}
def setup_inputs(rng):
    top = rng.permutation(np.array([15, 15, 40, 40, 100, 100, 255, 255]))
    return pack(rays(rng, top, rng.choice(np.array([0.1, 0.3, 0.6, 1.0]), (N, 8, 16, 1))), coefs(rng, 2, 6))
def setup_inputs_room(rng):
    nn = rng.choice(np.array([0, 1, CAP - 1, CAP, CAP + 1, 2 * CAP]), (N, 8)); pz = rng.choice(np.array([0, 1, MP - 1, MP, MP + 1]), (N, 8))
    nn[0] = (CAP, CAP + 1, CAP - 1, CAP, 1, 0, 2 * CAP, CAP + 1); pz[0] = (MP, MP + 1, MP - 1, 1, MP, MP + 1, MP, 0)
    nn[XS[0]] = (2 * CAP, CAP, CAP + 1, CAP - 1, CAP, CAP, 1, CAP); pz[XS[0]] = (MP + 1, MP, MP, MP - 1, MP, MP + 1, MP, MP)
    x, c, P, M = plant(rng, nn, pz, np.zeros(8, np.int64))
    return pack(x, c)
def setup_inputs_full(rng):
    few = CAP + rng.integers(0, 64, (N, 8)); many = W - MP - rng.integers(72, 136, (N, 8))
    nn = np.where(np.array([0, 1, 1, 0, 0, 1, 1, 0]) == 1, many, few); pz = MP + rng.integers(0, 64, (N, 8))
    o = XS[0]; p = W // (2 ** LP + 1)
    nn[0, 0] = CAP; nn[o, 3] = CAP; pz[0, :2] = MP; nn[0, 2] = W - p; pz[0, 2] = p
    x, c, P, M = plant(rng, nn, pz, np.array([0, 0, 0, 0, 1, 1, 2, 2]), True)
    a, b, e, f0, f1, f2, f3 = P[2, :7]
    up = x[0, 2, a] > x[0, 2, b]; dn = x[o, 2, a] < x[o, 2, b]
    x[0, 2, a] = np.where(up, rng.integers(1, 16, W), 0); x[0, 2, b] = np.where(up, 0, rng.integers(2, 8, W))
    u = np.zeros(W, np.int64); u[up] = rng.permutation(4096)[:p]
    for k, v in ((f0, u >> 6), (f1, 63 - (u >> 6)), (f2, u & 63), (f3, 63 - (u & 63))):
        x[0, 2, k] = np.where(up, v, x[0, 2, k]); x[o, 2, k] = np.where(dn, 0, x[o, 2, k])
    x[o, 2, a] = np.where(dn, 0, x[o, 2, a]); x[o, 2, b] = np.where(dn, 1, x[o, 2, b])
    return pack(x, c)
def setup_inputs_ties(rng):
    c = coefs(rng, 2, 4); c[:, :, 8:] = -c[:, :, rng.permutation(8)]; c[0, :, 15] = 0; c[4, :, 0] = 0
    x = rays(rng, np.array([1, 1, 2, 2, 3, 1, 2, 15]), rng.choice(np.array([0.4, 0.6, 0.9]), (N, 8, 16, 1)))
    h = W // 2
    for g in (2, 5): x[:, g, :, h:] = x[:, g][:, :, rng.permutation(h)]
    x[:, 7] = 255 * (rng.random((N, 16, W)) < 0.4)
    return pack(x, c)
def setup_inputs_lean(rng):
    h = W // 2; nn = rng.integers(h // 4, h // 2, (N, 8)); pz = rng.integers(h // 4, h // 2, (N, 8)); o = XS[0]
    nn[:, 0] = 0; pz[:, 1] = 0
    nn[0, 2] = W; pz[0, 2] = 0; nn[o, 2] = h; pz[o, 2] = W - h
    nn[0, 3] = 0; pz[0, 3] = 0; nn[o, 3] = 0; pz[o, 3] = W
    nn[0, 6] = 1; pz[0, 6] = W - 1
    for r in (0, XS[1], XS[0] ^ XS[1]): nn[r, 4] = h // 2; pz[r, 4] = h // 16
    nn[o, 4] = 16; pz[o, 4] = h // 2
    x, c, P, M = plant(rng, nn, pz, np.array([0, 0, 0, 0, 1, 2, 1, 2]), False, (0, 1, 4))
    a, b, e, k, l = P[0, :5]; m = M[0]
    c[0][:, [0, m]] = c[0][:, [m, 0]]; c[0, b, 0] = 0; x[:, 0, a] -= x[:, 0, b]
    c[0, :, 1] = 0; c[0, e, 1] = 2 * rng.integers(0, 2) - 1; c[0, k, 1] = 2; c[0, l, 1] = -2
    a, b = P[1, :2]; c[1, a, M[1]] = 0; x[:, 1, b] -= x[:, 1, a]
    c[4, :, (M[4] + rng.integers(1, 16)) % 16] = c[4, :, M[4]]
    return pack(x, c)
def setup_inputs_spread(rng):
    u = rng.random((N, 8, 16, W)); u[:, 6] = 0.5 + 0.5 * u[:, 6]
    v = np.floor(np.exp2(3 + 5 * rng.random((N, 8, 1, W))) * u) * (rng.random((N, 8, 1, W)) > 0.0625)
    kept = rng.random((N, 8, 16, W)) < rng.choice(np.array([0.4, 0.7, 1.0]), (N, 8, 16, 1)); kept[:, 6] = True
    v = np.minimum(v * kept, 255).astype(np.int64); c = coefs(rng, 2, 16)
    up = rng.permutation(16) < 8; side = (rng.random((N, 1, W)) < 0.5) == up[None, :, None]
    v[:, 7] = np.where(side, rng.integers(192, 256, (N, 16, W)), rng.integers(0, 32, (N, 16, W)))
    c[7] = np.where(up[:, None], 1, -1) * rng.choice(np.array([2, 3, 3, 3]), (16, 16)) * rng.choice(np.array([-1, 1]), (1, 16))
    return pack(v, c)
def check_inputs(d):
    bad = []; x = np.asarray(d["x"]).astype(np.float32); q = np.asarray(d["q"])
    if not (np.all(x >= 0) and np.all(x <= 255) and np.all(x == np.floor(x))): bad.append("range of x")
    if np.min(q) < -3 or np.max(q) > 3: bad.append("range of q")
    if not np.all(q == q[:1]): bad.append("q alike on all ranks")
    return bad
def reference(x, q):
    cur = np.ascontiguousarray(x.astype(np.float32).reshape(N, 8, 16, W).transpose(0, 1, 3, 2)).astype(np.int16)
    co = q[0].astype(np.float32).reshape(8, 16, 16)
    used = np.zeros((8, 16), bool)
    k = np.arange(K); i = k >> LP
    for t in range(len(XS)):
        val = np.matmul(cur.astype(np.float32), co[None])
        cnt = np.where(used, N * W + 1, np.count_nonzero(val, axis=(0, 2)))
        m = np.argmin(cnt, axis=1)
        used[np.arange(8), m] = True
        s = np.take_along_axis(val, m[None, :, None, None], 3)[..., 0].astype(np.int64)
        j = (37 * i + (CAP >> LP) * (k & (2 ** LP - 1)) + t) & (CAP - 1)
        new = cur.copy()
        for r in range(N):
            o = r ^ XS[t]
            for g in range(8):
                own = cur[r, g]; neg = np.flatnonzero(s[r, g] < 0); pos = np.flatnonzero(s[r, g] > 0); guest = np.flatnonzero(s[o, g] < 0)[:CAP]
                ks = np.flatnonzero((i < len(pos)) & (j < len(guest)))
                a = pos[i[ks]]; b = guest[j[ks]]; keep = s[r, g, a] + s[o, g, b] >= 0
                a = a[keep]; b = b[keep]
                z = np.minimum(own[a] + cur[o, g][b], 255)
                v = (17 * a + 5 * j[ks][keep]) & (W - 1); alive = np.ones(len(a), bool)
                for n in range(PR):
                    c = np.where(v == a, 16, np.count_nonzero(own[v] > z, axis=1))
                    alive = alive & (c > 0)
                    v = (5 * v + 241 * c + 1) & (W - 1)
                z = z[alive]; h = min(len(z), len(neg))
                new[r, g, neg[:h]] = z[:h]
        cur = new
    return {"y": np.ascontiguousarray(cur.transpose(0, 1, 3, 2)).reshape(N, 128, W).astype(np.float32).astype(BF)}

@@ -1,0 +1,522 @@
+from concourse.bass import DstId, RemoteDMATransfer
+from concourse.mybir import AluOpType, AxisListType, ActivationFunctionType
+
+ALU, ACT = AluOpType, ActivationFunctionType
+W, K, CAP, MP, PR, NR = 2048, 4096, 256, 1024, 8, 8
+XS = (4, 3)
+NH = 1648
+X6, ZS = 6 * W, 7 * W + 16
+MV = 80
+NS = 16 * (128 - MV)
+C0, K1, BIG = 393216.0, 16.0625, 30000.0
+HC = (0, 36, 72, NH // 16)
+VC = (6, 9)
+
+SCRATCH = {}
+for _d, _l in (
+    ("bfloat16", [("XT", W), ("XR", ZS + NH), ("Z", K + 16), ("FL", K), ("GS", 2 * NS), ("PRS", MP), ("GN", CAP), ("GE0", 704), ("GE1", 704),
+                  ("QB", 128), ("NZ", W), ("NZ2", 1024), ("BLK", 128), ("ID", 128), ("NID", 128), ("W241", 128), ("IDW", 128), ("TRI", 128),
+                  ("TRU", 128), ("TMP", 128), ("UU", 128), ("SW1", 144), ("I16", 128), ("SB", 128), ("G8B", 8), ("C8", 8), ("NC8", 8),
+                  ("CB", 256), ("ONE", 128), ("NEG", 128), ("T255", 128), ("FS", 256), ("AS", 288), ("SF", NH), ("HH", 256),
+                  ("EQ", 8 * 256), ("FF", 8 * 256), ("SG", 256), ("AL", 256), ("A5", 272)]),
+    ("float32", [("LD0", 32), ("LD1", 32), ("QF", 16), ("PC", 8), ("CI", 144), ("CG", 128), ("CR", 128), ("CQ", 128), ("BLKF", 128),
+                 ("E16", 16), ("G8", 8), ("KM", 16), ("KD", 16), ("OH", 16), ("OQ", 16), ("COL", 16), ("QS", NH - 16 * HC[2]), ("TF", 256),
+                 ("PL", 128), ("W3", 272), ("W2", 32), ("T1", 4), ("AK", 256), ("W35", 264), ("W25", 24), ("T5", 4), ("KEY", 128),
+                 ("DL", 128), ("TT", 128), ("TU", 128)]),
+    ("float16", [("IH", 128), ("I5", 128), ("I17", 128), ("SQ", 512), ("QH", NH), ("QN0", 256), ("QN1", 256), ("J50", 256), ("J51", 256),
+                 ("A16", 64), ("AP", 256), ("DD", 256), ("RR", 256)]),
+    ("int32", [("QI", 16), ("PI", 8), ("TI", 256), ("TJ", 256)]),
+    ("uint16", [("SO", 128), ("OF", 256), ("FO", 128)]),
+):
+    for _n, _c in _l: SCRATCH[_n] = ("sbuf", [128, _c], _d)
+for _b in range(8):
+    SCRATCH["B%d" % _b] = ("psum", [128, 512], "float32")
+SEMAPHORES = ["sV", "sS", "sP", "sG", "lq", "lx0", "lx1", "lx2", "lx3", "ca0", "ca1", "cl0", "cl1", "ga0", "ga1", "gl0", "gl1",
+              "y0", "y1", "y2", "y3"]
+TWO = ("bfloat16", "float16", "uint16")
+CYC, PEC, GAT, FIXV, FIXS, HOP, SELF, GL = 1.0, 0.5, 1.56, 60.0, 90.0, 100.0, 60.0, 3000.0
+PLAN = {}
+
+
+def R(name, a=0, b=None, s=1):
+    return (name, a, SCRATCH[name][1][1] if b is None else b, s)
+
+
+def width(r):
+    return (r[2] - r[1] + r[3] - 1) // r[3]
+
+
+def build(g, core, T, topo):
+    rank = T.rank_of(core)
+    ops = []; chain = [False]; after = [None]
+
+    def ap(r):
+        if not isinstance(r, tuple): return r
+        if r[0] == "ind": return ap(r[1]).indirect(ap(r[2]))
+        if r[3] == 1: return T[r[0]][:, r[1]:r[2]]
+        return T[r[0]][:, r[1]:r[2]:r[3]]
+
+    def regs(rs):
+        out = []
+        for r in rs:
+            if isinstance(r, tuple):
+                if r[0] == "ind": out += [r[1], r[2]]
+                else: out.append(r)
+        return out
+
+    def add(eng, fn, reads, writes, cost, tok=None, lat=0.0):
+        ops.append({"e": eng, "f": fn, "r": regs(reads), "w": regs(writes), "c": cost, "tok": tok, "lat": lat,
+                    "chain": chain[0], "after": after[0]})
+
+    def vcost(out, ins, two=False):
+        n = width(out)
+        if ins[0][0] == "ind": return FIXV + n * GAT * CYC
+        if two: k = 1.0 if any(SCRATCH[r[0]][0] == "psum" for r in ins) else 2.0
+        else: k = 0.5 if all(SCRATCH[r[0]][2] in TWO for r in [out] + ins) else 1.0
+        return FIXV + max(30.0, n * k) * CYC
+
+    def ts(out, in0, s1, op0, s2=None, op1=None):
+        if op1 is None: fn = lambda: [g.vector.tensor_scalar(ap(out), ap(in0), ap(s1), None, op0)]
+        else: fn = lambda: [g.vector.tensor_scalar(ap(out), ap(in0), ap(s1), ap(s2), op0, op1)]
+        add("V", fn, [in0, s1, s2], [out], vcost(out, [in0]))
+
+    def tt(out, in0, in1, op):
+        add("V", lambda: [g.vector.tensor_tensor(ap(out), ap(in0), ap(in1), op)], [in0, in1], [out], vcost(out, [in0, in1], True))
+
+    def cp(out, in_):
+        add("V", lambda: [g.vector.tensor_copy(ap(out), ap(in_))], [in_], [out], vcost(out, [in_]))
+
+    def red(out, in_, op):
+        add("V", lambda: [g.vector.tensor_reduce(ap(out), ap(in_), AxisListType.X, op)], [in_], [out], FIXV + max(30, width(in_)) * CYC)
+
+    def scan(out, d0, d1, init, op0, op1):
+        add("V", lambda: [g.vector.tensor_tensor_scan(ap(out), ap(d0), ap(d1), ap(init), op0, op1)], [d0, d1, init], [out], vcost(out, [d0, d1]))
+
+    def fill(out, v):
+        add("V", lambda: [g.vector.memset(ap(out), v)], [], [out], vcost(out, [out]))
+
+    def act(out, in_, func, bias=None, scale=None, acc=None):
+        def fn():
+            kw = {}
+            if bias is not None: kw["bias"] = ap(bias)
+            if scale is not None: kw["scale"] = ap(scale)
+            if acc is not None: kw["accum_out"] = ap(acc)
+            return [g.scalar.activation(ap(out), ap(in_), func, **kw)]
+        add("S", fn, [in_, bias, scale], [out, acc], FIXS + width(out) * (GAT if in_[0] == "ind" else 1.0) * CYC)
+
+    def mm(items):
+        cost = 20.0
+        for o, l, r, a, b in items:
+            cost += max(min(64, width(l)), width(r)) * PEC * (4 if SCRATCH[l[0]][2] == "float32" else 1)
+        add("P", lambda: [g.tensor.matmul(ap(o), ap(l), ap(r), a, b) for o, l, r, a, b in items],
+            [x[1] for x in items] + [x[2] for x in items], [x[0] for x in items], cost)
+
+    def group(out, pairs):
+        mm([(out, l, r, n == 0, n == len(pairs) - 1) for n, (l, r) in enumerate(pairs)])
+
+    def iota(out, pattern, base, cm):
+        small = SCRATCH[out[0]][2] != "int32"
+
+        def fn():
+            if small: return [g.iota(ap(out), pattern, base, cm, allow_small_or_imprecise_dtypes=True)]
+            return [g.iota(ap(out), pattern, base, cm)]
+        add("G", fn, [], [out], 130 + 2 * width(out) * CYC)
+
+    def ind(win, off):
+        return ("ind", win, off)
+
+    def sel(r):
+        return R("SW1", 15 - r, 143 - r)
+
+    add("Y", lambda: [g.sync.dma_start(ap(R("QI")), T.q[:]).then_inc(T.sem.lq, 16)], [], [R("QI")], 60, ("lq", 16), 1800)
+    for k in range(4):
+        q = g.sync if k % 2 == 0 else g.scalar
+        add("Y" if k % 2 == 0 else "S",
+            lambda q=q, k=k: [q.dma_start(ap(R("XT", 512 * k, 512 * k + 512)), T.x[:, 512 * k:512 * k + 512]).then_inc(T.sem["lx%d" % k], 16)],
+            [], [R("XT", 512 * k, 512 * k + 512)], 60, ("lx%d" % k, 16), 2300 + 200 * k)
+
+    pc, gc16, rc, gcol, bigc, bjc = (R("PC", k, k + 1) for k in range(6))
+    iota(R("PI", 0, 1), [[0, 1]], 0, 1)
+    iota(R("CI"), [[1, 144]], 0, 0)
+    iota(R("CG"), [[1, 8], [0, 16]], 0, 0)
+    iota(R("CR"), [[0, 8], [1, 16]], 0, 0)
+    iota(R("CQ"), [[16, 8], [1, 4], [0, 4]], 0, 0)
+    cp(pc, R("PI", 0, 1))
+    ts(R("PI", 1, 2), R("PI", 0, 1), 4, ALU.arith_shift_right)
+    cp(gcol, R("PI", 1, 2))
+    ts(R("G8"), R("CI", 0, 8), gcol, ALU.is_equal)
+    ts(R("G8B"), R("CI", 0, 8), gcol, ALU.is_equal)
+    cp(R("QF"), R("QI"))
+    for k in range(8):
+        if k < 5: ts(R("QB", 16 * k, 16 * k + 16), R("QF"), R("G8", k, k + 1), ALU.mult)
+        else: act(R("QB", 16 * k, 16 * k + 16), R("QF"), ACT.Identity, None, R("G8", k, k + 1))
+    ts(gc16, gcol, 16.0, ALU.mult, 15.0, ALU.add)
+    ts(R("PI", 2, 3), R("PI", 0, 1), 15, ALU.bitwise_and)
+    cp(rc, R("PI", 2, 3))
+    ts(bigc, rc, 8.0, ALU.is_ge, BIG, ALU.mult)
+    ts(R("PI", 3, 4), R("PI", 0, 1), 2, ALU.arith_shift_right, 3, ALU.bitwise_and)
+    ts(R("PI", 4, 5), R("PI", 0, 1), 3, ALU.bitwise_and)
+    ts(R("PC", 6, 7), R("PI", 3, 4), 37.0, ALU.mult)
+    ts(bjc, R("PI", 4, 5), 64.0, ALU.mult, R("PC", 6, 7), ALU.add)
+    ts(R("E16"), R("CI", 0, 16), rc, ALU.is_equal)
+    ts(R("KM"), R("E16"), rc, ALU.mult)
+    ts(R("BLKF"), R("CG"), gcol, ALU.is_equal)
+    ts(R("BLK"), R("CG"), gcol, ALU.is_equal)
+    ts(R("ID"), R("CI", 0, 128), pc, ALU.is_equal)
+    for nm, v in (("IH", 1.0), ("I5", 5.0), ("I17", 17.0)):
+        ts(R(nm), R("ID"), v, ALU.mult)
+    for nm, v in (("NID", -1.0), ("W241", 241.0 / 16), ("IDW", 8192.0), ("I16", 16.0)):
+        act(R(nm), R("ID"), ACT.Identity, None, v)
+    ts(R("UU"), R("CI", 0, 128), pc, ALU.is_ge)
+    ts(R("TMP"), R("CR"), rc, ALU.is_ge)
+    tt(R("TRI"), R("TMP"), R("BLK"), ALU.mult)
+    tt(R("TRU"), R("BLK"), R("TRI"), ALU.subtract)
+    ts(R("SW1"), R("CI"), gc16, ALU.is_equal)
+    for q in range(4):
+        ts(R("SQ", 128 * q, 128 * q + 128), R("CQ"), 4.0 * q, ALU.add, pc, ALU.is_equal)
+    fill(R("ONE"), 1.0); fill(R("NEG"), -1.0); fill(R("T255"), 255.0)
+    cp(R("QH", 0, 128), R("CI", 0, 128))
+    for a in (128, 256, 512, 1024):
+        b = min(2 * a, NH); ts(R("QH", a, b), R("QH", 0, b - a), float(a), ALU.add)
+    fill(R("XR", 7 * W, ZS), 0.0); fill(R("Z", K, K + 16), 0.0)
+    fill(R("AS", 0, 16), 0.0); fill(R("AS", 144, 160), 0.0); fill(R("A5", 0, 16), 0.0)
+    fill(R("W3"), BIG); fill(R("W2"), BIG); fill(R("W35", 256, 264), BIG); fill(R("W25", 16, 24), BIG)
+
+    def round_constants(t):
+        iota(R("TI"), [[37, 256]], t, 0)
+        ts(R("TJ"), R("TI"), 255, ALU.bitwise_and)
+        cp(R("TF"), R("TJ")); cp(R("QN%d" % t), R("TF"))
+        iota(R("TF"), [[148, 256]], t, 0)
+        ts(R("TI"), R("TF"), bjc, ALU.add)
+        ts(R("TJ"), R("TI"), 255, ALU.bitwise_and)
+        cp(R("TF"), R("TJ"))
+        ts(R("J5%d" % t), R("TF"), 5.0, ALU.mult, -1.0, ALU.add)
+        if t == 0:
+            iota(R("TT"), [[16, 128]], 0, 0)
+            ts(R("PL"), R("TT"), rc, ALU.add)
+            iota(R("QS"), [[1, NH - 16 * HC[2]]], 16 * HC[2], 0)
+
+    def search(bank, c0, c1, qry, t1, w2, w3, s_first=None, parts=1):
+        n = c1 - c0; fl = R("SF", 16 * c0, 16 * c1); so = R("SO", c0, c1); pb = R(bank, 0, n)
+
+        def count(first):
+            group(pb, first + [(sel(r), R("SF", 16 * c0 + r, 16 * c1, 16)) for r in range(16)])
+        if s_first is None: ts(fl, qry, t1, ALU.is_ge)
+        else: act(fl, s_first[0], ACT.Sigmoid, s_first[1], 256.0)
+        count([])
+        yield
+        for w in (w2, w3):
+            cp(so, pb); act(R("SB", c0, c1), pb, ACT.Copy)
+            m = n // parts
+            for u in range(parts):
+                tt(R("SF", 16 * (c0 + u * m), 16 * (c0 + u * m + m)), ind(w, R("SO", c0 + u * m, c0 + u * m + m)),
+                   R(qry[0], qry[1] + 16 * u * m, qry[1] + 16 * (u * m + m)), ALU.is_le)
+            count([(R("I16"), R("SB", c0, c1))])
+            yield
+        cp(so, pb)
+        yield
+
+    others = [r for r in range(NR) if r != rank]
+    for t in range(2):
+        LD, GE = "LD%d" % t, "GE%d" % t
+        for k in range(4):
+            group(R("B%d" % k), [(R("QB"), R("XT", 512 * k, 512 * k + 512))])
+        slot = 4 * rank
+        for k in range(2):
+            ts(R("NZ", 512 * k, 512 * k + 512), R("B%d" % k), 0.0, ALU.not_equal)
+            red(R(LD, slot + k, slot + k + 1), R("NZ", 512 * k, 512 * k + 512), ALU.add)
+        for k in range(2, 4):
+            act(R("NZ", 512 * k, 512 * k + 512), R("B%d" % k), ACT.Sign)
+            act(R("NZ2", 512 * (k - 2), 512 * (k - 1)), R("NZ", 512 * k, 512 * k + 512), ACT.Square, acc=R(LD, slot + k, slot + k + 1))
+        counted = len(ops) - 1
+
+        def send_counts(t=t, LD=LD, slot=slot):
+            mine = ap(R(LD, slot, slot + 4)); ids = []; m = None
+            for r in others:
+                rid, pid = topo.addr(T.cores[r], core); ids.append(DstId(rid=rid, pnc=pid))
+                mk = topo.mask(core, T.cores[r]); m = mk if m is None else m & mk
+            return [g.remote_dma_fused([RemoteDMATransfer(dst_ids=ids, dma_engine_mask=m, remote_sem=T.sem["ca%d" % t], src=mine,
+                                                          dsts=[mine] * len(ids))], local_sem=T.sem["cl%d" % t])]
+        ne = len(topo.engines(core, T.cores[others[0]]))
+        add("G", send_counts, [R(LD)], [R("COL", 8 + t, 9 + t)], 300, ("cl%d" % t, ne), 3000)
+        add("A", None, [R("COL", 8 + t, 9 + t)], [R(LD, 0, 32, 2)], 0, ("ca%d" % t, ne * len(others)), 2000)
+        after[0] = counted if t == 1 else None
+        round_constants(t)
+        after[0] = None
+        for u in range(28):
+            c, h = 6 - u // 4, u % 4
+            o, i = R("XR", c * W + 512 * h, c * W + 512 * h + 512), R("XT", 512 * h, 512 * h + 512)
+            if 4 <= u < 4 + VC[t]: ts(o, i, -1.0, ALU.mult, 255.0, ALU.add)
+            else: act(o, i, ACT.Identity, 255.0, -1.0)
+        tot, mn, coef = R("COL", 0, 1), R("COL", 1, 2), R("COL", 2, 3)
+        red(tot, R(LD), ALU.add)
+        ts(R("KD"), R("E16"), tot, ALU.mult, 16.0, ALU.mult)
+        group(R("B4", 0, 16), [(R("BLKF"), R("KM")), (R("BLKF"), R("KD"))])
+        red(mn, R("B4", 0, 16), ALU.min)
+        ts(R("OH"), R("B4", 0, 16), mn, ALU.is_equal)
+        tt(R("OQ"), R("OH"), R("QF"), ALU.mult)
+        red(coef, R("OQ"), ALU.add)
+        ts(R("C8"), R("G8"), coef, ALU.mult)
+        if t == 0:
+            tt(R("OQ"), R("OH"), R("E16"), ALU.mult)
+            ts(R("OQ"), R("OQ"), 524288.0, ALU.mult)
+            tt(R("KM"), R("KM"), R("OQ"), ALU.add)
+        mm([(R("B5", r, 128, 16), R("XT", r, W, 16), R("C8"), True, True) for r in range(16)])
+        ts(R("FS", 128, 256), R("B5", 0, 128), 0.0, ALU.is_lt)
+        ts(R("FS", 0, 128), R("B5", 0, 128), 0.0, ALU.is_gt)
+        mm([(R("B6", 128, 256), R("FS", 128, 256), R("UU"), True, True), (R("B6", 0, 128), R("FS", 0, 128), R("UU"), True, True)])
+        cp(R("AS", 160, 288), R("B6", 128, 256)); cp(R("AS", 16, 144), R("B6", 0, 128))
+        group(R("B4", 0, 2), [(sel(r), R("AS", 31 + 16 * r, 31 + 16 * r + 145, 144)) for r in range(8)])
+        ts(R("T1", 0, 2), R("B4", 0, 2), bigc, ALU.add)
+        group(R("B3", 0, 17), [(sel(r), R("AS", 16 + r, 288, 16)) for r in range(16)])
+        act(R("W2", 16, 24), R("B3", 9, 17), ACT.Copy); act(R("W2", 0, 8), R("B3", 0, 8), ACT.Copy)
+        mm([(R("B7", 128, 256), R("TRI"), R("AS", 160, 288), True, False), (R("B7", 128, 256), R("TRU"), R("AS", 159, 287), False, True),
+            (R("B7", 0, 128), R("TRI"), R("AS", 16, 144), True, False), (R("B7", 0, 128), R("TRU"), R("AS", 15, 143), False, True)])
+        act(R("W3", 136, 264), R("B7", 128, 256), ACT.Copy); act(R("W3", 0, 128), R("B7", 0, 128), ACT.Copy)
+        win = R("XR", X6, ZS)
+        for _ in search("B0", 64, 80, R("QN%d" % t), R("T1", 1, 2), R("W2", 16, 32), R("W3", 136, 272)): pass
+        act(R("GN"), ind(win, R("SO", 64, 80)), ACT.Identity, 255.0, -1.0)
+        partner = T.cores[rank ^ XS[t]]
+
+        def send_guests(t=t, GE=GE, partner=partner):
+            rid, pid = topo.addr(partner, core)
+            return [g.remote_dma(ap(R(GE, 0, CAP)), ap(R("GN")), T.sem["ga%d" % t], T.sem["gl%d" % t], pid, rid, topo.mask(core, partner))]
+        ne = len(topo.engines(core, partner))
+        add("G", send_guests, [R("GN")], [R("COL", 10 + t, 11 + t)], 300, ("gl%d" % t, ne), GL)
+        add("A", None, [R("COL", 10 + t, 11 + t)], [R(GE, 0, CAP)], 0, ("ga%d" % t, ne), 1200)
+        for s in range(2):
+            for _ in search("B%d" % (1 + s), 32 * s, 32 * s + 32, R("QH", 512 * s, 512 * s + 512), R("T1", 0, 1), R("W2", 0, 16),
+                            R("W3", 0, 136), None, 2 - s): pass
+            cp(R("A16", 32 * s, 32 * s + 32), R("B%d" % (1 + s), 0, 32))
+            act(R("PRS", 512 * s, 512 * s + 512), ind(win, R("SO", 32 * s, 32 * s + 32)), ACT.Copy)
+        tt(R("TT"), R("AS", 159, 287), R("AS", 160, 288), ALU.subtract)
+        ts(R("TT"), R("TT"), 8192.0, ALU.mult, 8192.0, ALU.add)
+        tt(R("KEY"), R("TT"), R("W3", 136, 264), ALU.add)
+        tt(R("TU"), R("W3", 136, 264), R("PL"), ALU.subtract)
+        ts(R("DL"), R("TU"), float(ZS - X6 - 1), ALU.add)
+        for s in range(2):
+            c = 128 * s; pbk = R("B%d" % (5 + s), 0, 128); ab = "B7" if s else "B3"
+            mm([(R(ab, q, 128, 4), R("SQ", 128 * q, 128 * q + 128), R("A16", 32 * s, 32 * s + 32), True, True) for q in range(4)])
+            cp(R("AP", c, c + 128), R(ab, 0, 128))
+            act(R("AK", c, c + 128), R(ab, 0, 128), ACT.Identity, -(K1 + C0))
+            first = [(R("I17"), R("AP", c, c + 128)), (R("IH"), R("J5%d" % t, c, c + 128)), (R("W241"), R("NEG"))]
+            group(pbk, first)
+            act(R("HH", c, c + 128), pbk, ACT.Identity, C0 - 1023.5 + K1)
+            group(pbk, first + [(R("NID"), R("HH", c, c + 128))])
+            ts(R("OF", c, c + 128), pbk, K1 + C0, ALU.add)
+        cp(R(GE, 256, 512), R(GE, 0, 256)); act(R(GE, 512, 704), R(GE, 0, 192), ACT.Copy)
+        group(R("B4"), [(R("ID"), R("PRS", 0, 512))])
+        for kk in range(4):
+            tt(R("Z", kk, W, 4), R("B4"), R(GE, 64 * kk, 64 * kk + 512), ALU.subtract)
+        for kk in range(4):
+            bk = R("B%d" % (kk % 2))
+            group(bk, [(R("ID"), R("PRS", 512, 1024)), (R("NID"), R(GE, 64 * kk, 64 * kk + 512))])
+            act(R("Z", W + kk, K, 4), bk, ACT.Copy)
+        xw = R("XR", 0, 7 * W); m1 = (128 - MV + 2) // 4 * 2; cut = (0, m1, 128 - MV)
+        tal = (R("B7", 0, 128), R("B4", 0, 128))
+
+        def part(n, s):
+            c = 128 * s
+            return (c, W * s, R("B%d" % (5 + s), 0, 128), R("DD", c, c + 128), R("EQ", 256 * n + c, 256 * n + c + 128),
+                    R("FF", 256 * n + c, 256 * n + c + 128))
+
+        def counts(n, s):
+            mm([(R("B3", 128 * s + r, 128 * s + 128, 16), R("FL", W * s + r, W * s + W, 16), R("G8B"), True, True) for r in range(16)])
+
+        def relu(n, s):
+            act(part(n, s)[5], R("B3", 128 * s, 128 * s + 128), ACT.Relu, -1.0, 16.0)
+
+        def same(n, s):
+            ts(part(n, s)[4], part(n, s)[3], 0.0, ALU.is_equal, 255.0, ALU.mult)
+
+        def tally(n, s):
+            mm([(tal[s], R("ID"), part(n, s)[4], n == 0, False), (tal[s], part(n, s)[5], R("ID"), False, n == PR - 1)])
+
+        def step(n, s):
+            c, _, _, d, eq, f = part(n, s)
+            return [(R("I5"), d), (R("I5"), R("AP", c, c + 128)), (R("W241"), eq), (f, R("W241"))]
+
+        def strand(r):
+            return R("B2", r // 16 * 128 + r % 16, r // 16 * 128 + 128, 16)
+        ts(R("CB", 0, 128), R("BLK"), coef, ALU.mult); ts(R("CB", 128, 256), R("BLK"), coef, ALU.mult); ts(R("NC8"), R("C8"), -1.0, ALU.mult)
+        mm([(R("B2", 0, 256), R("T255"), R("CB"), True, False)])
+        for u in range(0, 32, 8):
+            mm([(strand(r), R("PRS", r // 16 * 512 + r % 16 // 4, r // 16 * 512 + 512, 4), R("NC8"), False, False) for r in range(u, u + 8)])
+        chain[0] = True
+        for k in range(2 * PR):
+            n, s = k // 2, k % 2; pn, ps = (k - 1) // 2, (k - 1) % 2
+            c, e, pbk, d, eq, f = part(n, s)
+            gs = [R("GS", NS * s + 16 * cut[h], NS * s + 16 * cut[h + 1]) for h in range(2)]
+            zs = [(e + 16 * (MV + cut[h]), e + 16 * (MV + cut[h + 1])) for h in range(2)]
+            bk = [R("B%d" % h, 0, 16 * (cut[h + 1] - cut[h])) for h in range(2)]
+            if n > 0: ts(R("OF", c, c + 128), pbk, K1, ALU.add)
+            if k > 0: same(pn, ps)
+            if n > 0: ts(R("HH", c, c + 128), R("OF", c, c + 128), C0 - 1023.5, ALU.add)
+            mm([(bk[0], R("ID"), R("Z", *zs[0]), True, False)])
+            if k > 0: counts(pn, ps)
+            mm([(bk[1], R("ID"), R("Z", *zs[1]), True, False)])
+            act(gs[0], ind(xw, R("OF", c + MV, c + MV + m1)), ACT.Copy)
+            if k > 0: relu(pn, ps)
+            mm([(bk[0], R("NID"), gs[0], False, True)])
+            if k > 0 and pn < PR - 1: group(part(pn, ps)[2], step(pn, ps))
+            if n > 0: group(pbk, step(n - 1, s) + [(R("NID"), R("HH", c, c + 128))])
+            act(gs[1], ind(xw, R("OF", c + MV + m1, c + 128)), ACT.Copy)
+            mm([(bk[1], R("NID"), gs[1], False, True)])
+            tt(R("FL", e, e + 16 * MV), ind(xw, R("OF", c, c + MV)), R("Z", e, e + 16 * MV), ALU.is_lt)
+            for h in range(2):
+                act(R("FL", *zs[h]), bk[h], ACT.Sigmoid, -128.0, 256.0)
+            tt(d, pbk, R("AK", c, c + 128), ALU.subtract)
+            if k == 2 * PR - 1: same(n, s)
+            if k > 0: tally(pn, ps)
+            if 2 <= k < 10:
+                mm([(strand(r), R(GE, r % 16 // 4 + 64 * (r % 4), r % 16 // 4 + 64 * (r % 4) + 509, 4), R("C8"), False, r == 31)
+                    for r in range(4 * k - 8, 4 * k - 4)])
+            if k == 10: act(R("SG"), R("B2", 0, 256), ACT.Sign, 0.5)
+            if k in (12, 13): mm([(tal[s], R("SG", c, c + 128), R("IDW"), False, False)])
+        chain[0] = False
+        for s in range(2):
+            c = 128 * s
+            if s == 1:
+                counts(PR - 1, 1); relu(PR - 1, 1); tally(PR - 1, 1)
+            ts(R("RR", c, c + 128), tal[s], 8197.0, ALU.max)
+            tt(R("AL", c, c + 128), tal[s], R("RR", c, c + 128), ALU.is_equal)
+            scan(R("A5", 16 + c, 144 + c), R("ONE"), R("AL", c, c + 128), R("A5", 15 + c, 16 + c), ALU.mult, ALU.add)
+            mm([(R("B2", 0, 1), sel(r), R("A5", 31 + 16 * r, 32 + 16 * r), r == 0, r == 15) for r in range(8 * s, 8 * s + 8)]
+               + [(R("B2", 1, 2), R("BLK"), R("A5", 271, 272), True, True)] * s)
+        cp(R("T5", 0, 2), R("B2", 0, 2))
+        act(R("T5", 2, 3), R("T5", 0, 1), ACT.Identity, 128.0, -256.0)
+        group(R("B3", 0, 16), [(sel(r), R("A5", 16 + r, 272, 16)) for r in range(16)])
+        act(R("W25", 0, 16), R("B3", 0, 16), ACT.Copy)
+        group(R("B0", 0, 256), [(R("TRI"), R("A5", 16, 272)), (R("TRU"), R("A5", 15, 271))])
+        act(R("W35", 0, 256), R("B0", 0, 256), ACT.Copy)
+        zw = R("Z")
+        ts(R("TT"), R("KEY"), R("T5", 1, 2), ALU.is_le)
+        se = [search("B%d" % (4 + u), HC[u], HC[u + 1], R("QH", 16 * HC[u], 16 * HC[u + 1]), R("T5", 0, 1), R("W25"), R("W35"),
+                     (R("QS"), R("T5", 2, 3)) if u == 2 else None) for u in range(3)]
+        done = [0, 0, 0]; chain[0] = True
+        for u in (0, 2, 1, 0, 1, 0, 2, 0, 1, 2, 1, 2):
+            next(se[u]); done[u] += 1
+            if done[u] < 4: continue
+            a, b = HC[u], HC[u + 1]
+            if u == 1:
+                tt(R("TU"), R("TT"), R("DL"), ALU.mult)
+                tt(R("TT"), R("TU"), R("PL"), ALU.add)
+                cp(R("FO"), R("TT"))
+            if u == 2:
+                h = a + 24
+                ts(R("XR", ZS + 16 * a, ZS + 16 * h), ind(zw, R("SO", a, h)), 0.0, ALU.max)
+                act(R("XR", ZS + 16 * h, ZS + 16 * b), ind(zw, R("SO", h, b)), ACT.Relu)
+            else: act(R("XR", ZS + 16 * a, ZS + 16 * b), ind(zw, R("SO", a, b)), ACT.Relu)
+        chain[0] = False
+        fw = R("XR", X6, ZS + NH)
+        for k in range(4):
+            o = R("XT", 512 * k, 512 * k + 512); src = ind(fw, R("FO", 32 * k, 32 * k + 32))
+            if k < 2: ts(o, src, -1.0, ALU.mult, 255.0, ALU.add)
+            else: act(o, src, ACT.Identity, 255.0, -1.0)
+            if t == 1:
+                add("Y", lambda k=k, o=o: [g.sync.dma_start(T.y[:, 512 * k:512 * k + 512], ap(o)).then_inc(T.sem["y%d" % k], 16)],
+                    [o], [], 60, ("y%d" % k, 16), 2000)
+    return ops
+
+
+def depend(ops):
+    hist = {}; before = {}; deps = []
+    for i, o in enumerate(ops):
+        d = set()
+        for kind, rs in (("r", o["r"]), ("w", o["w"])):
+            for r in rs:
+                psum = SCRATCH[r[0]][0] == "psum"
+                if psum and hist.get(r[0]) and ops[hist[r[0]][-1][0]]["e"] == o["e"]: d.update(before.get(r[0], ()))
+                for j, kj, a, b in hist.get(r[0], ()):
+                    clash = (kind == "w" or kj == "w") and a < r[2] and r[1] < b
+                    if clash or (psum and (ops[j]["e"] != o["e"] or o["e"] == "P")): d.add(j)
+        for kind, rs in (("r", o["r"]), ("w", o["w"])):
+            for r in rs:
+                h = hist.setdefault(r[0], [])
+                if SCRATCH[r[0]][0] == "psum":
+                    if h and ops[h[-1][0]]["e"] != o["e"]:
+                        before[r[0]] = [x[0] for x in h]; del h[:]
+                elif kind == "w" and r[3] == 1: h[:] = [x for x in h if not (r[1] <= x[2] and x[3] <= r[2])]
+                h.append((i, kind, r[1], r[2]))
+        deps.append(d)
+    return deps
+
+
+def arrange(ops, hard):
+    n = len(ops); succ = [[] for _ in range(n)]
+    deps = [set(d) for d in hard]; prev = {}
+    for i, o in enumerate(ops):
+        if o["after"] is not None: deps[i].add(o["after"])
+        if o["chain"]:
+            if o["e"] in prev: deps[i].add(prev[o["e"]])
+            prev[o["e"]] = i
+    for i in range(n):
+        for j in deps[i]: succ[j].append(i)
+
+    def lag(j, i):
+        if j not in hard[i]: return 0.0
+        if ops[j]["e"] == ops[i]["e"]: return ops[j]["lat"] + (0.0 if ops[i]["e"] == "P" else SELF)
+        return ops[j]["lat"] + HOP
+    pri = [0.0] * n
+    for i in range(n - 1, -1, -1):
+        pri[i] = ops[i]["c"] + max([pri[k] + lag(i, k) for k in succ[i]] + [ops[i]["lat"]])
+    left = [len(d) for d in deps]; rdy = [0.0] * n; free = {}; order = []; placed = [False] * n
+    ready = [i for i in range(n) if left[i] == 0]
+    while ready:
+        st = [(max(rdy[i], free.get(ops[i]["e"], 0.0)), i) for i in ready]
+        t0, i0 = min(st); e = ops[i0]["e"]
+        p, i, s = max((pri[i], -i, s) for s, i in st if ops[i]["e"] == e and s <= t0 + 0.25 * ops[i0]["c"] + 40.0)
+        i = -i
+        soon = None; rs = dict((j, u) for u, j in st)
+        for u, j in st:
+            if ops[j]["e"] == e: continue
+            for k in succ[j]:
+                if ops[k]["e"] == e and pri[k] > p + 300.0:
+                    wait = [x for x in deps[k] if not placed[x]]
+                    if all(x in rs and ops[x]["e"] != e for x in wait):
+                        est = max([rdy[k]] + [rs[x] + ops[x]["c"] + lag(x, k) for x in wait])
+                        if est < s + ops[i]["c"] - 60.0 and (soon is None or est < soon): soon = est
+        if soon is not None and soon + 1 > rdy[i] and min(u for u, j in st if ops[j]["e"] != e) <= soon:
+            rdy[i] = soon + 1.0
+            continue
+        ready.remove(i); order.append(i); placed[i] = True
+        free[e] = s + ops[i]["c"]
+        for k in succ[i]:
+            rdy[k] = max(rdy[k], free[e] + lag(i, k)); left[k] -= 1
+            if left[k] == 0: ready.append(k)
+    return order
+
+
+def rank_program(g, core, T, topo):
+    if T.rank_of(core) is None:
+        return
+    ops = build(g, core, T, topo)
+    if not PLAN:
+        PLAN["deps"] = depend(ops)
+        PLAN["order"] = arrange(ops, PLAN["deps"])
+    deps = PLAN["deps"]
+    queue = {"V": g.vector, "S": g.scalar, "P": g.tensor, "G": g, "Y": g.sync}
+    count = {}; known = {e: {} for e in queue}; token = {}; clock = {}
+    for i in PLAN["order"]:
+        o = ops[i]; e = o["e"]
+        if e == "A":
+            token[i] = o["tok"]; clock[i] = {}; count[o["tok"][0]] = o["tok"][1]
+            continue
+        kn = known[e]
+        for j in sorted((j for j in deps[i] if not (e == "P" and ops[j]["e"] == "P")), key=lambda j: -token[j][1]):
+            s, v = token[j]
+            if kn.get(s, 0) < v:
+                queue[e].wait_ge(T.sem[s], v); kn[s] = v
+            for s2, v2 in clock[j].items():
+                if kn.get(s2, 0) < v2: kn[s2] = v2
+        ins = o["f"]()
+        if o["tok"] is None:
+            s = "s" + e
+            for x in ins:
+                x.then_inc(T.sem[s], 1); count[s] = count.get(s, 0) + 1
+            token[i] = (s, count[s])
+        else:
+            token[i] = o["tok"]; count[o["tok"][0]] = o["tok"][1]
+        clock[i] = dict(kn)
+    for s, v in count.items():
+        g.wait_ge(T.sem[s], v)

@@ -5,36 +5,45 @@ ALU, ACT = AluOpType, ActivationFunctionType
 W, K, CAP, MP, PR, NR = 2048, 4096, 256, 1024, 8, 8
 XS = (4, 3)
 NH = 1648
-X6, ZS = 6 * W, 7 * W + 16
-MV = 80
+X1, ZS = W, 2 * W + 16
+MV = 82
+M1 = 26
+ET, RS = PR - 3, (3, 0)
 NS = 16 * (128 - MV)
-C0, K1, BIG = 393216.0, 16.0625, 30000.0
-HC = (0, 36, 72, NH // 16)
-VC = (6, 9)
+CR2, BIG, MOD = 1.5 * 2.0 ** 34, 30000.0, 16512.0
+AN = 160
+HC = (0, 32, 64, NH // 16)
+FP = ((0, 4), (4, 8), (8, 11), (11, 14), (14, 16))
+FV = ((0, 4), (0, 2, 4))
+ZV = (320, 192)
+CV = ((32, 0, 16), (16, 16, 8))
+PS, SS = (0, 0), ((16, 0, 23), (32, 8, 0))
 
 SCRATCH = {}
+DIAG = {"NID": -1.0, "I5": 5.0, "IN5": -5.0, "I113": 113.0, "IN113": -113.0, "I238": 238.0, "IC": CR2, "INC": -CR2, "IN128": -128.0,
+        "IN16": -16.0, "I17": 17.0, "IK": 8192.0, "INK": -8192.0}
 for _d, _l in (
-    ("bfloat16", [("XT", W), ("XR", ZS + NH), ("Z", K + 16), ("FL", K), ("GS", 2 * NS), ("PRS", MP), ("GN", CAP), ("GE0", 704), ("GE1", 704),
-                  ("QB", 128), ("NZ", W), ("NZ2", 1024), ("BLK", 128), ("ID", 128), ("NID", 128), ("W241", 128), ("IDW", 128), ("TRI", 128),
-                  ("TRU", 128), ("TMP", 128), ("UU", 128), ("SW1", 144), ("I16", 128), ("SB", 128), ("G8B", 8), ("C8", 8), ("NC8", 8),
-                  ("CB", 256), ("ONE", 128), ("NEG", 128), ("T255", 128), ("FS", 256), ("AS", 288), ("SF", NH), ("HH", 256),
-                  ("EQ", 8 * 256), ("FF", 8 * 256), ("SG", 256), ("AL", 256), ("A5", 272)]),
-    ("float32", [("LD0", 32), ("LD1", 32), ("QF", 16), ("PC", 8), ("CI", 144), ("CG", 128), ("CR", 128), ("CQ", 128), ("BLKF", 128),
-                 ("E16", 16), ("G8", 8), ("KM", 16), ("KD", 16), ("OH", 16), ("OQ", 16), ("COL", 16), ("QS", NH - 16 * HC[2]), ("TF", 256),
-                 ("PL", 128), ("W3", 272), ("W2", 32), ("T1", 4), ("AK", 256), ("W35", 264), ("W25", 24), ("T5", 4), ("KEY", 128),
-                 ("DL", 128), ("TT", 128), ("TU", 128)]),
-    ("float16", [("IH", 128), ("I5", 128), ("I17", 128), ("SQ", 512), ("QH", NH), ("QN0", 256), ("QN1", 256), ("J50", 256), ("J51", 256),
-                 ("A16", 64), ("AP", 256), ("DD", 256), ("RR", 256)]),
+    ("bfloat16", [("XT", W), ("XA", ZS + NH), ("XB", ZS + NH), ("Z", K + 16), ("FL", K), ("GS", 2 * NS), ("PRS", 1024), ("GN", CAP),
+                  ("G0", CAP), ("GM", 256), ("WN", 4704), ("GE0", 512), ("GE1", 512), ("QB", 128), ("NZ", W), ("NZ2", 512), ("BLK", 128), ("BP", 128), ("BN", 128), ("ID", 128),
+                  ("TRI", 128), ("TRU", 128), ("TMP", 128), ("UU", 146), ("SW1", 144), ("SW16", 144), ("SW4", 144), ("SB", 128), ("SM", 16), ("G8B", 8),
+                  ("CB", 128), ("ONE", 128), ("TM255", 128), ("FS", 256), ("AS", 320), ("SF", NH), ("SN", CAP), ("BL", NH), ("SG", 256),
+                  ("AL", 256), ("A5", 272), ("MK", 128), ("CIB", 256), ("WP", 4704), ("WS", 9248), ("KM", 32), ("QS", 32), ("US", 32)]
+     + [(n, 128) for n in DIAG]),
+    ("float32", [("QF", 16), ("PC", 8), ("CI", 146), ("CG", 128), ("CR", 128), ("CQ", 144), ("E32", 32), ("KD", 32), ("BLKF", 128), ("LD0", 32), ("LD1", 32), ("G16", 24), ("COL", 16),
+                 ("TF", 128), ("PL", 128), ("W3", 272), ("W2", 16), ("T1", 4), ("W35", 264), ("T5", 4), ("L1", 256), ("TT", 128), ("RB", 256)]),
+    ("float16", [("SH", NH), ("QH", NH), ("QN0", 256), ("QN1", 256), ("J50", 128), ("J51", 128), ("AP", 256), ("ST", 8 * 256),
+                 ("FF", 8 * 256), ("RR", 256), ("JB", 128), ("JS", 2), ("G4", 24), ("L2", 256), ("KEY", 128), ("TK", 128)]),
     ("int32", [("QI", 16), ("PI", 8), ("TI", 256), ("TJ", 256)]),
-    ("uint16", [("SO", 128), ("OF", 256), ("FO", 128)]),
+    ("uint16", [("SO", 128), ("SP", 128), ("PM0", 16), ("PM1", 16), ("SC", 20), ("OF", 256), ("FO", 128)]),
 ):
     for _n, _c in _l: SCRATCH[_n] = ("sbuf", [128, _c], _d)
 for _b in range(8):
     SCRATCH["B%d" % _b] = ("psum", [128, 512], "float32")
 SEMAPHORES = ["sV", "sS", "sP", "sG", "lq", "lx0", "lx1", "lx2", "lx3", "ca0", "ca1", "cl0", "cl1", "ga0", "ga1", "gl0", "gl1",
-              "y0", "y1", "y2", "y3"]
+              "y0", "y1", "y2", "y3", "y4", "y5", "y6", "y7", "xc0", "xc1"]
 TWO = ("bfloat16", "float16", "uint16")
-CYC, PEC, GAT, FIXV, FIXS, HOP, SELF, GL = 1.0, 0.5, 1.56, 60.0, 90.0, 100.0, 60.0, 3000.0
+CYC, PEC, GAT, SCA, FIXV, FIXS, HOP, SELF, GL = 1.0, 0.5, 1.56, 3.8, 60.0, 90.0, 100.0, 60.0, 3000.0
+TRIES = 300
 PLAN = {}
 
 
@@ -43,6 +52,7 @@ def R(name, a=0, b=None, s=1):
 
 
 def width(r):
+    if r[0] == "ind": return 16 * width(r[2])
     return (r[2] - r[1] + r[3] - 1) // r[3]
 
 
@@ -86,6 +96,9 @@ def build(g, core, T, topo):
     def cp(out, in_):
         add("V", lambda: [g.vector.tensor_copy(ap(out), ap(in_))], [in_], [out], vcost(out, [in_]))
 
+    def scatter(win, off, in_):
+        add("V", lambda: [g.vector.tensor_copy(ap(ind(win, off)), ap(in_))], [in_, off], [win], FIXV + width(in_) * SCA * CYC)
+
     def red(out, in_, op):
         add("V", lambda: [g.vector.tensor_reduce(ap(out), ap(in_), AxisListType.X, op)], [in_], [out], FIXV + max(30, width(in_)) * CYC)
 
@@ -95,14 +108,13 @@ def build(g, core, T, topo):
     def fill(out, v):
         add("V", lambda: [g.vector.memset(ap(out), v)], [], [out], vcost(out, [out]))
 
-    def act(out, in_, func, bias=None, scale=None, acc=None):
+    def act(out, in_, func, bias=None, scale=None):
         def fn():
             kw = {}
             if bias is not None: kw["bias"] = ap(bias)
             if scale is not None: kw["scale"] = ap(scale)
-            if acc is not None: kw["accum_out"] = ap(acc)
             return [g.scalar.activation(ap(out), ap(in_), func, **kw)]
-        add("S", fn, [in_, bias, scale], [out, acc], FIXS + width(out) * (GAT if in_[0] == "ind" else 1.0) * CYC)
+        add("S", fn, [in_, bias, scale], [out], FIXS + width(out) * (GAT if in_[0] == "ind" else 1.0) * CYC)
 
     def mm(items):
         cost = 20.0
@@ -111,8 +123,8 @@ def build(g, core, T, topo):
         add("P", lambda: [g.tensor.matmul(ap(o), ap(l), ap(r), a, b) for o, l, r, a, b in items],
             [x[1] for x in items] + [x[2] for x in items], [x[0] for x in items], cost)
 
-    def group(out, pairs):
-        mm([(out, l, r, n == 0, n == len(pairs) - 1) for n, (l, r) in enumerate(pairs)])
+    def group(out, pairs, start=True, stop=True):
+        mm([(out, l, r, start and n == 0, stop and n == len(pairs) - 1) for n, (l, r) in enumerate(pairs)])
 
     def iota(out, pattern, base, cm):
         small = SCRATCH[out[0]][2] != "int32"
@@ -120,13 +132,16 @@ def build(g, core, T, topo):
         def fn():
             if small: return [g.iota(ap(out), pattern, base, cm, allow_small_or_imprecise_dtypes=True)]
             return [g.iota(ap(out), pattern, base, cm)]
-        add("G", fn, [], [out], 130 + 2 * width(out) * CYC)
+        add("G", fn, [], [out], 150 + 2 * width(out) * CYC)
 
     def ind(win, off):
         return ("ind", win, off)
 
-    def sel(r):
-        return R("SW1", 15 - r, 143 - r)
+    def sel(r, nm="SW1"):
+        return R(nm, 15 - r, 143 - r)
+
+    ID, NID, ONE = R("ID"), R("NID"), R("ONE")
+    rnd = [(R("IC"), ONE), (R("INC"), ONE)]
 
     add("Y", lambda: [g.sync.dma_start(ap(R("QI")), T.q[:]).then_inc(T.sem.lq, 16)], [], [R("QI")], 60, ("lq", 16), 1800)
     for k in range(4):
@@ -135,147 +150,172 @@ def build(g, core, T, topo):
             lambda q=q, k=k: [q.dma_start(ap(R("XT", 512 * k, 512 * k + 512)), T.x[:, 512 * k:512 * k + 512]).then_inc(T.sem["lx%d" % k], 16)],
             [], [R("XT", 512 * k, 512 * k + 512)], 60, ("lx%d" % k, 16), 2300 + 200 * k)
 
-    pc, gc16, rc, gcol, bigc, bjc = (R("PC", k, k + 1) for k in range(6))
+    pc, gc16, rc, gcol, r80, bjc, p4k, g43 = (R("PC", k, k + 1) for k in range(8))
     iota(R("PI", 0, 1), [[0, 1]], 0, 1)
-    iota(R("CI"), [[1, 144]], 0, 0)
-    iota(R("CG"), [[1, 8], [0, 16]], 0, 0)
+    iota(R("CI"), [[1, 146]], 0, 0)
     iota(R("CR"), [[0, 8], [1, 16]], 0, 0)
-    iota(R("CQ"), [[16, 8], [1, 4], [0, 4]], 0, 0)
+    iota(R("CG"), [[1, 8], [0, 16]], 0, 0)
+    iota(R("CQ"), [[1, 36], [0, 4]], 0, 0)
     cp(pc, R("PI", 0, 1))
     ts(R("PI", 1, 2), R("PI", 0, 1), 4, ALU.arith_shift_right)
     cp(gcol, R("PI", 1, 2))
-    ts(R("G8"), R("CI", 0, 8), gcol, ALU.is_equal)
-    ts(R("G8B"), R("CI", 0, 8), gcol, ALU.is_equal)
+    ts(R("G16"), R("CI", 0, 24), -8.0, ALU.add, gcol, ALU.is_equal)
     cp(R("QF"), R("QI"))
     for k in range(8):
-        if k < 5: ts(R("QB", 16 * k, 16 * k + 16), R("QF"), R("G8", k, k + 1), ALU.mult)
-        else: act(R("QB", 16 * k, 16 * k + 16), R("QF"), ACT.Identity, None, R("G8", k, k + 1))
-    ts(gc16, gcol, 16.0, ALU.mult, 15.0, ALU.add)
+        if k < 5: ts(R("QB", 16 * k, 16 * k + 16), R("QI"), R("G16", 8 + k, 9 + k), ALU.mult)
+        else: act(R("QB", 16 * k, 16 * k + 16), R("QF"), ACT.Identity, None, R("G16", 8 + k, 9 + k))
+    fill(ONE, 1.0)
     ts(R("PI", 2, 3), R("PI", 0, 1), 15, ALU.bitwise_and)
     cp(rc, R("PI", 2, 3))
-    ts(bigc, rc, 8.0, ALU.is_ge, BIG, ALU.mult)
+    ts(R("E32"), R("CR", 0, 32), rc, ALU.is_equal)
+    cp(R("G8B"), R("G16", 8, 16)); ts(R("G4"), R("G16"), 4.0, ALU.mult)
+    ts(gc16, gcol, 16.0, ALU.mult, 15.0, ALU.add)
+    ts(g43, gcol, 4.0, ALU.mult, 3.0, ALU.add)
+    ts(p4k, pc, 4096.0, ALU.add)
+    ts(r80, gcol, 256.0 - 37 * 16 % 256, ALU.mult)
     ts(R("PI", 3, 4), R("PI", 0, 1), 2, ALU.arith_shift_right, 3, ALU.bitwise_and)
     ts(R("PI", 4, 5), R("PI", 0, 1), 3, ALU.bitwise_and)
-    ts(R("PC", 6, 7), R("PI", 3, 4), 37.0, ALU.mult)
-    ts(bjc, R("PI", 4, 5), 64.0, ALU.mult, R("PC", 6, 7), ALU.add)
-    ts(R("E16"), R("CI", 0, 16), rc, ALU.is_equal)
-    ts(R("KM"), R("E16"), rc, ALU.mult)
+    ts(R("COL", 4, 5), R("PI", 3, 4), 37.0, ALU.mult)
+    ts(bjc, R("PI", 4, 5), 64.0, ALU.mult, R("COL", 4, 5), ALU.add)
+    act(R("KM"), R("CR", 0, 32), ACT.Identity, 3.0 / 128, 1.0 / 16)
+    iota(R("QS", 0, 16), [[0, 16]], 0, 0); act(R("QS", 16, 32), R("QF"), ACT.Identity, None, 1.0 / 128)
     ts(R("BLKF"), R("CG"), gcol, ALU.is_equal)
-    ts(R("BLK"), R("CG"), gcol, ALU.is_equal)
-    ts(R("ID"), R("CI", 0, 128), pc, ALU.is_equal)
-    for nm, v in (("IH", 1.0), ("I5", 5.0), ("I17", 17.0)):
-        ts(R(nm), R("ID"), v, ALU.mult)
-    for nm, v in (("NID", -1.0), ("W241", 241.0 / 16), ("IDW", 8192.0), ("I16", 16.0)):
-        act(R(nm), R("ID"), ACT.Identity, None, v)
-    ts(R("UU"), R("CI", 0, 128), pc, ALU.is_ge)
+    act(R("BLK"), R("BLKF"), ACT.Copy)
+    ts(ID, R("CI", 0, 128), pc, ALU.is_equal)
+    for nm, v in DIAG.items(): act(R(nm), ID, ACT.Identity, None, v)
+    act(R("BP"), R("BLK"), ACT.Identity, None, 2048.0); act(R("BN"), R("BLK"), ACT.Identity, None, -2048.0)
+    ts(R("COL", 6, 7), pc, -256.0, ALU.mult, -128.0, ALU.add)
+    act(R("UU"), R("CI"), ACT.Sigmoid, R("COL", 6, 7), 256.0)
     ts(R("TMP"), R("CR"), rc, ALU.is_ge)
     tt(R("TRI"), R("TMP"), R("BLK"), ALU.mult)
     tt(R("TRU"), R("BLK"), R("TRI"), ALU.subtract)
-    ts(R("SW1"), R("CI"), gc16, ALU.is_equal)
-    for q in range(4):
-        ts(R("SQ", 128 * q, 128 * q + 128), R("CQ"), 4.0 * q, ALU.add, pc, ALU.is_equal)
-    fill(R("ONE"), 1.0); fill(R("NEG"), -1.0); fill(R("T255"), 255.0)
+    ts(R("SW1"), R("CI", 0, 144), gc16, ALU.is_equal)
+    act(R("SW16"), R("SW1"), ACT.Identity, None, 1.0 / 16)
+    ts(R("SW4"), R("CQ"), g43, ALU.is_equal)
+    ts(R("MK"), R("CR"), rc, ALU.is_equal)
+    ts(R("JB"), R("MK"), p4k, ALU.mult, -4096.0, ALU.add)
+    ts(R("COL", 5, 6), rc, 4.0, ALU.mult, 4640.0, ALU.add)
+    ts(R("JS", 0, 1), rc, 0.0, ALU.is_gt, R("COL", 5, 6), ALU.mult)
+    act(R("TM255"), ONE, ACT.Identity, None, -255.0)
     cp(R("QH", 0, 128), R("CI", 0, 128))
     for a in (128, 256, 512, 1024):
         b = min(2 * a, NH); ts(R("QH", a, b), R("QH", 0, b - a), float(a), ALU.add)
-    fill(R("XR", 7 * W, ZS), 0.0); fill(R("Z", K, K + 16), 0.0)
-    fill(R("AS", 0, 16), 0.0); fill(R("AS", 144, 160), 0.0); fill(R("A5", 0, 16), 0.0)
-    fill(R("W3"), BIG); fill(R("W2"), BIG); fill(R("W35", 256, 264), BIG); fill(R("W25", 16, 24), BIG)
+    cp(R("CIB"), R("QH", 0, 256))
+    for r in (R("XA", 2 * W, ZS), R("XB", 2 * W, ZS), R("Z", K, K + 16)): iota(r, [[0, 16]], 0, 0)
+    for r in (R("W3", 128, 136), R("W3", 264, 272), R("W35", 256, 264)): iota(r, [[0, 8]], int(BIG), 0)
 
     def round_constants(t):
-        iota(R("TI"), [[37, 256]], t, 0)
-        ts(R("TJ"), R("TI"), 255, ALU.bitwise_and)
-        cp(R("TF"), R("TJ")); cp(R("QN%d" % t), R("TF"))
-        iota(R("TF"), [[148, 256]], t, 0)
-        ts(R("TI"), R("TF"), bjc, ALU.add)
-        ts(R("TJ"), R("TI"), 255, ALU.bitwise_and)
-        cp(R("TF"), R("TJ"))
-        ts(R("J5%d" % t), R("TF"), 5.0, ALU.mult, -1.0, ALU.add)
+        iota(R("TI", 128, 144), [[37 * 16, 16]], t, 37)
+        ts(R("TJ", 128, 144), R("TI", 128, 144), 255, ALU.bitwise_and)
+        ts(R("TI", 144, 160), R("TJ", 128, 144), r80, ALU.add)
+        ts(R("TJ", 144, 160), R("TI", 144, 160), 255, ALU.bitwise_and)
+        cp(R("PM%d" % t), R("TJ", 144, 160))
+        iota(R("TF"), [[148, 128]], t, 0)
+        ts(R("TI", 0, 128), R("TF"), bjc, ALU.add)
+        ts(R("TJ", 0, 128), R("TI", 0, 128), 255, ALU.bitwise_and)
+        ts(R("J5%d" % t), R("TJ", 0, 128), 5.0, ALU.mult, -793.5, ALU.add)
+        iota(R("WN", 0, CAP), [[0, CAP]], 0, 0)
+        iota(R("WP", 0, MP), [[0, MP]], 0, 0)
         if t == 0:
-            iota(R("TT"), [[16, 128]], 0, 0)
+            iota(R("TT"), [[16, 128]], 1 + X1 - ZS, 0)
             ts(R("PL"), R("TT"), rc, ALU.add)
-            iota(R("QS"), [[1, NH - 16 * HC[2]]], 16 * HC[2], 0)
 
-    def search(bank, c0, c1, qry, t1, w2, w3, s_first=None, parts=1):
-        n = c1 - c0; fl = R("SF", 16 * c0, 16 * c1); so = R("SO", c0, c1); pb = R(bank, 0, n)
+    def starts(tb, jb, src, a, col, bias):
+        group(tb, [(R(src, a, a + 128), R("BLK"))])
+        group(jb, [(ID, R("JB")), (R(src, a, a + 128), R("BP")), (R(src, a + 1, a + 129), R("BN"))])
+        tt(R("L1", col, col + 128), tb, R("MK"), ALU.mult)
+        act(R("L2", col, col + 128), jb, ACT.Relu, bias)
 
-        def count(first):
-            group(pb, first + [(sel(r), R("SF", 16 * c0 + r, 16 * c1, 16)) for r in range(16)])
-        if s_first is None: ts(fl, qry, t1, ALU.is_ge)
-        else: act(fl, s_first[0], ACT.Sigmoid, s_first[1], 256.0)
-        count([])
-        yield
-        for w in (w2, w3):
-            cp(so, pb); act(R("SB", c0, c1), pb, ACT.Copy)
-            m = n // parts
-            for u in range(parts):
-                tt(R("SF", 16 * (c0 + u * m), 16 * (c0 + u * m + m)), ind(w, R("SO", c0 + u * m, c0 + u * m + m)),
-                   R(qry[0], qry[1] + 16 * u * m, qry[1] + 16 * (u * m + m)), ALU.is_le)
-            count([(R("I16"), R("SB", c0, c1))])
-            yield
-        cp(so, pb)
-        yield
+    def places(win, a, u, banks):
+        c = 128 * u; o, e = R(banks[0], 128, 138), R(banks[0], 136, 137)
+        starts(R(banks[0], 0, 128), R(banks[1], 0, 128), "AS", a, c, 520.0)
+        mm([(o, R("L1", c, c + 128), R("G16", 8, 18), True, False), (o, R("L2", c, c + 128), R("G4", 8, 18), False, False),
+            (e, sel(0), R("AS", a + 144, a + 145), False, False), (e, ID, R("JS", 0, 1), False, True)])
+        cp(R("SC", 10 * u, 10 * u + 10), o)
+        scatter(R(win), R("SC", 10 * u, 10 * u + 9), R("CIB", 0, 144))
+        group(R(banks[2], 0, 128), [(R("TRI"), R("AS", a + 1, a + 129)), (R("TRU"), R("AS", a, a + 128))])
+        act(R("W3", 136 * u, 136 * u + 128), R(banks[2], 0, 128), ACT.Copy)
+
+    def marks(win, c0, c1, z=0):
+        w = R(win, 16 * (c0 - z), 16 * (c1 - z))
+        scan(R("BL", 16 * c0, 16 * c1), w, w, R("BL", 16 * c0 - 1, 16 * c0) if c0 > z else 0.0, ALU.max, ALU.max)
+
+    def blocks(bank, c0, c1):
+        group(R(bank, 0, c1 - c0), [(sel(r, "SW16"), R("BL", 16 * c0 + r, 16 * c1, 16)) for r in range(16)])
+        cp(R("SO", c0, c1), R(bank, 0, c1 - c0)); act(R("SB", c0, c1), R(bank, 0, c1 - c0), ACT.Identity, None, -1.0)
+
+    def within(bank, w3, c0, c1, ns, sub, z=0):
+        h = c1 - ns
+        if ns:
+            act(R("SH", 16 * h, 16 * c1), ind(w3, R("SO", h, c1)), ACT.Copy)
+            group(R(sub, 0, 16 * ns), [(ID, R("QH", 16 * h, 16 * c1)), (NID, R("SH", 16 * h, 16 * c1))])
+            act(R("SF", 16 * h, 16 * c1), R(sub, 0, 16 * ns), ACT.Sigmoid, 128.0, 256.0)
+        if h > c0: tt(R("SF", 16 * c0, 16 * h), ind(w3, R("SO", c0, h)), R("QH", 16 * (c0 - z), 16 * (h - z)), ALU.is_le)
+        group(R(bank, 0, c1 - c0), [(R("IN16"), R("SB", c0, c1))] + [(sel(r), R("SF", 16 * c0 + r, 16 * c1, 16)) for r in range(16)])
+        cp(R("SP", c0, c1), R(bank, 0, c1 - c0))
+
+    def count_piece(t, u0, u1, scalar, first, last):
+        bank = "B%d" % ((u0 // 4, u0 // 2)[u1 - u0 < 4] % 4)
+        items = []
+        for u in range(u0, u1):
+            o = R(bank, 128 * (u - u0), 128 * (u - u0) + 128); a = 128 * u
+            if t == 0: items.append((o, R("XT", a, a + 128), R("QB"), True, True))
+            else: items += [(o, R("TM255"), R("QB"), True, False), (o, R("XB", X1 + a, X1 + a + 128), R("QB"), False, True)]
+        mm(items)
+        nz, pb = R("NZ", 128 * u0, 128 * u1), R(bank, 0, 128 * (u1 - u0))
+        if scalar:
+            act(R("NZ2"), pb, ACT.Sign); act(nz, R("NZ2"), ACT.Square)
+        else: ts(nz, pb, 0.0, ALU.not_equal)
+        return lambda: group(R("B7", 0, 1), [(R("NZ", 128 * u, 128 * u + 128), R("ONE", 0, 1)) for u in range(u0, u1)], first, last)
 
     others = [r for r in range(NR) if r != rank]
+    for f in [count_piece(0, 4 * k, 4 * k + 4, k == 0, k == 1, k == 3) for k in (1, 0, 2, 3)]: f()
     for t in range(2):
-        LD, GE = "LD%d" % t, "GE%d" % t
-        for k in range(4):
-            group(R("B%d" % k), [(R("QB"), R("XT", 512 * k, 512 * k + 512))])
-        slot = 4 * rank
-        for k in range(2):
-            ts(R("NZ", 512 * k, 512 * k + 512), R("B%d" % k), 0.0, ALU.not_equal)
-            red(R(LD, slot + k, slot + k + 1), R("NZ", 512 * k, 512 * k + 512), ALU.add)
-        for k in range(2, 4):
-            act(R("NZ", 512 * k, 512 * k + 512), R("B%d" % k), ACT.Sign)
-            act(R("NZ2", 512 * (k - 2), 512 * (k - 1)), R("NZ", 512 * k, 512 * k + 512), ACT.Square, acc=R(LD, slot + k, slot + k + 1))
-        counted = len(ops) - 1
+        LD, GE, XR = "LD%d" % t, "GE%d" % t, ("XA", "XB")[t]
+        mine = R(LD, 4 * rank, 4 * rank + 1)
+        cp(mine, R("B7", 0, 1))
 
-        def send_counts(t=t, LD=LD, slot=slot):
-            mine = ap(R(LD, slot, slot + 4)); ids = []; m = None
+        def send_counts(t=t, mine=mine):
+            ids = []; m = None
             for r in others:
                 rid, pid = topo.addr(T.cores[r], core); ids.append(DstId(rid=rid, pnc=pid))
                 mk = topo.mask(core, T.cores[r]); m = mk if m is None else m & mk
-            return [g.remote_dma_fused([RemoteDMATransfer(dst_ids=ids, dma_engine_mask=m, remote_sem=T.sem["ca%d" % t], src=mine,
-                                                          dsts=[mine] * len(ids))], local_sem=T.sem["cl%d" % t])]
+            return [g.remote_dma_fused([RemoteDMATransfer(dst_ids=ids, dma_engine_mask=m, remote_sem=T.sem["ca%d" % t], src=ap(mine),
+                                                          dsts=[ap(mine)] * len(ids))], local_sem=T.sem["cl%d" % t])]
         ne = len(topo.engines(core, T.cores[others[0]]))
         add("G", send_counts, [R(LD)], [R("COL", 8 + t, 9 + t)], 300, ("cl%d" % t, ne), 3000)
+        sent = len(ops) - 1
         add("A", None, [R("COL", 8 + t, 9 + t)], [R(LD, 0, 32, 2)], 0, ("ca%d" % t, ne * len(others)), 2000)
-        after[0] = counted if t == 1 else None
+        after[0] = sent if t == 1 else None
         round_constants(t)
+        after[0] = sent
+        iota(R("WS", 0, NH), [[0, NH]], 0, 0)
         after[0] = None
-        for u in range(28):
-            c, h = 6 - u // 4, u % 4
-            o, i = R("XR", c * W + 512 * h, c * W + 512 * h + 512), R("XT", 512 * h, 512 * h + 512)
-            if 4 <= u < 4 + VC[t]: ts(o, i, -1.0, ALU.mult, 255.0, ALU.add)
-            else: act(o, i, ACT.Identity, 255.0, -1.0)
-        tot, mn, coef = R("COL", 0, 1), R("COL", 1, 2), R("COL", 2, 3)
-        red(tot, R(LD), ALU.add)
-        ts(R("KD"), R("E16"), tot, ALU.mult, 16.0, ALU.mult)
-        group(R("B4", 0, 16), [(R("BLKF"), R("KM")), (R("BLKF"), R("KD"))])
-        red(mn, R("B4", 0, 16), ALU.min)
-        ts(R("OH"), R("B4", 0, 16), mn, ALU.is_equal)
-        tt(R("OQ"), R("OH"), R("QF"), ALU.mult)
-        red(coef, R("OQ"), ALU.add)
-        ts(R("C8"), R("G8"), coef, ALU.mult)
         if t == 0:
-            tt(R("OQ"), R("OH"), R("E16"), ALU.mult)
-            ts(R("OQ"), R("OQ"), 524288.0, ALU.mult)
-            tt(R("KM"), R("KM"), R("OQ"), ALU.add)
-        mm([(R("B5", r, 128, 16), R("XT", r, W, 16), R("C8"), True, True) for r in range(16)])
-        ts(R("FS", 128, 256), R("B5", 0, 128), 0.0, ALU.is_lt)
-        ts(R("FS", 0, 128), R("B5", 0, 128), 0.0, ALU.is_gt)
-        mm([(R("B6", 128, 256), R("FS", 128, 256), R("UU"), True, True), (R("B6", 0, 128), R("FS", 0, 128), R("UU"), True, True)])
-        cp(R("AS", 160, 288), R("B6", 128, 256)); cp(R("AS", 16, 144), R("B6", 0, 128))
-        group(R("B4", 0, 2), [(sel(r), R("AS", 31 + 16 * r, 31 + 16 * r + 145, 144)) for r in range(8)])
-        ts(R("T1", 0, 2), R("B4", 0, 2), bigc, ALU.add)
-        group(R("B3", 0, 17), [(sel(r), R("AS", 16 + r, 288, 16)) for r in range(16)])
-        act(R("W2", 16, 24), R("B3", 9, 17), ACT.Copy); act(R("W2", 0, 8), R("B3", 0, 8), ACT.Copy)
-        mm([(R("B7", 128, 256), R("TRI"), R("AS", 160, 288), True, False), (R("B7", 128, 256), R("TRU"), R("AS", 159, 287), False, True),
-            (R("B7", 0, 128), R("TRI"), R("AS", 16, 144), True, False), (R("B7", 0, 128), R("TRU"), R("AS", 15, 143), False, True)])
-        act(R("W3", 136, 264), R("B7", 128, 256), ACT.Copy); act(R("W3", 0, 128), R("B7", 0, 128), ACT.Copy)
-        win = R("XR", X6, ZS)
-        for _ in search("B0", 64, 80, R("QN%d" % t), R("T1", 1, 2), R("W2", 16, 32), R("W3", 136, 272)): pass
-        act(R("GN"), ind(win, R("SO", 64, 80)), ACT.Identity, 255.0, -1.0)
+            for k in range(4): ts(R(XR, X1 + 512 * k, X1 + 512 * k + 512), R("XT", 512 * k, 512 * k + 512), -1.0, ALU.mult, 255.0, ALU.add)
+        add("Y", lambda XR=XR, t=t: [g.sync.dma_start(ap(R(XR, 0, W)), ap(R(XR, X1, X1 + W))).then_inc(T.sem["xc%d" % t], 16)],
+            [R(XR, X1, X1 + W)], [R(XR, 0, W)], 60, ("xc%d" % t, 16), 4000)
+        mn0, mn1, coef = R("COL", 0, 1), R("COL", 1, 2), R("COL", 2, 3)
+        group(R("B4", 0, 32), [(ID, R("KM")), (ID, R("QS"))] + [(R("IC"), R("US"))] * t, True, False)
+        red(R("COL", 3, 4), R(LD, 0, 32, 4), ALU.add)
+        ts(R("KD"), R("E32"), R("COL", 3, 4), ALU.mult)
+        group(R("B4", 0, 32), [(R("BLKF"), R("KD"))], False, True)
+        red(mn0, R("B4", 0, 16), ALU.min); red(mn1, R("B4", 16, 32), ALU.min)
+        ts(coef, mn1, mn0, ALU.subtract, 128.0, ALU.mult)
+        ts(R("CB"), R("BLK"), coef, ALU.mult)
+        if t == 0: ts(R("US"), R("B4", 0, 32), mn0, ALU.subtract, 1.0 / 32, ALU.is_lt)
+        c8 = R("CB", 0, 128, 16)
+        mm([(R("B5", 0, 128), R("TM255"), R("CB"), True, False)]
+           + [(R("B5", r, 128, 16), R(XR, X1 + r, X1 + W, 16), c8, False, r == 15) for r in range(16)])
+        ts(R("FS", 128, 256), R("B5", 0, 128), 0.0, ALU.is_gt)
+        ts(R("FS", 0, 128), R("B5", 0, 128), 0.0, ALU.is_lt)
+        group(R("B6", 0, 146), [(R("FS", 128, 256), R("UU"))]); group(R("B7", 0, 146), [(R("FS", 0, 128), R("UU"))])
+        act(R("AS", AN, AN + 146), R("B6", 0, 146), ACT.Copy); cp(R("AS", 0, 146), R("B7", 0, 146))
+        win = R(XR, X1, ZS)
+        places("WN", AN, 1, ("B0", "B1", "B6"))
+        marks("WN", 64, 80, 64); blocks("B4", 64, 80); within("B4", R("W3", 136, 272), 64, 80, 0, None, 64)
+        act(R("G0"), ind(win, R("SP", 64, 80)), ACT.Identity, 255.0, -1.0)
+        act(R("GN"), ind(R("G0"), R("PM%d" % t)), ACT.Copy)
         partner = T.cores[rank ^ XS[t]]
 
         def send_guests(t=t, GE=GE, partner=partner):
@@ -284,137 +324,130 @@ def build(g, core, T, topo):
         ne = len(topo.engines(core, partner))
         add("G", send_guests, [R("GN")], [R("COL", 10 + t, 11 + t)], 300, ("gl%d" % t, ne), GL)
         add("A", None, [R("COL", 10 + t, 11 + t)], [R(GE, 0, CAP)], 0, ("ga%d" % t, ne), 1200)
+        places("WP", 0, 0, ("B2", "B3", "B7"))
+        marks("WP", 0, 64); blocks("B0", 0, 64)
         for s in range(2):
-            for _ in search("B%d" % (1 + s), 32 * s, 32 * s + 32, R("QH", 512 * s, 512 * s + 512), R("T1", 0, 1), R("W2", 0, 16),
-                            R("W3", 0, 136), None, 2 - s): pass
-            cp(R("A16", 32 * s, 32 * s + 32), R("B%d" % (1 + s), 0, 32))
-            act(R("PRS", 512 * s, 512 * s + 512), ind(win, R("SO", 32 * s, 32 * s + 32)), ACT.Copy)
-        tt(R("TT"), R("AS", 159, 287), R("AS", 160, 288), ALU.subtract)
-        ts(R("TT"), R("TT"), 8192.0, ALU.mult, 8192.0, ALU.add)
-        tt(R("KEY"), R("TT"), R("W3", 136, 264), ALU.add)
-        tt(R("TU"), R("W3", 136, 264), R("PL"), ALU.subtract)
-        ts(R("DL"), R("TU"), float(ZS - X6 - 1), ALU.add)
+            c = 128 * s; pbk = R("B%d" % (5 + s), 0, 128); ab = R("B7" if s else "B3", 0, 128); a = R("AP", c, c + 128)
+            group(ab, [(R("SW4", 12 - 4 * q, 140 - 4 * q), R("BL", 512 * s + q, 512 * s + 512, 4)) for q in range(4)], True, False)
+            within("B%d" % s, R("W3", 0, 136), 32 * s, 32 * s + 32, PS[s], "B2")
+            act(R("PRS", 512 * s, 512 * s + 512), ind(win, R("SP", 32 * s, 32 * s + 32)), ACT.Copy)
+            group(ab, [(R("SW4", 12 - 4 * q, 140 - 4 * q), R("SF", 512 * s + q, 512 * s + 512, 4)) for q in range(4)], False, True)
+            ts(a, ab, 2047.0, ALU.min, -1023.5, ALU.add)
+            group(pbk, [(R("I238"), ONE), (NID, R("J5%d" % t)), (R("IN16"), a)] + rnd + [(ID, R("J5%d" % t)), (R("I17"), a)])
+        group(R("B2", 0, 128), [(R("TRI"), R("AS", AN + 1, AN + 129)), (R("TRU"), R("AS", AN, AN + 128)), (R("IK"), ONE),
+                                (R("INK"), R("AS", AN + 1, AN + 129)), (R("IK"), R("AS", AN, AN + 128))])
+        act(R("KEY"), R("B2", 0, 128), ACT.Copy)
+        act(R(GE, 256, 512), R(GE, 0, 256), ACT.Copy)
+        turn = 0
         for s in range(2):
-            c = 128 * s; pbk = R("B%d" % (5 + s), 0, 128); ab = "B7" if s else "B3"
-            mm([(R(ab, q, 128, 4), R("SQ", 128 * q, 128 * q + 128), R("A16", 32 * s, 32 * s + 32), True, True) for q in range(4)])
-            cp(R("AP", c, c + 128), R(ab, 0, 128))
-            act(R("AK", c, c + 128), R(ab, 0, 128), ACT.Identity, -(K1 + C0))
-            first = [(R("I17"), R("AP", c, c + 128)), (R("IH"), R("J5%d" % t, c, c + 128)), (R("W241"), R("NEG"))]
-            group(pbk, first)
-            act(R("HH", c, c + 128), pbk, ACT.Identity, C0 - 1023.5 + K1)
-            group(pbk, first + [(R("NID"), R("HH", c, c + 128))])
-            ts(R("OF", c, c + 128), pbk, K1 + C0, ALU.add)
-        cp(R(GE, 256, 512), R(GE, 0, 256)); act(R(GE, 512, 704), R(GE, 0, 192), ACT.Copy)
-        group(R("B4"), [(R("ID"), R("PRS", 0, 512))])
-        for kk in range(4):
-            tt(R("Z", kk, W, 4), R("B4"), R(GE, 64 * kk, 64 * kk + 512), ALU.subtract)
-        for kk in range(4):
-            bk = R("B%d" % (kk % 2))
-            group(bk, [(R("ID"), R("PRS", 512, 1024)), (R("NID"), R(GE, 64 * kk, 64 * kk + 512))])
-            act(R("Z", W + kk, K, 4), bk, ACT.Copy)
-        xw = R("XR", 0, 7 * W); m1 = (128 - MV + 2) // 4 * 2; cut = (0, m1, 128 - MV)
+            nv = ZV[s]; pv = R(("B4", "B7")[s], 0, nv)
+            group(pv, [(ID, R("PRS", 512 * s, 512 * s + nv))])
+            for kk in range(4): tt(R("Z", W * s + kk, W * s + 4 * nv, 4), pv, R(GE, 64 * kk, 64 * kk + nv), ALU.subtract)
+            for i in range(nv, 512, 128):
+                bank = ("B2", "B3")[turn % 2]; turn += 1; m = min(128, 512 - i)
+                for kk in range(4):
+                    group(R(bank, kk, 4 * m, 4), [(ID, R("PRS", 512 * s + i, 512 * s + i + m)),
+                                                  (NID, R(GE, i % 256 + 64 * kk, i % 256 + 64 * kk + m))])
+                act(R("Z", W * s + 4 * i, W * s + 4 * (i + m)), R(bank, 0, 4 * m), ACT.Copy)
+        xw = R(XR, 0, 2 * W); m1 = M1; cut = (0, m1, 128 - MV)
         tal = (R("B7", 0, 128), R("B4", 0, 128))
 
         def part(n, s):
-            c = 128 * s
-            return (c, W * s, R("B%d" % (5 + s), 0, 128), R("DD", c, c + 128), R("EQ", 256 * n + c, 256 * n + c + 128),
-                    R("FF", 256 * n + c, 256 * n + c + 128))
+            c = 256 * n + 128 * s
+            return R("B%d" % (5 + s), 0, 128), R("ST", c, c + 128), R("FF", c, c + 128), R("AP", 128 * s, 128 * s + 128)
 
-        def counts(n, s):
+        def counts(s):
             mm([(R("B3", 128 * s + r, 128 * s + 128, 16), R("FL", W * s + r, W * s + W, 16), R("G8B"), True, True) for r in range(16)])
 
         def relu(n, s):
-            act(part(n, s)[5], R("B3", 128 * s, 128 * s + 128), ACT.Relu, -1.0, 16.0)
+            act(part(n, s)[2], R("B3", 128 * s, 128 * s + 128), ACT.Relu, -16.0, 129.0)
 
-        def same(n, s):
-            ts(part(n, s)[4], part(n, s)[3], 0.0, ALU.is_equal, 255.0, ALU.mult)
+        def state(n, s):
+            ts(part(n, s)[1], R("OF", 128 * s, 128 * s + 128), -2048.0, ALU.add)
 
         def tally(n, s):
-            mm([(tal[s], R("ID"), part(n, s)[4], n == 0, False), (tal[s], part(n, s)[5], R("ID"), False, n == PR - 1)])
-
-        def step(n, s):
-            c, _, _, d, eq, f = part(n, s)
-            return [(R("I5"), d), (R("I5"), R("AP", c, c + 128)), (R("W241"), eq), (f, R("W241"))]
-
-        def strand(r):
-            return R("B2", r // 16 * 128 + r % 16, r // 16 * 128 + 128, 16)
-        ts(R("CB", 0, 128), R("BLK"), coef, ALU.mult); ts(R("CB", 128, 256), R("BLK"), coef, ALU.mult); ts(R("NC8"), R("C8"), -1.0, ALU.mult)
-        mm([(R("B2", 0, 256), R("T255"), R("CB"), True, False)])
-        for u in range(0, 32, 8):
-            mm([(strand(r), R("PRS", r // 16 * 512 + r % 16 // 4, r // 16 * 512 + 512, 4), R("NC8"), False, False) for r in range(u, u + 8)])
+            _, st, _, a = part(n, s)
+            if n < ET: group(tal[s], [(NID, st), (ID, a)] + rnd, n == 0, False)
+            else: group(tal[s], [(part(u, s)[2], R("IN128")) for u in (range(4) if n == ET else range(4, PR - 1))], False, n == PR - 2)
         chain[0] = True
         for k in range(2 * PR):
             n, s = k // 2, k % 2; pn, ps = (k - 1) // 2, (k - 1) % 2
-            c, e, pbk, d, eq, f = part(n, s)
+            c, e = 128 * s, W * s
+            pbk, st, f, a = part(n, s)
             gs = [R("GS", NS * s + 16 * cut[h], NS * s + 16 * cut[h + 1]) for h in range(2)]
             zs = [(e + 16 * (MV + cut[h]), e + 16 * (MV + cut[h + 1])) for h in range(2)]
             bk = [R("B%d" % h, 0, 16 * (cut[h + 1] - cut[h])) for h in range(2)]
-            if n > 0: ts(R("OF", c, c + 128), pbk, K1, ALU.add)
-            if k > 0: same(pn, ps)
-            if n > 0: ts(R("HH", c, c + 128), R("OF", c, c + 128), C0 - 1023.5, ALU.add)
-            mm([(bk[0], R("ID"), R("Z", *zs[0]), True, False)])
-            if k > 0: counts(pn, ps)
-            mm([(bk[1], R("ID"), R("Z", *zs[1]), True, False)])
+            ts(R("OF", c, c + 128), pbk, 1809.0, ALU.add)
+            if 0 < k < 2 * PR - 1: state(pn, ps)
+            mm([(bk[0], ID, R("Z", *zs[0]), True, False)])
+            more = k > 0 and pn < PR - 1
+            if more: counts(ps)
+            if more: group(part(pn, ps)[0], [(R("I238"), ONE), (ID, part(pn, ps)[3]), (R("IN5"), part(pn, ps)[1])], True, False)
+            mm([(bk[1], ID, R("Z", *zs[1]), True, False)])
             act(gs[0], ind(xw, R("OF", c + MV, c + MV + m1)), ACT.Copy)
-            if k > 0: relu(pn, ps)
-            mm([(bk[0], R("NID"), gs[0], False, True)])
-            if k > 0 and pn < PR - 1: group(part(pn, ps)[2], step(pn, ps))
-            if n > 0: group(pbk, step(n - 1, s) + [(R("NID"), R("HH", c, c + 128))])
+            if more: relu(pn, ps)
+            mm([(bk[0], NID, gs[0], False, True)])
+            if more:
+                pb, pst, pf, _ = part(pn, ps)
+                group(pb, [(pf, R("IN113"))] + rnd + [(pf, R("I113")), (R("I5"), pst)], False, True)
             act(gs[1], ind(xw, R("OF", c + MV + m1, c + 128)), ACT.Copy)
-            mm([(bk[1], R("NID"), gs[1], False, True)])
+            if n == PR - 1:
+                state(n, s)
+            mm([(bk[1], NID, gs[1], False, True)])
             tt(R("FL", e, e + 16 * MV), ind(xw, R("OF", c, c + MV)), R("Z", e, e + 16 * MV), ALU.is_lt)
             for h in range(2):
                 act(R("FL", *zs[h]), bk[h], ACT.Sigmoid, -128.0, 256.0)
-            tt(d, pbk, R("AK", c, c + 128), ALU.subtract)
-            if k == 2 * PR - 1: same(n, s)
-            if k > 0: tally(pn, ps)
+            if more: tally(pn, ps)
             if 2 <= k < 10:
-                mm([(strand(r), R(GE, r % 16 // 4 + 64 * (r % 4), r % 16 // 4 + 64 * (r % 4) + 509, 4), R("C8"), False, r == 31)
-                    for r in range(4 * k - 8, 4 * k - 4)])
-            if k == 10: act(R("SG"), R("B2", 0, 256), ACT.Sign, 0.5)
-            if k in (12, 13): mm([(tal[s], R("SG", c, c + 128), R("IDW"), False, False)])
+                v, u = (k - 2) // 4, (k - 2) % 4
+                mm([(R("B2", 128 * v, 128 * v + 128), R("TM255"), R("CB"), True, False)] * (u == 0)
+                   + [(R("B2", 128 * v + r, 128 * v + 128, 16), R("Z", W * v + r, W * v + W, 16), c8, False, r == 15) for r in range(4 * u, 4 * u + 4)])
+            if k == 10: act(R("SG"), R("B2", 0, 256), ACT.Sign, 0.5, -1.0)
         chain[0] = False
         for s in range(2):
-            c = 128 * s
-            if s == 1:
-                counts(PR - 1, 1); relu(PR - 1, 1); tally(PR - 1, 1)
-            ts(R("RR", c, c + 128), tal[s], 8197.0, ALU.max)
-            tt(R("AL", c, c + 128), tal[s], R("RR", c, c + 128), ALU.is_equal)
-            scan(R("A5", 16 + c, 144 + c), R("ONE"), R("AL", c, c + 128), R("A5", 15 + c, 16 + c), ALU.mult, ALU.add)
-            mm([(R("B2", 0, 1), sel(r), R("A5", 31 + 16 * r, 32 + 16 * r), r == 0, r == 15) for r in range(8 * s, 8 * s + 8)]
-               + [(R("B2", 1, 2), R("BLK"), R("A5", 271, 272), True, True)] * s)
-        cp(R("T5", 0, 2), R("B2", 0, 2))
-        act(R("T5", 2, 3), R("T5", 0, 1), ACT.Identity, 128.0, -256.0)
-        group(R("B3", 0, 16), [(sel(r), R("A5", 16 + r, 272, 16)) for r in range(16)])
-        act(R("W25", 0, 16), R("B3", 0, 16), ACT.Copy)
-        group(R("B0", 0, 256), [(R("TRI"), R("A5", 16, 272)), (R("TRU"), R("A5", 15, 271))])
-        act(R("W35", 0, 256), R("B0", 0, 256), ACT.Copy)
-        zw = R("Z")
-        ts(R("TT"), R("KEY"), R("T5", 1, 2), ALU.is_le)
-        se = [search("B%d" % (4 + u), HC[u], HC[u + 1], R("QH", 16 * HC[u], 16 * HC[u + 1]), R("T5", 0, 1), R("W25"), R("W35"),
-                     (R("QS"), R("T5", 2, 3)) if u == 2 else None) for u in range(3)]
-        done = [0, 0, 0]; chain[0] = True
-        for u in (0, 2, 1, 0, 1, 0, 2, 0, 1, 2, 1, 2):
-            next(se[u]); done[u] += 1
-            if done[u] < 4: continue
-            a, b = HC[u], HC[u + 1]
-            if u == 1:
-                tt(R("TU"), R("TT"), R("DL"), ALU.mult)
-                tt(R("TT"), R("TU"), R("PL"), ALU.add)
-                cp(R("FO"), R("TT"))
-            if u == 2:
-                h = a + 24
-                ts(R("XR", ZS + 16 * a, ZS + 16 * h), ind(zw, R("SO", a, h)), 0.0, ALU.max)
-                act(R("XR", ZS + 16 * h, ZS + 16 * b), ind(zw, R("SO", h, b)), ACT.Relu)
-            else: act(R("XR", ZS + 16 * a, ZS + 16 * b), ind(zw, R("SO", a, b)), ACT.Relu)
-        chain[0] = False
-        fw = R("XR", X6, ZS + NH)
-        for k in range(4):
-            o = R("XT", 512 * k, 512 * k + 512); src = ind(fw, R("FO", 32 * k, 32 * k + 32))
-            if k < 2: ts(o, src, -1.0, ALU.mult, 255.0, ALU.add)
-            else: act(o, src, ACT.Identity, 255.0, -1.0)
-            if t == 1:
-                add("Y", lambda k=k, o=o: [g.sync.dma_start(T.y[:, 512 * k:512 * k + 512], ap(o)).then_inc(T.sem["y%d" % k], 16)],
+            c = 128 * s; last = "B%d" % (5 + s); al = R("AL", c, c + 128)
+            if RS[s] & 1: act(R("RR", c, c + 128), tal[s], ACT.Identity, 1536.0 - 6144.0 / MOD, 1.0 / MOD)
+            else: ts(R("RR", c, c + 128), tal[s], 1.0 / MOD, ALU.mult, 1536.0 - 6144.0 / MOD, ALU.add)
+            if RS[s] & 2: act(R("RB", c, c + 128), R("RR", c, c + 128), ACT.Identity, 14336.0 - 1536.0 * MOD, MOD)
+            else: ts(R("RB", c, c + 128), R("RR", c, c + 128), MOD, ALU.mult, 14336.0 - 1536.0 * MOD, ALU.add)
+            tt(R("GM", c, c + 128), tal[s], R("RB", c, c + 128), ALU.subtract)
+            for u in range(ET, PR): group(R(last, 0, 128), [(part(u, s)[1], NID), (part(u, s)[3], ID)] + rnd, u == ET, False)
+            group(R(last, 0, 128), [(R("IK"), R("SG", c, c + 128)), (R("GM", c, c + 128), ID)], False, False)
+            mm([(R(last, r, 128, 16), R("FL", W * s + r, W * s + W, 16), R("G8B"), False, r == 15) for r in range(16)])
+            ts(al, R(last, 0, 128), 8192.5, ALU.is_gt)
+            pre = R(tal[s][0], s, 129)
+            group(pre, [(R("AL", 0, 128), ONE)] * s + [(al, R("UU", s, 129))])
+            act(R("A5", 15 + s + c, 144 + c), pre, ACT.Copy)
+            starts(R("B%d" % (2 * s), 0, 128), R("B%d" % (2 * s + 1), 0, 128), "A5", 15 + c, c, 1030.0 + c)
+            group(R(last, 0, 8), [(R("L1", c, c + 128), R("G16", 8, 16)), (R("L2", c, c + 128), R("G4", 8, 16))])
+            cp(R("SC", 8 * s, 8 * s + 8), R(last, 0, 8))
+            scatter(R("WS"), R("SC", 8 * s, 8 * s + 8), R("CIB", c, c + 128))
+        group(R("B3", 0, 256), [(R("TRI"), R("A5", 16, 272)), (R("TRU"), R("A5", 15, 271))])
+        act(R("W35", 0, 256), R("B3", 0, 256), ACT.Copy)
+        group(R("B7", 0, 1), [(R("BLK"), R("A5", 271, 272))])
+        ts(R("TK"), R("KEY"), R("B7", 0, 1), ALU.subtract, 0.0, ALU.max)
+        group(R("B7", 0, 128), [(ID, R("KEY")), (R("INK"), R("TK"))])
+        tt(R("TT"), R("B7", 0, 128), R("PL"), ALU.max)
+        ts(R("FO"), R("TT"), float(ZS - X1 - 1), ALU.add)
+        marks("WS", HC[0], HC[1]); blocks("B4", HC[0], HC[1])
+        marks("WS", HC[1], HC[-1]); blocks("B5", HC[1], HC[-1])
+        for u in range(len(HC) - 1):
+            within("B%d" % (4 + u % 3), R("W35"), HC[u], HC[u + 1], SS[t][u], "B%d" % (2 + u % 2))
+            a, h, b = HC[u], HC[u] + CV[t][u], HC[u + 1]
+            if h > a: ts(R(XR, ZS + 16 * a, ZS + 16 * h), ind(R("Z"), R("SP", a, h)), 0.0, ALU.max)
+            if b > h: act(R(XR, ZS + 16 * h, ZS + 16 * b), ind(R("Z"), R("SP", h, b)), ACT.Relu)
+        for k, (u0, u1) in enumerate(FP):
+            src = ind(R(XR, X1, ZS + min(128 * u1, NH)), R("FO", 8 * u0, 8 * u1))
+            if t == 0:
+                o = R("XB", X1 + 128 * u0, X1 + 128 * u1)
+                if k in FV[t]: cp(o, src)
+                else: act(o, src, ACT.Copy)
+                count_piece(1, u0, u1, False, k == 0, k == len(FP) - 1)()
+            else:
+                o = R("XT", 128 * u0, 128 * u1)
+                if k in FV[t]: ts(o, src, -1.0, ALU.mult, 255.0, ALU.add)
+                else: act(o, src, ACT.Identity, 255.0, -1.0)
+                add("Y", lambda k=k, o=o: [g.sync.dma_start(T.y[:, o[1]:o[2]], ap(o)).then_inc(T.sem["y%d" % k], 16)],
                     [o], [], 60, ("y%d" % k, 16), 2000)
     return ops
 
@@ -438,53 +471,50 @@ def depend(ops):
                         before[r[0]] = [x[0] for x in h]; del h[:]
                 elif kind == "w" and r[3] == 1: h[:] = [x for x in h if not (r[1] <= x[2] and x[3] <= r[2])]
                 h.append((i, kind, r[1], r[2]))
+        d.discard(i)
         deps.append(d)
     return deps
 
 
 def arrange(ops, hard):
-    n = len(ops); succ = [[] for _ in range(n)]
-    deps = [set(d) for d in hard]; prev = {}
+    n = len(ops); deps = [{} for _ in ops]; succ = [{} for _ in ops]; prev = {}
     for i, o in enumerate(ops):
-        if o["after"] is not None: deps[i].add(o["after"])
+        for j in hard[i]:
+            deps[i][j] = ops[j]["lat"] + (HOP if ops[j]["e"] != o["e"] else 0.0 if o["e"] == "P" else SELF)
+        if o["after"] is not None: deps[i].setdefault(o["after"], 0.0)
         if o["chain"]:
-            if o["e"] in prev: deps[i].add(prev[o["e"]])
+            if o["e"] in prev: deps[i].setdefault(prev[o["e"]], 0.0)
             prev[o["e"]] = i
-    for i in range(n):
-        for j in deps[i]: succ[j].append(i)
+        for j, v in deps[i].items(): succ[j][i] = v
 
-    def lag(j, i):
-        if j not in hard[i]: return 0.0
-        if ops[j]["e"] == ops[i]["e"]: return ops[j]["lat"] + (0.0 if ops[i]["e"] == "P" else SELF)
-        return ops[j]["lat"] + HOP
-    pri = [0.0] * n
-    for i in range(n - 1, -1, -1):
-        pri[i] = ops[i]["c"] + max([pri[k] + lag(i, k) for k in succ[i]] + [ops[i]["lat"]])
-    left = [len(d) for d in deps]; rdy = [0.0] * n; free = {}; order = []; placed = [False] * n
-    ready = [i for i in range(n) if left[i] == 0]
-    while ready:
-        st = [(max(rdy[i], free.get(ops[i]["e"], 0.0)), i) for i in ready]
-        t0, i0 = min(st); e = ops[i0]["e"]
-        p, i, s = max((pri[i], -i, s) for s, i in st if ops[i]["e"] == e and s <= t0 + 0.25 * ops[i0]["c"] + 40.0)
-        i = -i
-        soon = None; rs = dict((j, u) for u, j in st)
-        for u, j in st:
-            if ops[j]["e"] == e: continue
-            for k in succ[j]:
-                if ops[k]["e"] == e and pri[k] > p + 300.0:
-                    wait = [x for x in deps[k] if not placed[x]]
-                    if all(x in rs and ops[x]["e"] != e for x in wait):
-                        est = max([rdy[k]] + [rs[x] + ops[x]["c"] + lag(x, k) for x in wait])
-                        if est < s + ops[i]["c"] - 60.0 and (soon is None or est < soon): soon = est
-        if soon is not None and soon + 1 > rdy[i] and min(u for u, j in st if ops[j]["e"] != e) <= soon:
-            rdy[i] = soon + 1.0
-            continue
-        ready.remove(i); order.append(i); placed[i] = True
-        free[e] = s + ops[i]["c"]
-        for k in succ[i]:
-            rdy[k] = max(rdy[k], free[e] + lag(i, k)); left[k] -= 1
-            if left[k] == 0: ready.append(k)
-    return order
+    def lay(keys, before, first):
+        busy = {}; end = [0.0] * n
+        for i in sorted(range(n), key=lambda i: keys[i]):
+            s = max([end[j] + v for j, v in before[i].items()] + [first[i]]); c = ops[i]["c"]
+            b = busy.setdefault(ops[i]["e"], []); x, hi = 0, len(b)
+            while x < hi:
+                if b[(x + hi) // 2][0] <= s: x = (x + hi) // 2 + 1
+                else: hi = (x + hi) // 2
+            if x and b[x - 1][1] > s: s = b[x - 1][1]
+            while x < len(b) and s + c > b[x][0]:
+                s = b[x][1]; x += 1
+            b.insert(x, (s, s + c)); end[i] = s + c
+        return end
+    zero = [0.0] * n; tail = [o["lat"] for o in ops]; best = None
+    for k in range(TRIES):
+        pri = [0.0] * n
+        for i in range(n - 1, -1, -1):
+            pri[i] = ops[i]["c"] * (1 + (k * (i + 7) * 7919 % 1009) / 1700.0) + max([pri[x] + v for x, v in succ[i].items()] + [tail[i]])
+        end = lay([(-pri[i], i) for i in range(n)], deps, zero); last = 1e18
+        while True:
+            back = lay([(-end[i], -i) for i in range(n)], succ, tail)
+            end = lay([(-back[i], i) for i in range(n)], deps, zero)
+            span = max(end[i] + tail[i] for i in range(n))
+            if best is None or span < best[0]: best = (span, end)
+            if span > last - 1: break
+            last = span
+    end = best[1]
+    return sorted(range(n), key=lambda i: (end[i] - ops[i]["c"], end[i], i))
 
 
 def rank_program(g, core, T, topo):

@@ -6,32 +6,34 @@ W, K, CAP, MP, PR, NR = 2048, 4096, 256, 1024, 8, 8
 XS = (4, 3)
 NH = 1648
 X1, ZS = W, 2 * W + 16
-MV = 82
+MV = 84
 M1 = 26
-ET, RS = PR - 3, (3, 0)
-NS = 16 * (128 - MV)
+ET, RS = PR - 1, (3, 1)
+NS = 768
 CR2, BIG, MOD = 1.5 * 2.0 ** 34, 30000.0, 16512.0
+LS, AS_ = False, (0, 0)
 AN = 160
 HC = (0, 32, 64, NH // 16)
-FP = ((0, 4), (4, 8), (8, 11), (11, 14), (14, 16))
-FV = ((0, 4), (0, 2, 4))
-ZV = (320, 192)
-CV = ((32, 0, 16), (16, 16, 8))
-PS, SS = (0, 0), ((16, 0, 23), (32, 8, 0))
+FP = ((0, 4), (4, 8), (8, 12), (12, 14), (14, 16))
+FV = ((0, 2), (0, 2, 4))
+NP, NV = ((0, 4), (4, 8), (8, 11), (11, 13)), ()
+ZV = (320, 128)
+CV = ((0, 0, 16), (16, 0, 16))
+PS, SS = (0, 0), ((16, 16, 0), (16, 16, 15))
 
 SCRATCH = {}
 DIAG = {"NID": -1.0, "I5": 5.0, "IN5": -5.0, "I113": 113.0, "IN113": -113.0, "I238": 238.0, "IC": CR2, "INC": -CR2, "IN128": -128.0,
         "IN16": -16.0, "I17": 17.0, "IK": 8192.0, "INK": -8192.0}
 for _d, _l in (
-    ("bfloat16", [("XT", W), ("XA", ZS + NH), ("XB", ZS + NH), ("Z", K + 16), ("FL", K), ("GS", 2 * NS), ("PRS", 1024), ("GN", CAP),
-                  ("G0", CAP), ("GM", 256), ("WN", 4704), ("GE0", 512), ("GE1", 512), ("QB", 128), ("NZ", W), ("NZ2", 512), ("BLK", 128), ("BP", 128), ("BN", 128), ("ID", 128),
-                  ("TRI", 128), ("TRU", 128), ("TMP", 128), ("UU", 146), ("SW1", 144), ("SW16", 144), ("SW4", 144), ("SB", 128), ("SM", 16), ("G8B", 8),
-                  ("CB", 128), ("ONE", 128), ("TM255", 128), ("FS", 256), ("AS", 320), ("SF", NH), ("SN", CAP), ("BL", NH), ("SG", 256),
+    ("bfloat16", [("XT", W), ("XA", ZS + NH + 16), ("NC", NH + 16), ("NK", W), ("KP", 128), ("KT", 128), ("MC", 104), ("XB", ZS + NH), ("Z", K + 16), ("FL", K), ("GS", 2 * NS), ("PRS", 1024), ("GN", CAP), ("MN", 128), ("DM", CAP),
+                  ("G0", CAP), ("WN", 4704), ("GE0", 512), ("GE1", 512), ("QB", 128), ("NZ", W), ("NZ2", 512), ("BLK", 128), ("BP", 128), ("BN", 128), ("ID", 128),
+                  ("TRI", 128), ("TRU", 128), ("UU", 146), ("SW1", 144), ("SW16", 144), ("SW4", 144), ("SB", 128), ("G8B", 8),
+                  ("CB", 128), ("ONE", 128), ("TM255", 128), ("FS", 384), ("AS", 480), ("SF", NH), ("BL", NH), ("SG", 256),
                   ("AL", 256), ("A5", 272), ("MK", 128), ("CIB", 256), ("WP", 4704), ("WS", 9248), ("KM", 32), ("QS", 32), ("US", 32)]
      + [(n, 128) for n in DIAG]),
     ("float32", [("QF", 16), ("PC", 8), ("CI", 146), ("CG", 128), ("CR", 128), ("CQ", 144), ("E32", 32), ("KD", 32), ("BLKF", 128), ("LD0", 32), ("LD1", 32), ("G16", 24), ("COL", 16),
-                 ("TF", 128), ("PL", 128), ("W3", 272), ("W2", 16), ("T1", 4), ("W35", 264), ("T5", 4), ("L1", 256), ("TT", 128), ("RB", 256)]),
-    ("float16", [("SH", NH), ("QH", NH), ("QN0", 256), ("QN1", 256), ("J50", 128), ("J51", 128), ("AP", 256), ("ST", 8 * 256),
+                 ("TF", 160), ("PL", 128), ("W3", 272), ("HP", 104), ("HG", 104), ("C8", 8), ("W35", 264), ("T5", 4), ("L1", 256), ("AC", 256), ("IDF", 128), ("TT", 128)]),
+    ("float16", [("SH", NH), ("QH", NH), ("TM", 128), ("IM", 128), ("G80", 104), ("LG", 104), ("J50", 128), ("J51", 128), ("AP", 256), ("ST", 8 * 256),
                  ("FF", 8 * 256), ("RR", 256), ("JB", 128), ("JS", 2), ("G4", 24), ("L2", 256), ("KEY", 128), ("TK", 128)]),
     ("int32", [("QI", 16), ("PI", 8), ("TI", 256), ("TJ", 256)]),
     ("uint16", [("SO", 128), ("SP", 128), ("PM0", 16), ("PM1", 16), ("SC", 20), ("OF", 256), ("FO", 128)]),
@@ -42,8 +44,8 @@ for _b in range(8):
 SEMAPHORES = ["sV", "sS", "sP", "sG", "lq", "lx0", "lx1", "lx2", "lx3", "ca0", "ca1", "cl0", "cl1", "ga0", "ga1", "gl0", "gl1",
               "y0", "y1", "y2", "y3", "y4", "y5", "y6", "y7", "xc0", "xc1"]
 TWO = ("bfloat16", "float16", "uint16")
-CYC, PEC, GAT, SCA, FIXV, FIXS, HOP, SELF, GL = 1.0, 0.5, 1.56, 3.8, 60.0, 90.0, 100.0, 60.0, 3000.0
-TRIES = 300
+CYC, PEC, GAT, SCA, FIXV, FIXS, HOP, SELF, GL = 1.0, 0.5, 1.56, 3.8, 60.0, 90.0, 75.0, 50.0, 2200.0
+TRIES = 5000
 PLAN = {}
 
 
@@ -181,22 +183,23 @@ def build(g, core, T, topo):
     iota(R("QS", 0, 16), [[0, 16]], 0, 0); act(R("QS", 16, 32), R("QF"), ACT.Identity, None, 1.0 / 128)
     ts(R("BLKF"), R("CG"), gcol, ALU.is_equal)
     act(R("BLK"), R("BLKF"), ACT.Copy)
-    ts(ID, R("CI", 0, 128), pc, ALU.is_equal)
+    ts(ID, R("CI", 0, 128), pc, ALU.is_equal); act(R("IDF"), ID, ACT.Copy)
     for nm, v in DIAG.items(): act(R(nm), ID, ACT.Identity, None, v)
     act(R("BP"), R("BLK"), ACT.Identity, None, 2048.0); act(R("BN"), R("BLK"), ACT.Identity, None, -2048.0)
     ts(R("COL", 6, 7), pc, -256.0, ALU.mult, -128.0, ALU.add)
     act(R("UU"), R("CI"), ACT.Sigmoid, R("COL", 6, 7), 256.0)
-    ts(R("TMP"), R("CR"), rc, ALU.is_ge)
-    tt(R("TRI"), R("TMP"), R("BLK"), ALU.mult)
-    tt(R("TRU"), R("BLK"), R("TRI"), ALU.subtract)
+    for nm, d, op in (("TRI", 1, ALU.is_ge), ("TRU", -1, ALU.is_gt)):
+        add("G", lambda nm=nm, d=d, op=op: [g.affine_select(ap(R(nm)), ap(R("BLK")), [[d, 128]], op, 0.0, 0, -d)], [R("BLK")], [R(nm)], 200 + 256 * CYC)
     ts(R("SW1"), R("CI", 0, 144), gc16, ALU.is_equal)
     act(R("SW16"), R("SW1"), ACT.Identity, None, 1.0 / 16)
     ts(R("SW4"), R("CQ"), g43, ALU.is_equal)
     ts(R("MK"), R("CR"), rc, ALU.is_equal)
     ts(R("JB"), R("MK"), p4k, ALU.mult, -4096.0, ALU.add)
+    act(R("MN"), R("MK"), ACT.Identity, -8192.0, 8192.0)
+    for a in (0, 128): act(R("DM", a, a + 128), R("MK"), ACT.Identity, None, 256.0)
     ts(R("COL", 5, 6), rc, 4.0, ALU.mult, 4640.0, ALU.add)
     ts(R("JS", 0, 1), rc, 0.0, ALU.is_gt, R("COL", 5, 6), ALU.mult)
-    act(R("TM255"), ONE, ACT.Identity, None, -255.0)
+    act(R("TM255"), ONE, ACT.Identity, None, -255.0); act(R("TM"), ONE, ACT.Identity, None, -1536.0); act(R("IM"), ID, ACT.Identity, None, -MOD)
     cp(R("QH", 0, 128), R("CI", 0, 128))
     for a in (128, 256, 512, 1024):
         b = min(2 * a, NH); ts(R("QH", a, b), R("QH", 0, b - a), float(a), ALU.add)
@@ -205,30 +208,32 @@ def build(g, core, T, topo):
     for r in (R("W3", 128, 136), R("W3", 264, 272), R("W35", 256, 264)): iota(r, [[0, 8]], int(BIG), 0)
 
     def round_constants(t):
-        iota(R("TI", 128, 144), [[37 * 16, 16]], t, 37)
+        iota(R("TF", 128, 144), [[37 * 16, 16]], t, 37)
+        ts(R("TI", 128, 144), R("TF", 128, 144), r80, ALU.add)
         ts(R("TJ", 128, 144), R("TI", 128, 144), 255, ALU.bitwise_and)
-        ts(R("TI", 144, 160), R("TJ", 128, 144), r80, ALU.add)
-        ts(R("TJ", 144, 160), R("TI", 144, 160), 255, ALU.bitwise_and)
-        cp(R("PM%d" % t), R("TJ", 144, 160))
-        iota(R("TF"), [[148, 128]], t, 0)
-        ts(R("TI", 0, 128), R("TF"), bjc, ALU.add)
+        cp(R("PM%d" % t), R("TJ", 128, 144))
+        iota(R("TF", 0, 128), [[148, 128]], t, 0)
+        ts(R("TI", 0, 128), R("TF", 0, 128), bjc, ALU.add)
         ts(R("TJ", 0, 128), R("TI", 0, 128), 255, ALU.bitwise_and)
         ts(R("J5%d" % t), R("TJ", 0, 128), 5.0, ALU.mult, -793.5, ALU.add)
-        iota(R("WN", 0, CAP), [[0, CAP]], 0, 0)
-        iota(R("WP", 0, MP), [[0, MP]], 0, 0)
         if t == 0:
+            iota(R("HP"), [[128, 13], [0, 8]], 0, 1)
+            iota(R("HG"), [[0, 13], [16, 8]], 0, 0)
+            ts(R("G80"), R("HG"), pc, ALU.is_equal, 4096.0, ALU.mult)
+            iota(R("XA", ZS + NH, ZS + NH + 16), [[0, 16]], 0, 0)
             iota(R("TT"), [[16, 128]], 1 + X1 - ZS, 0)
             ts(R("PL"), R("TT"), rc, ALU.add)
 
-    def starts(tb, jb, src, a, col, bias):
-        group(tb, [(R(src, a, a + 128), R("BLK"))])
+    def starts(tb, jb, src, a, col, bias, scalar):
+        group(tb, [(ID, R("MN"))] * scalar + [(R(src, a, a + 128), R("BLK"))])
         group(jb, [(ID, R("JB")), (R(src, a, a + 128), R("BP")), (R(src, a + 1, a + 129), R("BN"))])
-        tt(R("L1", col, col + 128), tb, R("MK"), ALU.mult)
+        if scalar: act(R("L1", col, col + 128), tb, ACT.Relu)
+        else: tt(R("L1", col, col + 128), tb, R("MK"), ALU.mult)
         act(R("L2", col, col + 128), jb, ACT.Relu, bias)
 
-    def places(win, a, u, banks):
+    def places(win, a, u, banks, scalar):
         c = 128 * u; o, e = R(banks[0], 128, 138), R(banks[0], 136, 137)
-        starts(R(banks[0], 0, 128), R(banks[1], 0, 128), "AS", a, c, 520.0)
+        starts(R(banks[0], 0, 128), R(banks[1], 0, 128), "AS", a, c, 520.0, scalar)
         mm([(o, R("L1", c, c + 128), R("G16", 8, 18), True, False), (o, R("L2", c, c + 128), R("G4", 8, 18), False, False),
             (e, sel(0), R("AS", a + 144, a + 145), False, False), (e, ID, R("JS", 0, 1), False, True)])
         cp(R("SC", 10 * u, 10 * u + 10), o)
@@ -254,26 +259,29 @@ def build(g, core, T, topo):
         group(R(bank, 0, c1 - c0), [(R("IN16"), R("SB", c0, c1))] + [(sel(r), R("SF", 16 * c0 + r, 16 * c1, 16)) for r in range(16)])
         cp(R("SP", c0, c1), R(bank, 0, c1 - c0))
 
-    def count_piece(t, u0, u1, scalar, first, last):
-        bank = "B%d" % ((u0 // 4, u0 // 2)[u1 - u0 < 4] % 4)
-        items = []
+    def flags(t, bank, u0, u1, scalar):
+        items = []; nm = ("NZ", "NC", "NK")[t]
         for u in range(u0, u1):
-            o = R(bank, 128 * (u - u0), 128 * (u - u0) + 128); a = 128 * u
-            if t == 0: items.append((o, R("XT", a, a + 128), R("QB"), True, True))
-            else: items += [(o, R("TM255"), R("QB"), True, False), (o, R("XB", X1 + a, X1 + a + 128), R("QB"), False, True)]
+            o = R(bank, 128 * (u - u0), 128 * (u - u0) + 128); a = ZS + 128 * u
+            if t == 0: items.append((o, R("XT", 128 * u, 128 * u + 128), R("QB"), True, True))
+            elif t == 2: items.append((o, R("XT", u, W, 16), R("QB"), True, True))
+            else: items += [(o, R("TM255"), R("QB"), True, False), (o, R("XA", a, a + 128), R("QB"), False, True)]
         mm(items)
-        nz, pb = R("NZ", 128 * u0, 128 * u1), R(bank, 0, 128 * (u1 - u0))
+        nz, pb = R(nm, 128 * u0, 128 * u1), R(bank, 0, 128 * (u1 - u0))
         if scalar:
-            act(R("NZ2"), pb, ACT.Sign); act(nz, R("NZ2"), ACT.Square)
+            act(R("NZ2", 0, width(nz)), pb, ACT.Sign); act(nz, R("NZ2", 0, width(nz)), ACT.Square)
         else: ts(nz, pb, 0.0, ALU.not_equal)
-        return lambda: group(R("B7", 0, 1), [(R("NZ", 128 * u, 128 * u + 128), R("ONE", 0, 1)) for u in range(u0, u1)], first, last)
 
     others = [r for r in range(NR) if r != rank]
-    for f in [count_piece(0, 4 * k, 4 * k + 4, k == 0, k == 1, k == 3) for k in (1, 0, 2, 3)]: f()
+    for k in range(4): flags(0, "B%d" % k, 4 * k, 4 * k + 4, k == 0)
+    for k in (1, 0, 2, 3):
+        group(R("B7", 0, 1), [(R("NZ", 128 * u, 128 * u + 128), R("ONE", 0, 1)) for u in range(4 * k, 4 * k + 4)], k == 1, k == 3)
     for t in range(2):
         LD, GE, XR = "LD%d" % t, "GE%d" % t, ("XA", "XB")[t]
         mine = R(LD, 4 * rank, 4 * rank + 1)
-        cp(mine, R("B7", 0, 1))
+        if t == 0: cp(mine, R("B7", 0, 1))
+        else:
+            tt(R("C8"), R("B7", 0, 8), R("G16", 8, 16), ALU.mult); red(mine, R("C8"), ALU.add)
 
         def send_counts(t=t, mine=mine):
             ids = []; m = None
@@ -283,18 +291,21 @@ def build(g, core, T, topo):
             return [g.remote_dma_fused([RemoteDMATransfer(dst_ids=ids, dma_engine_mask=m, remote_sem=T.sem["ca%d" % t], src=ap(mine),
                                                           dsts=[ap(mine)] * len(ids))], local_sem=T.sem["cl%d" % t])]
         ne = len(topo.engines(core, T.cores[others[0]]))
-        add("G", send_counts, [R(LD)], [R("COL", 8 + t, 9 + t)], 300, ("cl%d" % t, ne), 3000)
+        add("G", send_counts, [R(LD)], [R("COL", 8 + t, 9 + t)], 300, ("cl%d" % t, ne), GL)
         sent = len(ops) - 1
-        add("A", None, [R("COL", 8 + t, 9 + t)], [R(LD, 0, 32, 2)], 0, ("ca%d" % t, ne * len(others)), 2000)
+        add("A", None, [R("COL", 8 + t, 9 + t)], [R(LD, 0, 32, 2)], 0, ("ca%d" % t, ne * len(others)), 1500)
         after[0] = sent if t == 1 else None
         round_constants(t)
         after[0] = sent
-        iota(R("WS", 0, NH), [[0, NH]], 0, 0)
+        for nm, n in (("WN", CAP), ("WP", MP), ("WS", NH)): iota(R(nm, 0, n), [[0, n]], 0, 0)
+        if t == 0:
+            for k in range(4): flags(2, "B%d" % k, 4 * k, 4 * k + 4, k < 3)
         after[0] = None
         if t == 0:
             for k in range(4): ts(R(XR, X1 + 512 * k, X1 + 512 * k + 512), R("XT", 512 * k, 512 * k + 512), -1.0, ALU.mult, 255.0, ALU.add)
         add("Y", lambda XR=XR, t=t: [g.sync.dma_start(ap(R(XR, 0, W)), ap(R(XR, X1, X1 + W))).then_inc(T.sem["xc%d" % t], 16)],
             [R(XR, X1, X1 + W)], [R(XR, 0, W)], 60, ("xc%d" % t, 16), 4000)
+        AO = AN
         mn0, mn1, coef = R("COL", 0, 1), R("COL", 1, 2), R("COL", 2, 3)
         group(R("B4", 0, 32), [(ID, R("KM")), (ID, R("QS"))] + [(R("IC"), R("US"))] * t, True, False)
         red(R("COL", 3, 4), R(LD, 0, 32, 4), ALU.add)
@@ -307,13 +318,16 @@ def build(g, core, T, topo):
         c8 = R("CB", 0, 128, 16)
         mm([(R("B5", 0, 128), R("TM255"), R("CB"), True, False)]
            + [(R("B5", r, 128, 16), R(XR, X1 + r, X1 + W, 16), c8, False, r == 15) for r in range(16)])
-        ts(R("FS", 128, 256), R("B5", 0, 128), 0.0, ALU.is_gt)
-        ts(R("FS", 0, 128), R("B5", 0, 128), 0.0, ALU.is_lt)
-        group(R("B6", 0, 146), [(R("FS", 128, 256), R("UU"))]); group(R("B7", 0, 146), [(R("FS", 0, 128), R("UU"))])
-        act(R("AS", AN, AN + 146), R("B6", 0, 146), ACT.Copy); cp(R("AS", 0, 146), R("B7", 0, 146))
         win = R(XR, X1, ZS)
-        places("WN", AN, 1, ("B0", "B1", "B6"))
-        marks("WN", 64, 80, 64); blocks("B4", 64, 80); within("B4", R("W3", 136, 272), 64, 80, 0, None, 64)
+        ts(R("FS", 128, 256), R("B5", 0, 128), 0.0, ALU.is_gt)
+        act(R("FS", 0, 128), R("B5", 0, 128), ACT.Sigmoid, -128.0, -256.0)
+        group(R("B6", 0, 146), [(R("FS", 128, 256), R("UU"))]); group(R("B7", 0, 146), [(R("FS", 0, 128), R("UU"))])
+        cp(R("AS", AN, AN + 146), R("B6", 0, 146)); act(R("AS", 0, 146), R("B7", 0, 146), ACT.Copy)
+        places("WN", AN, 1, ("B0", "B1", "B6"), False)
+        marks("WN", 64, 80, 64)
+        scan(R("G0"), R("DM"), R("BL", 1024, 1280), 0.0, ALU.add, ALU.min)
+        cp(R("SO", 64, 80), R("G0", 15, CAP, 16)); act(R("SB", 64, 80), R("G0", 15, CAP, 16), ACT.Identity, None, -1.0)
+        within("B4", R("W3", 136, 272), 64, 80, 0, None, 64)
         act(R("G0"), ind(win, R("SP", 64, 80)), ACT.Identity, 255.0, -1.0)
         act(R("GN"), ind(R("G0"), R("PM%d" % t)), ACT.Copy)
         partner = T.cores[rank ^ XS[t]]
@@ -323,21 +337,25 @@ def build(g, core, T, topo):
             return [g.remote_dma(ap(R(GE, 0, CAP)), ap(R("GN")), T.sem["ga%d" % t], T.sem["gl%d" % t], pid, rid, topo.mask(core, partner))]
         ne = len(topo.engines(core, partner))
         add("G", send_guests, [R("GN")], [R("COL", 10 + t, 11 + t)], 300, ("gl%d" % t, ne), GL)
-        add("A", None, [R("COL", 10 + t, 11 + t)], [R(GE, 0, CAP)], 0, ("ga%d" % t, ne), 1200)
-        places("WP", 0, 0, ("B2", "B3", "B7"))
-        marks("WP", 0, 64); blocks("B0", 0, 64)
+        add("A", None, [R("COL", 10 + t, 11 + t)], [R(GE, 0, CAP)], 0, ("ga%d" % t, ne), 900)
+        act(R(GE, 256, 512), R(GE, 0, 256), ACT.Copy)
+        places("WP", 0, 0, ("B2", "B3", "B7"), LS)
+        for s in range(2):
+            marks("WP", 32 * s, 32 * s + 32); blocks("B%d" % s, 32 * s, 32 * s + 32)
         for s in range(2):
             c = 128 * s; pbk = R("B%d" % (5 + s), 0, 128); ab = R("B7" if s else "B3", 0, 128); a = R("AP", c, c + 128)
             group(ab, [(R("SW4", 12 - 4 * q, 140 - 4 * q), R("BL", 512 * s + q, 512 * s + 512, 4)) for q in range(4)], True, False)
             within("B%d" % s, R("W3", 0, 136), 32 * s, 32 * s + 32, PS[s], "B2")
             act(R("PRS", 512 * s, 512 * s + 512), ind(win, R("SP", 32 * s, 32 * s + 32)), ACT.Copy)
             group(ab, [(R("SW4", 12 - 4 * q, 140 - 4 * q), R("SF", 512 * s + q, 512 * s + 512, 4)) for q in range(4)], False, True)
-            ts(a, ab, 2047.0, ALU.min, -1023.5, ALU.add)
+            if AS_[s]: act(a, ab, ACT.Identity, -1023.5)
+            else: ts(a, ab, -1023.5, ALU.add)
             group(pbk, [(R("I238"), ONE), (NID, R("J5%d" % t)), (R("IN16"), a)] + rnd + [(ID, R("J5%d" % t)), (R("I17"), a)])
-        group(R("B2", 0, 128), [(R("TRI"), R("AS", AN + 1, AN + 129)), (R("TRU"), R("AS", AN, AN + 128)), (R("IK"), ONE),
-                                (R("INK"), R("AS", AN + 1, AN + 129)), (R("IK"), R("AS", AN, AN + 128))])
+        group(R("B2", 0, 128), [(R("TRI"), R("AS", AO + 1, AO + 129)), (R("TRU"), R("AS", AO, AO + 128)), (R("IK"), ONE),
+                                (R("INK"), R("AS", AO + 1, AO + 129)), (R("IK"), R("AS", AO, AO + 128))])
         act(R("KEY"), R("B2", 0, 128), ACT.Copy)
-        act(R(GE, 256, 512), R(GE, 0, 256), ACT.Copy)
+        if t == 0:
+            group(R("B2", 128, 129), [(R("BLK"), R("AS", AO + 144, AO + 145))]); act(R("T5", 0, 1), R("B2", 128, 129), ACT.Copy)
         turn = 0
         for s in range(2):
             nv = ZV[s]; pv = R(("B4", "B7")[s], 0, nv)
@@ -367,8 +385,8 @@ def build(g, core, T, topo):
 
         def tally(n, s):
             _, st, _, a = part(n, s)
-            if n < ET: group(tal[s], [(NID, st), (ID, a)] + rnd, n == 0, False)
-            else: group(tal[s], [(part(u, s)[2], R("IN128")) for u in (range(4) if n == ET else range(4, PR - 1))], False, n == PR - 2)
+            if n < ET: group(tal[s], [(st, NID), (a, ID)] + rnd, n == 0, False)
+
         chain[0] = True
         for k in range(2 * PR):
             n, s = k // 2, k % 2; pn, ps = (k - 1) // 2, (k - 1) % 2
@@ -406,19 +424,21 @@ def build(g, core, T, topo):
         chain[0] = False
         for s in range(2):
             c = 128 * s; last = "B%d" % (5 + s); al = R("AL", c, c + 128)
+            for u in range(PR - 1): group(tal[s], [(R("IN128"), part(u, s)[2])], False, u == PR - 2)
             if RS[s] & 1: act(R("RR", c, c + 128), tal[s], ACT.Identity, 1536.0 - 6144.0 / MOD, 1.0 / MOD)
             else: ts(R("RR", c, c + 128), tal[s], 1.0 / MOD, ALU.mult, 1536.0 - 6144.0 / MOD, ALU.add)
-            if RS[s] & 2: act(R("RB", c, c + 128), R("RR", c, c + 128), ACT.Identity, 14336.0 - 1536.0 * MOD, MOD)
-            else: ts(R("RB", c, c + 128), R("RR", c, c + 128), MOD, ALU.mult, 14336.0 - 1536.0 * MOD, ALU.add)
-            tt(R("GM", c, c + 128), tal[s], R("RB", c, c + 128), ALU.subtract)
+            if RS[s] & 2: act(R("AC", c, c + 128), tal[s], ACT.Copy)
+            else: cp(R("AC", c, c + 128), tal[s])
             for u in range(ET, PR): group(R(last, 0, 128), [(part(u, s)[1], NID), (part(u, s)[3], ID)] + rnd, u == ET, False)
-            group(R(last, 0, 128), [(R("IK"), R("SG", c, c + 128)), (R("GM", c, c + 128), ID)], False, False)
-            mm([(R(last, r, 128, 16), R("FL", W * s + r, W * s + W, 16), R("G8B"), False, r == 15) for r in range(16)])
-            ts(al, R(last, 0, 128), 8192.5, ALU.is_gt)
+            group(R(last, 0, 128), [(R("IM"), R("RR", c, c + 128)), (R("IM"), R("TM")), (R("IDF"), R("AC", c, c + 128))], False, False)
+            mm([(R(last, 0, 128), R("IK"), R("SG", c, c + 128), False, False)]
+               + [(R(last, r, 128, 16), R("FL", W * s + r, W * s + W, 16), R("G8B"), False, r == 15) for r in range(16)])
+            ts(al, R(last, 0, 128), 14336.0 + 8192.5, ALU.is_gt)
             pre = R(tal[s][0], s, 129)
             group(pre, [(R("AL", 0, 128), ONE)] * s + [(al, R("UU", s, 129))])
-            act(R("A5", 15 + s + c, 144 + c), pre, ACT.Copy)
-            starts(R("B%d" % (2 * s), 0, 128), R("B%d" % (2 * s + 1), 0, 128), "A5", 15 + c, c, 1030.0 + c)
+            if s: act(R("A5", 15 + s + c, 144 + c), pre, ACT.Copy)
+            else: cp(R("A5", 15 + s + c, 144 + c), pre)
+            starts(R("B%d" % (2 * s), 0, 128), R("B%d" % (2 * s + 1), 0, 128), "A5", 15 + c, c, 1030.0 + c, False)
             group(R(last, 0, 8), [(R("L1", c, c + 128), R("G16", 8, 16)), (R("L2", c, c + 128), R("G4", 8, 16))])
             cp(R("SC", 8 * s, 8 * s + 8), R(last, 0, 8))
             scatter(R("WS"), R("SC", 8 * s, 8 * s + 8), R("CIB", c, c + 128))
@@ -426,9 +446,17 @@ def build(g, core, T, topo):
         act(R("W35", 0, 256), R("B3", 0, 256), ACT.Copy)
         group(R("B7", 0, 1), [(R("BLK"), R("A5", 271, 272))])
         ts(R("TK"), R("KEY"), R("B7", 0, 1), ALU.subtract, 0.0, ALU.max)
-        group(R("B7", 0, 128), [(ID, R("KEY")), (R("INK"), R("TK"))])
-        tt(R("TT"), R("B7", 0, 128), R("PL"), ALU.max)
-        ts(R("FO"), R("TT"), float(ZS - X1 - 1), ALU.add)
+        if t == 0:
+            ts(R("KP"), R("KEY"), R("B7", 0, 1), ALU.is_gt)
+            ts(R("LG"), R("G80"), R("B7", 0, 1), ALU.min, R("T5", 0, 1), ALU.min)
+            group(R("B0", 0, 128), [(R("KP"), ID)]); act(R("KT"), R("B0", 0, 128), ACT.Copy)
+            group(R("B1", 0, 104), [(ONE, R("LG"))]); tt(R("MC"), R("B1", 0, 104), R("HP"), ALU.is_gt)
+
+        def sources(bank):
+            group(R(bank, 0, 128), [(ID, R("KEY")), (R("INK"), R("TK"))])
+            tt(R("TT"), R(bank, 0, 128), R("PL"), ALU.max)
+            ts(R("FO"), R("TT"), float(ZS - X1 - 1), ALU.add)
+        if t == 1: sources("B7")
         marks("WS", HC[0], HC[1]); blocks("B4", HC[0], HC[1])
         marks("WS", HC[1], HC[-1]); blocks("B5", HC[1], HC[-1])
         for u in range(len(HC) - 1):
@@ -436,13 +464,19 @@ def build(g, core, T, topo):
             a, h, b = HC[u], HC[u] + CV[t][u], HC[u + 1]
             if h > a: ts(R(XR, ZS + 16 * a, ZS + 16 * h), ind(R("Z"), R("SP", a, h)), 0.0, ALU.max)
             if b > h: act(R(XR, ZS + 16 * h, ZS + 16 * b), ind(R("Z"), R("SP", h, b)), ACT.Relu)
+        if t == 0:
+            sources("B6")
+            for k, (u0, u1) in enumerate(NP):
+                flags(1, "B%d" % (k % 2), u0, u1, k in NV)
+                group(R("B7", 0, 8), [(R("NC", 128 * u, 128 * u + 128), R("MC", 8 * u, 8 * u + 8)) for u in range(u0, u1)], k == 0, u1 == 13)
+                if k == 0:
+                    for h in (0, 8): group(R("B7", 0, 8), [(R("NK", 128 * r, 128 * r + 128), R("KT", r, 128, 16)) for r in range(h, h + 8)], False, False)
         for k, (u0, u1) in enumerate(FP):
             src = ind(R(XR, X1, ZS + min(128 * u1, NH)), R("FO", 8 * u0, 8 * u1))
             if t == 0:
                 o = R("XB", X1 + 128 * u0, X1 + 128 * u1)
                 if k in FV[t]: cp(o, src)
                 else: act(o, src, ACT.Copy)
-                count_piece(1, u0, u1, False, k == 0, k == len(FP) - 1)()
             else:
                 o = R("XT", 128 * u0, 128 * u1)
                 if k in FV[t]: ts(o, src, -1.0, ALU.mult, 255.0, ALU.add)
@@ -460,8 +494,8 @@ def depend(ops):
             for r in rs:
                 psum = SCRATCH[r[0]][0] == "psum"
                 if psum and hist.get(r[0]) and ops[hist[r[0]][-1][0]]["e"] == o["e"]: d.update(before.get(r[0], ()))
-                for j, kj, a, b in hist.get(r[0], ()):
-                    clash = (kind == "w" or kj == "w") and a < r[2] and r[1] < b
+                for j, kj, a, b, step in hist.get(r[0], ()):
+                    clash = (kind == "w" or kj == "w") and a < r[2] and r[1] < b and not (step == r[3] == 4 and (a - r[1]) % 4)
                     if clash or (psum and (ops[j]["e"] != o["e"] or o["e"] == "P")): d.add(j)
         for kind, rs in (("r", o["r"]), ("w", o["w"])):
             for r in rs:
@@ -470,7 +504,7 @@ def depend(ops):
                     if h and ops[h[-1][0]]["e"] != o["e"]:
                         before[r[0]] = [x[0] for x in h]; del h[:]
                 elif kind == "w" and r[3] == 1: h[:] = [x for x in h if not (r[1] <= x[2] and x[3] <= r[2])]
-                h.append((i, kind, r[1], r[2]))
+                h.append((i, kind, r[1], r[2], r[3]))
         d.discard(i)
         deps.append(d)
     return deps
@@ -500,19 +534,29 @@ def arrange(ops, hard):
                 s = b[x][1]; x += 1
             b.insert(x, (s, s + c)); end[i] = s + c
         return end
-    zero = [0.0] * n; tail = [o["lat"] for o in ops]; best = None
+    zero = [0.0] * n; tail = [o["lat"] for o in ops]; seed = [1]
+
+    def passes(key):
+        end = lay([(-key[i], i) for i in range(n)], deps, zero)
+        back = lay([(-end[i], -i) for i in range(n)], succ, tail)
+        end = lay([(-back[i], i) for i in range(n)], deps, zero)
+        return max(end[i] + tail[i] for i in range(n)), end, back
+
+    def draw(m):
+        seed[0] = (seed[0] * 1103515245 + 12345) % 2 ** 31
+        return (seed[0] >> 8) % m
+    pri = [0.0] * n
+    for i in range(n - 1, -1, -1):
+        pri[i] = ops[i]["c"] + max([pri[x] + v for x, v in succ[i].items()] + [tail[i]])
+    best = passes(pri); free = [i for i in range(n) if not ops[i]["chain"]]
     for k in range(TRIES):
-        pri = [0.0] * n
+        key = list(best[2]); c = free[draw(len(free))]; near = [i for i in free if abs(best[1][i] - best[1][c]) < 3000]
+        for u in range(4): key[near[draw(len(near))]] += draw(2500)
         for i in range(n - 1, -1, -1):
-            pri[i] = ops[i]["c"] * (1 + (k * (i + 7) * 7919 % 1009) / 1700.0) + max([pri[x] + v for x, v in succ[i].items()] + [tail[i]])
-        end = lay([(-pri[i], i) for i in range(n)], deps, zero); last = 1e18
-        while True:
-            back = lay([(-end[i], -i) for i in range(n)], succ, tail)
-            end = lay([(-back[i], i) for i in range(n)], deps, zero)
-            span = max(end[i] + tail[i] for i in range(n))
-            if best is None or span < best[0]: best = (span, end)
-            if span > last - 1: break
-            last = span
+            for x in succ[i]:
+                if key[i] <= key[x]: key[i] = key[x] + 1e-3
+        r = passes(key)
+        if r[0] <= best[0]: best = r
     end = best[1]
     return sorted(range(n), key=lambda i: (end[i] - ops[i]["c"], end[i], i))
 

@@ -6,35 +6,48 @@ W, K, CAP, MP, PR, NR = 2048, 4096, 256, 1024, 8, 8
 XS = (4, 3)
 NH = 1648
 X1, ZS = W, 2 * W + 16
-MV = 84
+MV0 = 84
 M1 = 26
-ET, RS = PR - 1, (3, 1)
-NS = 768
-CR2, BIG, MOD = 1.5 * 2.0 ** 34, 30000.0, 16512.0
-LS, AS_ = False, (0, 0)
+MF, M1F = 76, 30
+MK_ = {(0, 0): (92, 30), (0, 15): (76, 20), (1, 14): (80, 20), (1, 15): (80, 30)}
+TS = {}
+ES = (((0, 0, 0, 0), (0, 1, 0, 0)),) * 2
+PV = ((0, 0), (0, 0))
+GV = (0, 0)
+CM = ((0, 128),)
+FT = (7, 8, 9, 10, 11, 12)
+FB = ("B2", "B3", "B2")
+FL8 = (0, 0, 0)
+F0, O0, F2 = (1, 0, 0, 0), (1, 0, 2, 3), (1, 1, 1, 0)
+TKS = (0, 0)
+SK = ((2, 2, 3, 4, 5, 2, 3, 4, 5, 6), (3, 4, 5, 6, 7, 8, 9, 10, 11, 12))
+NS = 1024
+CR2, BIG, SV = 1.5 * 2.0 ** 34, 30000.0, 65536.0
+LS, AS_ = True, (1, 0)
 AN = 160
-HC = (0, 32, 64, NH // 16)
-FP = ((0, 4), (4, 8), (8, 12), (12, 14), (14, 16))
-FV = ((0, 2), (0, 2, 4))
-NP, NV = ((0, 4), (4, 8), (8, 11), (11, 13)), ()
-ZV = (320, 128)
-CV = ((0, 0, 16), (16, 0, 16))
-PS, SS = (0, 0), ((16, 16, 0), (16, 16, 15))
+HB, HC = ((0, 32, 103),) * 2, ((0, 32, 64, 103),) * 2
+FP = (((0, 4), (4, 8), (8, 12), (12, 14), (14, 16)),) * 2
+FV = ((1, 4), (0, 2, 4))
+ZC = ("SVVSSVSS", "SVSSS")
+ZB = (("B4", "B7", "B0", "B1", "B3", "B3", "B1", "B4"), ("B2", "B3", "B2", "B3", "B2"))
+ZV = ((0, 0), (256, 128))
+CV = ((16, 16, 16), (16, 0, 16))
+PS, SS = (0, 0), ((16, 16, 0), (16, 16, 0))
 
 SCRATCH = {}
-DIAG = {"NID": -1.0, "I5": 5.0, "IN5": -5.0, "I113": 113.0, "IN113": -113.0, "I238": 238.0, "IC": CR2, "INC": -CR2, "IN128": -128.0,
-        "IN16": -16.0, "I17": 17.0, "IK": 8192.0, "INK": -8192.0}
+DIAG = {"NID": -1.0, "I5": 5.0, "IN5": -5.0, "I113": 113.0, "IN113": -113.0, "IC": CR2, "INC": -CR2, "I19": 19.0,
+        "IN39": -2.0 ** 39, "I8S": 8.0 * SV, "IHS": SV / 2, "IN16": -16.0, "I17": 17.0, "IK": 8192.0, "INK": -8192.0}
 for _d, _l in (
-    ("bfloat16", [("XT", W), ("XA", ZS + NH + 16), ("NC", NH + 16), ("NK", W), ("KP", 128), ("KT", 128), ("MC", 104), ("XB", ZS + NH), ("Z", K + 16), ("FL", K), ("GS", 2 * NS), ("PRS", 1024), ("GN", CAP), ("MN", 128), ("DM", CAP),
-                  ("G0", CAP), ("WN", 4704), ("GE0", 512), ("GE1", 512), ("QB", 128), ("NZ", W), ("NZ2", 512), ("BLK", 128), ("BP", 128), ("BN", 128), ("ID", 128),
-                  ("TRI", 128), ("TRU", 128), ("UU", 146), ("SW1", 144), ("SW16", 144), ("SW4", 144), ("SB", 128), ("G8B", 8),
+    ("bfloat16", [("XT", W), ("XA", ZS + NH + 16), ("NC", K), ("NK", W), ("KP", 128), ("KT", 128), ("LM", 256), ("CBS", 144), ("G82", 16), ("C16", 16), ("XB", ZS + NH), ("Z", K + 16), ("FL", K), ("GS", 2 * NS), ("PRS", 1024), ("GN", CAP), ("MN", 128), ("DM", CAP),
+                  ("G0", CAP), ("WN", 4704), ("GE0", 768), ("GE1", 768), ("QB", 128), ("NZ", W), ("NZ2", 1024), ("BLK", 128), ("BP", 128), ("BN", 128), ("ID", 128),
+                  ("TRI", 128), ("TRU", 128), ("UU", 146), ("SW1", 144), ("SW16", 144), ("SW4", 144), ("SB", 128), ("G8B", 8), ("G8K", 8), ("ICX", 128),
                   ("CB", 128), ("ONE", 128), ("TM255", 128), ("FS", 384), ("AS", 480), ("SF", NH), ("BL", NH), ("SG", 256),
                   ("AL", 256), ("A5", 272), ("MK", 128), ("CIB", 256), ("WP", 4704), ("WS", 9248), ("KM", 32), ("QS", 32), ("US", 32)]
      + [(n, 128) for n in DIAG]),
-    ("float32", [("QF", 16), ("PC", 8), ("CI", 146), ("CG", 128), ("CR", 128), ("CQ", 144), ("E32", 32), ("KD", 32), ("BLKF", 128), ("LD0", 32), ("LD1", 32), ("G16", 24), ("COL", 16),
-                 ("TF", 160), ("PL", 128), ("W3", 272), ("HP", 104), ("HG", 104), ("C8", 8), ("W35", 264), ("T5", 4), ("L1", 256), ("AC", 256), ("IDF", 128), ("TT", 128)]),
-    ("float16", [("SH", NH), ("QH", NH), ("TM", 128), ("IM", 128), ("G80", 104), ("LG", 104), ("J50", 128), ("J51", 128), ("AP", 256), ("ST", 8 * 256),
-                 ("FF", 8 * 256), ("RR", 256), ("JB", 128), ("JS", 2), ("G4", 24), ("L2", 256), ("KEY", 128), ("TK", 128)]),
+    ("float32", [("QF", 16), ("PC", 8), ("CI", 146), ("CG", 128), ("CR", 128), ("CQ", 144), ("E32", 32), ("KD", 32), ("BLKF", 128), ("G16", 24), ("COL", 16),
+                 ("TF", 160), ("PL", 128), ("W3", 272), ("QT", 512), ("W35", 264), ("T5", 4), ("TT", 128)]),
+    ("float16", [("SH", NH), ("QH", NH), ("LD0", 64), ("LD1", 64), ("DN", 128), ("I785", 128), ("J50", 128), ("J51", 128), ("AP", 256), ("ST", 8 * 256),
+                 ("FF", 8 * 256), ("JB", 128), ("JS", 2), ("G4", 24), ("G1", 24), ("L1", 256), ("L2", 256), ("KEY", 128), ("TK", 128)]),
     ("int32", [("QI", 16), ("PI", 8), ("TI", 256), ("TJ", 256)]),
     ("uint16", [("SO", 128), ("SP", 128), ("PM0", 16), ("PM1", 16), ("SC", 20), ("OF", 256), ("FO", 128)]),
 ):
@@ -42,10 +55,12 @@ for _d, _l in (
 for _b in range(8):
     SCRATCH["B%d" % _b] = ("psum", [128, 512], "float32")
 SEMAPHORES = ["sV", "sS", "sP", "sG", "lq", "lx0", "lx1", "lx2", "lx3", "ca0", "ca1", "cl0", "cl1", "ga0", "ga1", "gl0", "gl1",
-              "y0", "y1", "y2", "y3", "y4", "y5", "y6", "y7", "xc0", "xc1"]
+              "y0", "y1", "y2", "y3", "y4", "y5", "y6", "y7", "xc0", "xc1", "ge0", "ge1"]
 TWO = ("bfloat16", "float16", "uint16")
 CYC, PEC, GAT, SCA, FIXV, FIXS, HOP, SELF, GL = 1.0, 0.5, 1.56, 3.8, 60.0, 90.0, 75.0, 50.0, 2200.0
-TRIES = 5000
+LC, LG = (1500.0, 2500.0), 900.0
+CASES = ()
+TRIES, SLACK = 12000, 100.0
 PLAN = {}
 
 
@@ -65,6 +80,7 @@ def build(g, core, T, topo):
     def ap(r):
         if not isinstance(r, tuple): return r
         if r[0] == "ind": return ap(r[1]).indirect(ap(r[2]))
+        if len(r) > 4: return T[r[0]][r[4]:r[5], r[1]:r[2]:r[3]]
         if r[3] == 1: return T[r[0]][:, r[1]:r[2]]
         return T[r[0]][:, r[1]:r[2]:r[3]]
 
@@ -78,6 +94,7 @@ def build(g, core, T, topo):
 
     def add(eng, fn, reads, writes, cost, tok=None, lat=0.0):
         ops.append({"e": eng, "f": fn, "r": regs(reads), "w": regs(writes), "c": cost, "tok": tok, "lat": lat,
+                    "n": sum(width(r) for r in reads if isinstance(r, tuple) and r[0] == "ind"),
                     "chain": chain[0], "after": after[0]})
 
     def vcost(out, ins, two=False):
@@ -170,7 +187,7 @@ def build(g, core, T, topo):
     ts(R("PI", 2, 3), R("PI", 0, 1), 15, ALU.bitwise_and)
     cp(rc, R("PI", 2, 3))
     ts(R("E32"), R("CR", 0, 32), rc, ALU.is_equal)
-    cp(R("G8B"), R("G16", 8, 16)); ts(R("G4"), R("G16"), 4.0, ALU.mult)
+    cp(R("G8B"), R("G16", 8, 16)); ts(R("G4"), R("G16"), 4.0, ALU.mult); act(R("G1"), R("G16"), ACT.Copy)
     ts(gc16, gcol, 16.0, ALU.mult, 15.0, ALU.add)
     ts(g43, gcol, 4.0, ALU.mult, 3.0, ALU.add)
     ts(p4k, pc, 4096.0, ALU.add)
@@ -183,8 +200,9 @@ def build(g, core, T, topo):
     iota(R("QS", 0, 16), [[0, 16]], 0, 0); act(R("QS", 16, 32), R("QF"), ACT.Identity, None, 1.0 / 128)
     ts(R("BLKF"), R("CG"), gcol, ALU.is_equal)
     act(R("BLK"), R("BLKF"), ACT.Copy)
-    ts(ID, R("CI", 0, 128), pc, ALU.is_equal); act(R("IDF"), ID, ACT.Copy)
+    ts(ID, R("CI", 0, 128), pc, ALU.is_equal)
     for nm, v in DIAG.items(): act(R(nm), ID, ACT.Identity, None, v)
+    act(R("I785"), ID, ACT.Identity, None, -785.5); act(R("G8K"), R("G16", 8, 16), ACT.Identity, None, 2048.0)
     act(R("BP"), R("BLK"), ACT.Identity, None, 2048.0); act(R("BN"), R("BLK"), ACT.Identity, None, -2048.0)
     ts(R("COL", 6, 7), pc, -256.0, ALU.mult, -128.0, ALU.add)
     act(R("UU"), R("CI"), ACT.Sigmoid, R("COL", 6, 7), 256.0)
@@ -193,19 +211,26 @@ def build(g, core, T, topo):
     ts(R("SW1"), R("CI", 0, 144), gc16, ALU.is_equal)
     act(R("SW16"), R("SW1"), ACT.Identity, None, 1.0 / 16)
     ts(R("SW4"), R("CQ"), g43, ALU.is_equal)
+    for a in (0, 8): act(R("G82", a, a + 8), R("G16", 8, 16), ACT.Copy)
     ts(R("MK"), R("CR"), rc, ALU.is_equal)
     ts(R("JB"), R("MK"), p4k, ALU.mult, -4096.0, ALU.add)
     act(R("MN"), R("MK"), ACT.Identity, -8192.0, 8192.0)
     for a in (0, 128): act(R("DM", a, a + 128), R("MK"), ACT.Identity, None, 256.0)
     ts(R("COL", 5, 6), rc, 4.0, ALU.mult, 4640.0, ALU.add)
     ts(R("JS", 0, 1), rc, 0.0, ALU.is_gt, R("COL", 5, 6), ALU.mult)
-    act(R("TM255"), ONE, ACT.Identity, None, -255.0); act(R("TM"), ONE, ACT.Identity, None, -1536.0); act(R("IM"), ID, ACT.Identity, None, -MOD)
+    act(R("TM255"), ONE, ACT.Identity, None, -255.0)
     cp(R("QH", 0, 128), R("CI", 0, 128))
     for a in (128, 256, 512, 1024):
         b = min(2 * a, NH); ts(R("QH", a, b), R("QH", 0, b - a), float(a), ALU.add)
     cp(R("CIB"), R("QH", 0, 256))
-    for r in (R("XA", 2 * W, ZS), R("XB", 2 * W, ZS), R("Z", K, K + 16)): iota(r, [[0, 16]], 0, 0)
-    for r in (R("W3", 128, 136), R("W3", 264, 272), R("W35", 256, 264)): iota(r, [[0, 8]], int(BIG), 0)
+
+    def late_constants():
+        for r in (R("XA", 2 * W, ZS), R("XB", 2 * W, ZS), R("Z", K, K + 16)): iota(r, [[0, 16]], 0, 0)
+        for r in (R("W3", 128, 136), R("W3", 264, 272), R("W35", 256, 264)): iota(r, [[0, 8]], int(BIG), 0)
+        iota(R("ICX"), [[0, 128]], 0, 0)
+        for k in range(3):
+            add("G", lambda k=k: [g.affine_select(ap(R("ICX")), ap(R("ICX")), [[0, 128]], ALU.not_equal, 255.0 * 2 ** (31 - 8 * k), -k, 1)],
+                [R("ICX")], [R("ICX")], 200 + 256 * CYC)
 
     def round_constants(t):
         iota(R("TF", 128, 144), [[37 * 16, 16]], t, 37)
@@ -215,18 +240,18 @@ def build(g, core, T, topo):
         iota(R("TF", 0, 128), [[148, 128]], t, 0)
         ts(R("TI", 0, 128), R("TF", 0, 128), bjc, ALU.add)
         ts(R("TJ", 0, 128), R("TI", 0, 128), 255, ALU.bitwise_and)
-        ts(R("J5%d" % t), R("TJ", 0, 128), 5.0, ALU.mult, -793.5, ALU.add)
+        ts(R("J5%d" % t), R("TJ", 0, 128), 5.0, ALU.mult, 239.0, ALU.add)
         if t == 0:
-            iota(R("HP"), [[128, 13], [0, 8]], 0, 1)
-            iota(R("HG"), [[0, 13], [16, 8]], 0, 0)
-            ts(R("G80"), R("HG"), pc, ALU.is_equal, 4096.0, ALU.mult)
-            iota(R("XA", ZS + NH, ZS + NH + 16), [[0, 16]], 0, 0)
+            group(R("B5", 0, 128), [(R("TM255"), R("QB"))])
+            for a in range(0, 512, 128): act(R("QT", a, a + 128), R("B5", 0, 128), ACT.Identity, None, -1.0)
             iota(R("TT"), [[16, 128]], 1 + X1 - ZS, 0)
             ts(R("PL"), R("TT"), rc, ALU.add)
 
-    def starts(tb, jb, src, a, col, bias, scalar):
-        group(tb, [(ID, R("MN"))] * scalar + [(R(src, a, a + 128), R("BLK"))])
-        group(jb, [(ID, R("JB")), (R(src, a, a + 128), R("BP")), (R(src, a + 1, a + 129), R("BN"))])
+    def starts(tb, jb, src, a, col, bias, scalar, less=False):
+        group(jb, [(ID, R("JB"))], True, False)
+        if scalar or less: group(tb, [(ID, R("MN")) if scalar else (R("BN"), R("MK"))], True, False)
+        group(jb, [(R(src, a, a + 128), R("BP")), (R(src, a + 1, a + 129), R("BN"))], False, True)
+        group(tb, [(R(src, a, a + 128), R("BLK"))], not (scalar or less), True)
         if scalar: act(R("L1", col, col + 128), tb, ACT.Relu)
         else: tt(R("L1", col, col + 128), tb, R("MK"), ALU.mult)
         act(R("L2", col, col + 128), jb, ACT.Relu, bias)
@@ -234,7 +259,7 @@ def build(g, core, T, topo):
     def places(win, a, u, banks, scalar):
         c = 128 * u; o, e = R(banks[0], 128, 138), R(banks[0], 136, 137)
         starts(R(banks[0], 0, 128), R(banks[1], 0, 128), "AS", a, c, 520.0, scalar)
-        mm([(o, R("L1", c, c + 128), R("G16", 8, 18), True, False), (o, R("L2", c, c + 128), R("G4", 8, 18), False, False),
+        mm([(o, R("L1", c, c + 128), R("G1", 8, 18), True, False), (o, R("L2", c, c + 128), R("G4", 8, 18), False, False),
             (e, sel(0), R("AS", a + 144, a + 145), False, False), (e, ID, R("JS", 0, 1), False, True)])
         cp(R("SC", 10 * u, 10 * u + 10), o)
         scatter(R(win), R("SC", 10 * u, 10 * u + 9), R("CIB", 0, 144))
@@ -249,8 +274,12 @@ def build(g, core, T, topo):
         group(R(bank, 0, c1 - c0), [(sel(r, "SW16"), R("BL", 16 * c0 + r, 16 * c1, 16)) for r in range(16)])
         cp(R("SO", c0, c1), R(bank, 0, c1 - c0)); act(R("SB", c0, c1), R(bank, 0, c1 - c0), ACT.Identity, None, -1.0)
 
+    def pick(c0):
+        scan(R("G0"), R("DM"), R("BL", 16 * c0, 16 * c0 + CAP), 0.0, ALU.add, ALU.min)
+        cp(R("SO", c0, c0 + 16), R("G0", 15, CAP, 16)); act(R("SB", c0, c0 + 16), R("G0", 15, CAP, 16), ACT.Identity, None, -1.0)
+
     def within(bank, w3, c0, c1, ns, sub, z=0):
-        h = c1 - ns
+        h = (c1 - ns + 1) // 2 * 2 if ns else c1; ns = c1 - h
         if ns:
             act(R("SH", 16 * h, 16 * c1), ind(w3, R("SO", h, c1)), ACT.Copy)
             group(R(sub, 0, 16 * ns), [(ID, R("QH", 16 * h, 16 * c1)), (NID, R("SH", 16 * h, 16 * c1))])
@@ -259,29 +288,36 @@ def build(g, core, T, topo):
         group(R(bank, 0, c1 - c0), [(R("IN16"), R("SB", c0, c1))] + [(sel(r), R("SF", 16 * c0 + r, 16 * c1, 16)) for r in range(16)])
         cp(R("SP", c0, c1), R(bank, 0, c1 - c0))
 
-    def flags(t, bank, u0, u1, scalar):
+    def flags(t, bank, u0, u1, scalar, later=False):
         items = []; nm = ("NZ", "NC", "NK")[t]
         for u in range(u0, u1):
-            o = R(bank, 128 * (u - u0), 128 * (u - u0) + 128); a = ZS + 128 * u
+            o = R(bank, 128 * (u - u0), 128 * (u - u0) + 128); z = R("Z", W * (u // 16) + u % 16, W * (u // 16) + W, 16)
             if t == 0: items.append((o, R("XT", 128 * u, 128 * u + 128), R("QB"), True, True))
             elif t == 2: items.append((o, R("XT", u, W, 16), R("QB"), True, True))
-            else: items += [(o, R("TM255"), R("QB"), True, False), (o, R("XA", a, a + 128), R("QB"), False, True)]
+            else: items += [(o, R("TM255"), R("QB"), True, False)] * (scalar > 0) + [(o, z, R("QB"), not scalar, True)]
         mm(items)
         nz, pb = R(nm, 128 * u0, 128 * u1), R(bank, 0, 128 * (u1 - u0))
-        if scalar:
-            act(R("NZ2", 0, width(nz)), pb, ACT.Sign); act(nz, R("NZ2", 0, width(nz)), ACT.Square)
-        else: ts(nz, pb, 0.0, ALU.not_equal)
+
+        def flag():
+            if scalar:
+                sg = R("NZ2", 512 * (u0 // 4 % 2), 512 * (u0 // 4 % 2) + width(nz))
+                act(sg, pb, ACT.Sign)
+                if scalar == 2: ts(nz, sg, 0.0, ALU.not_equal)
+                else: act(nz, sg, ACT.Square)
+            elif t == 1: tt(nz, pb, R("QT", 0, width(nz)), ALU.not_equal)
+            else: ts(nz, pb, 0.0, ALU.not_equal)
+        if later: return flag
+        flag()
 
     others = [r for r in range(NR) if r != rank]
-    for k in range(4): flags(0, "B%d" % k, 4 * k, 4 * k + 4, k == 0)
-    for k in (1, 0, 2, 3):
-        group(R("B7", 0, 1), [(R("NZ", 128 * u, 128 * u + 128), R("ONE", 0, 1)) for u in range(4 * k, 4 * k + 4)], k == 1, k == 3)
+    for k in range(4): flags(0, "B%d" % k, 4 * k, 4 * k + 4, F0[k])
+    for k in range(4):
+        group(R("B7", 0, 2), [(R("NZ", 128 * u, 128 * u + 128), R("ONE", 0, 2)) for u in range(4 * O0[k], 4 * O0[k] + 4)], k == 0, k == 3)
     for t in range(2):
         LD, GE, XR = "LD%d" % t, "GE%d" % t, ("XA", "XB")[t]
-        mine = R(LD, 4 * rank, 4 * rank + 1)
-        if t == 0: cp(mine, R("B7", 0, 1))
-        else:
-            tt(R("C8"), R("B7", 0, 8), R("G16", 8, 16), ALU.mult); red(mine, R("C8"), ALU.add)
+        mine, slots = (R(LD, 8 * rank, 8 * rank + 8), R(LD)) if t else (R(LD, 8 * rank, 8 * rank + 2), R(LD, 0, 64, 8))
+        if t == 0: cp(mine, R("B7", 0, 2))
+        else: tt(mine, R("B2", 0, 8), R("G16", 8, 16), ALU.mult)
 
         def send_counts(t=t, mine=mine):
             ids = []; m = None
@@ -293,13 +329,14 @@ def build(g, core, T, topo):
         ne = len(topo.engines(core, T.cores[others[0]]))
         add("G", send_counts, [R(LD)], [R("COL", 8 + t, 9 + t)], 300, ("cl%d" % t, ne), GL)
         sent = len(ops) - 1
-        add("A", None, [R("COL", 8 + t, 9 + t)], [R(LD, 0, 32, 2)], 0, ("ca%d" % t, ne * len(others)), 1500)
-        after[0] = sent if t == 1 else None
-        round_constants(t)
+        add("A", None, [R("COL", 8 + t, 9 + t)], [R(LD)], 0, ("ca%d" % t, ne * len(others)), LC[t])
+        if t == 0: round_constants(0)
         after[0] = sent
+        if t == 0: round_constants(1)
         for nm, n in (("WN", CAP), ("WP", MP), ("WS", NH)): iota(R(nm, 0, n), [[0, n]], 0, 0)
         if t == 0:
-            for k in range(4): flags(2, "B%d" % k, 4 * k, 4 * k + 4, k < 3)
+            late_constants()
+            for k in range(4): flags(2, "B%d" % k, 4 * k, 4 * k + 4, F2[k])
         after[0] = None
         if t == 0:
             for k in range(4): ts(R(XR, X1 + 512 * k, X1 + 512 * k + 512), R("XT", 512 * k, 512 * k + 512), -1.0, ALU.mult, 255.0, ALU.add)
@@ -308,28 +345,32 @@ def build(g, core, T, topo):
         AO = AN
         mn0, mn1, coef = R("COL", 0, 1), R("COL", 1, 2), R("COL", 2, 3)
         group(R("B4", 0, 32), [(ID, R("KM")), (ID, R("QS"))] + [(R("IC"), R("US"))] * t, True, False)
-        red(R("COL", 3, 4), R(LD, 0, 32, 4), ALU.add)
+        red(R("COL", 3, 4), slots, ALU.add)
         ts(R("KD"), R("E32"), R("COL", 3, 4), ALU.mult)
         group(R("B4", 0, 32), [(R("BLKF"), R("KD"))], False, True)
         red(mn0, R("B4", 0, 16), ALU.min); red(mn1, R("B4", 16, 32), ALU.min)
         ts(coef, mn1, mn0, ALU.subtract, 128.0, ALU.mult)
-        ts(R("CB"), R("BLK"), coef, ALU.mult)
+        ts(R("C16"), R("G82"), coef, ALU.mult)
         if t == 0: ts(R("US"), R("B4", 0, 32), mn0, ALU.subtract, 1.0 / 32, ALU.is_lt)
-        c8 = R("CB", 0, 128, 16)
-        mm([(R("B5", 0, 128), R("TM255"), R("CB"), True, False)]
-           + [(R("B5", r, 128, 16), R(XR, X1 + r, X1 + W, 16), c8, False, r == 15) for r in range(16)])
+        act(R("CB"), R("BLK"), ACT.Identity, None, coef); act(R("CBS"), R("SW4"), ACT.Identity, None, coef)
+        if t == 0: mm([(R("B5", r, 128, 16), R("XT", r, W, 16), R("C16", 0, 8), True, True) for r in range(16)])
+        else:
+            mm([(R("B5", r, 128, 16), R(XR, X1 + r, X1 + W, 16), R("C16", 0, 8), r == 0, False) for r in range(16)])
+            group(R("B5", 0, 128), [(R("TM255"), R("CB"))], False, True)
         win = R(XR, X1, ZS)
-        ts(R("FS", 128, 256), R("B5", 0, 128), 0.0, ALU.is_gt)
-        act(R("FS", 0, 128), R("B5", 0, 128), ACT.Sigmoid, -128.0, -256.0)
+        ts(R("FS", 128, 256), R("B5", 0, 128), 0.0, ALU.is_gt if t else ALU.is_lt)
+        act(R("FS", 0, 128), R("B5", 0, 128), ACT.Sigmoid, -128.0, -256.0 if t else 256.0)
         group(R("B6", 0, 146), [(R("FS", 128, 256), R("UU"))]); group(R("B7", 0, 146), [(R("FS", 0, 128), R("UU"))])
         cp(R("AS", AN, AN + 146), R("B6", 0, 146)); act(R("AS", 0, 146), R("B7", 0, 146), ACT.Copy)
         places("WN", AN, 1, ("B0", "B1", "B6"), False)
         marks("WN", 64, 80, 64)
-        scan(R("G0"), R("DM"), R("BL", 1024, 1280), 0.0, ALU.add, ALU.min)
-        cp(R("SO", 64, 80), R("G0", 15, CAP, 16)); act(R("SB", 64, 80), R("G0", 15, CAP, 16), ACT.Identity, None, -1.0)
+        pick(64)
         within("B4", R("W3", 136, 272), 64, 80, 0, None, 64)
-        act(R("G0"), ind(win, R("SP", 64, 80)), ACT.Identity, 255.0, -1.0)
-        act(R("GN"), ind(R("G0"), R("PM%d" % t)), ACT.Copy)
+        u, v = GV
+        if u: ts(R("G0", 0, 16 * u), ind(win, R("SP", 64, 64 + u)), -255.0, ALU.add)
+        if u < 16: act(R("G0", 16 * u, CAP), ind(win, R("SP", 64 + u, 80)), ACT.Identity, -255.0)
+        if v: cp(R("GN", 0, 16 * v), ind(R("G0"), R("PM%d" % t, 0, v)))
+        if v < 16: act(R("GN", 16 * v, CAP), ind(R("G0"), R("PM%d" % t, v, 16)), ACT.Copy)
         partner = T.cores[rank ^ XS[t]]
 
         def send_guests(t=t, GE=GE, partner=partner):
@@ -337,8 +378,9 @@ def build(g, core, T, topo):
             return [g.remote_dma(ap(R(GE, 0, CAP)), ap(R("GN")), T.sem["ga%d" % t], T.sem["gl%d" % t], pid, rid, topo.mask(core, partner))]
         ne = len(topo.engines(core, partner))
         add("G", send_guests, [R("GN")], [R("COL", 10 + t, 11 + t)], 300, ("gl%d" % t, ne), GL)
-        add("A", None, [R("COL", 10 + t, 11 + t)], [R(GE, 0, CAP)], 0, ("ga%d" % t, ne), 900)
-        act(R(GE, 256, 512), R(GE, 0, 256), ACT.Copy)
+        add("A", None, [R("COL", 10 + t, 11 + t)], [R(GE, 0, CAP)], 0, ("ga%d" % t, ne), LG)
+        add("Y", lambda GE=GE, t=t: [g.sync.dma_start(ap(R(GE, a, a + CAP)), ap(R(GE, 0, CAP))).then_inc(T.sem["ge%d" % t], 16) for a in (CAP, 2 * CAP)],
+            [R(GE, 0, CAP)], [R(GE, CAP, 3 * CAP)], 120, ("ge%d" % t, 32), 2500)
         places("WP", 0, 0, ("B2", "B3", "B7"), LS)
         for s in range(2):
             marks("WP", 32 * s, 32 * s + 32); blocks("B%d" % s, 32 * s, 32 * s + 32)
@@ -346,28 +388,40 @@ def build(g, core, T, topo):
             c = 128 * s; pbk = R("B%d" % (5 + s), 0, 128); ab = R("B7" if s else "B3", 0, 128); a = R("AP", c, c + 128)
             group(ab, [(R("SW4", 12 - 4 * q, 140 - 4 * q), R("BL", 512 * s + q, 512 * s + 512, 4)) for q in range(4)], True, False)
             within("B%d" % s, R("W3", 0, 136), 32 * s, 32 * s + 32, PS[s], "B2")
-            act(R("PRS", 512 * s, 512 * s + 512), ind(win, R("SP", 32 * s, 32 * s + 32)), ACT.Copy)
+            u, v, w = 32 * s, 32 * s + PV[t][s], 32 * s + 32
+            if v > u: cp(R("PRS", 16 * u, 16 * v), ind(win, R("SP", u, v)))
+            if w > v: act(R("PRS", 16 * v, 16 * w), ind(win, R("SP", v, w)), ACT.Copy)
             group(ab, [(R("SW4", 12 - 4 * q, 140 - 4 * q), R("SF", 512 * s + q, 512 * s + 512, 4)) for q in range(4)], False, True)
-            if AS_[s]: act(a, ab, ACT.Identity, -1023.5)
-            else: ts(a, ab, -1023.5, ALU.add)
-            group(pbk, [(R("I238"), ONE), (NID, R("J5%d" % t)), (R("IN16"), a)] + rnd + [(ID, R("J5%d" % t)), (R("I17"), a)])
+            if AS_[s]: act(a, ab, ACT.Identity, -2048.0)
+            else: ts(a, ab, -2048.0, ALU.add)
+            group(pbk, [(R("I785"), ONE), (NID, R("J5%d" % t)), (R("IN16"), a)] + rnd + [(ID, R("J5%d" % t)), (R("I17"), a)])
         group(R("B2", 0, 128), [(R("TRI"), R("AS", AO + 1, AO + 129)), (R("TRU"), R("AS", AO, AO + 128)), (R("IK"), ONE),
                                 (R("INK"), R("AS", AO + 1, AO + 129)), (R("IK"), R("AS", AO, AO + 128))])
         act(R("KEY"), R("B2", 0, 128), ACT.Copy)
         if t == 0:
             group(R("B2", 128, 129), [(R("BLK"), R("AS", AO + 144, AO + 145))]); act(R("T5", 0, 1), R("B2", 128, 129), ACT.Copy)
-        turn = 0
+            act(R("DN"), NID, ACT.Identity, None, R("T5", 0, 1))
         for s in range(2):
-            nv = ZV[s]; pv = R(("B4", "B7")[s], 0, nv)
-            group(pv, [(ID, R("PRS", 512 * s, 512 * s + nv))])
-            for kk in range(4): tt(R("Z", W * s + kk, W * s + 4 * nv, 4), pv, R(GE, 64 * kk, 64 * kk + nv), ALU.subtract)
-            for i in range(nv, 512, 128):
-                bank = ("B2", "B3")[turn % 2]; turn += 1; m = min(128, 512 - i)
+            nv = ZV[t][s]; pv = R(("B4", "B7")[s], 0, nv)
+            if nv:
+                group(pv, [(ID, R("PRS", 512 * s, 512 * s + nv))])
                 for kk in range(4):
-                    group(R(bank, kk, 4 * m, 4), [(ID, R("PRS", 512 * s + i, 512 * s + i + m)),
-                                                  (NID, R(GE, i % 256 + 64 * kk, i % 256 + 64 * kk + m))])
-                act(R("Z", W * s + 4 * i, W * s + 4 * (i + m)), R(bank, 0, 4 * m), ACT.Copy)
-        xw = R(XR, 0, 2 * W); m1 = M1; cut = (0, m1, 128 - MV)
+                    h = min(nv, CAP - 64 * kk)
+                    tt(R("Z", W * s + kk, W * s + 4 * h, 4), R(pv[0], 0, h), R(GE, 64 * kk, 64 * kk + h), ALU.add)
+                    if h < nv: tt(R("Z", W * s + 4 * h + kk, W * s + 4 * nv, 4), R(pv[0], h, nv), R(GE, 0, nv - h), ALU.add)
+        pieces = [(i, min(128, 512 * s + 512 - i)) for s in range(2) for i in range(512 * s + ZV[t][s], 512 * s + 512, 128)]
+        for u, (i, m) in enumerate(pieces):
+            bank = ZB[t][u]
+            mm([(R(bank, kk, 4 * m, 4), ID, R("PRS", i, i + m), kk == 0, False) for kk in range(4)])
+            items = []
+            for kk in range(4):
+                a = (i + 64 * kk) % CAP; h = min(m, CAP - a)
+                items += [(R(bank, kk, 4 * h, 4), ID, R(GE, a, a + h), False, False)]
+                if h < m: items += [(R(bank, 4 * h + kk, 4 * m, 4), ID, R(GE, 0, m - h), False, False)]
+            mm(items[:-1] + [items[-1][:4] + (True,)])
+            if ZC[t][u] == "V": ts(R("Z", 4 * i, 4 * (i + m)), R(bank, 0, 4 * m), 0.0, ALU.max)
+            else: act(R("Z", 4 * i, 4 * (i + m)), R(bank, 0, 4 * m), ACT.Relu)
+        xw = R(XR, 0, 2 * W)
         tal = (R("B7", 0, 128), R("B4", 0, 128))
 
         def part(n, s):
@@ -384,94 +438,115 @@ def build(g, core, T, topo):
             ts(part(n, s)[1], R("OF", 128 * s, 128 * s + 128), -2048.0, ALU.add)
 
         def tally(n, s):
-            _, st, _, a = part(n, s)
-            if n < ET: group(tal[s], [(st, NID), (a, ID)] + rnd, n == 0, False)
+            _, st, f, a = part(n, s)
+            group(tal[s], [(R("I8S"), ONE)] * (n == 0) + [(st, NID), (a, ID), (R("I19"), f), (R("ICX"), ONE), (R("IN39"), ONE)], n == 0, False)
 
+        def shares(k):
+            MV, m1 = MK_.get((t, k), (MF, M1F) if t == 0 and k in FT else (MV0, M1))
+            return MV, (0, m1, 128 - MV)
+
+        def offsets(k):
+            ts(R("OF", 128 * (k % 2), 128 * (k % 2) + 128), part(0, k % 2)[0], 3857.0, ALU.add)
+
+        def gather(k, h):
+            MV, cut = shares(k); s = k % 2; c = 128 * s + MV
+            act(R("GS", NS * s + 16 * cut[h], NS * s + 16 * cut[h + 1]), ind(xw, R("OF", c + cut[h], c + cut[h + 1])), ACT.Copy)
+
+        sums = [[(R("B2", 128 * v, 128 * v + 128), R("TM255"), R("CB"), v == 0, False) for v in range(2)]]
+        sums += [[(R("B2", 128 * v, 128 * v + 128), R("PRS", 512 * v + u, 512 * v + 512, 4), R("CBS", 12 - 4 * u, 140 - 4 * u), False, False)
+                  for v in range(2)] for u in range(4)]
+        sums += [[(R("B2", 4 * u + kk, 256, 16), R(GE, u + 64 * kk, u + 64 * kk + 509, 4), R("C16"), False, u == 3 and kk == 3)
+                  for kk in range(4)] for u in range(4)]
         chain[0] = True
         for k in range(2 * PR):
             n, s = k // 2, k % 2; pn, ps = (k - 1) // 2, (k - 1) % 2
             c, e = 128 * s, W * s
-            pbk, st, f, a = part(n, s)
+            fl = t == 0 and k in FT
+            MV, cut = shares(k); cut = (0, min(cut[1], 32), cut[2])
             gs = [R("GS", NS * s + 16 * cut[h], NS * s + 16 * cut[h + 1]) for h in range(2)]
             zs = [(e + 16 * (MV + cut[h]), e + 16 * (MV + cut[h + 1])) for h in range(2)]
             bk = [R("B%d" % h, 0, 16 * (cut[h + 1] - cut[h])) for h in range(2)]
-            ts(R("OF", c, c + 128), pbk, 1809.0, ALU.add)
+            offsets(k)
             if 0 < k < 2 * PR - 1: state(pn, ps)
+            if n == PR - 1: state(n, s)
             mm([(bk[0], ID, R("Z", *zs[0]), True, False)])
             more = k > 0 and pn < PR - 1
             if more: counts(ps)
-            if more: group(part(pn, ps)[0], [(R("I238"), ONE), (ID, part(pn, ps)[3]), (R("IN5"), part(pn, ps)[1])], True, False)
+            if more: group(part(pn, ps)[0], [(R("I785"), ONE), (ID, part(pn, ps)[3]), (R("IN5"), part(pn, ps)[1])], True, False)
             mm([(bk[1], ID, R("Z", *zs[1]), True, False)])
-            act(gs[0], ind(xw, R("OF", c + MV, c + MV + m1)), ACT.Copy)
+            if fl: flag = flags(1, "B2", 4 * FT.index(k), 4 * FT.index(k) + 4, False, True)
+            gather(k, 0)
             if more: relu(pn, ps)
             mm([(bk[0], NID, gs[0], False, True)])
             if more:
                 pb, pst, pf, _ = part(pn, ps)
                 group(pb, [(pf, R("IN113"))] + rnd + [(pf, R("I113")), (R("I5"), pst)], False, True)
-            act(gs[1], ind(xw, R("OF", c + MV + m1, c + 128)), ACT.Copy)
-            if n == PR - 1:
-                state(n, s)
+            gather(k, 1)
             mm([(bk[1], NID, gs[1], False, True)])
-            tt(R("FL", e, e + 16 * MV), ind(xw, R("OF", c, c + MV)), R("Z", e, e + 16 * MV), ALU.is_lt)
+            cuts = list(zip((0,) + TS.get((t, k), ()), TS.get((t, k), ()) + (MV,)))
+            for u, v in cuts[1:] + cuts[:1] if k == 2 * PR - 1 else cuts:
+                tt(R("FL", e + 16 * u, e + 16 * v), ind(xw, R("OF", c + u, c + v)), R("Z", e + 16 * u, e + 16 * v), ALU.is_lt)
+            if fl: flag()
             for h in range(2):
                 act(R("FL", *zs[h]), bk[h], ACT.Sigmoid, -128.0, 256.0)
             if more: tally(pn, ps)
-            if 2 <= k < 10:
-                v, u = (k - 2) // 4, (k - 2) % 4
-                mm([(R("B2", 128 * v, 128 * v + 128), R("TM255"), R("CB"), True, False)] * (u == 0)
-                   + [(R("B2", 128 * v + r, 128 * v + 128, 16), R("Z", W * v + r, W * v + W, 16), c8, False, r == 15) for r in range(4 * u, 4 * u + 4)])
-            if k == 10: act(R("SG"), R("B2", 0, 256), ACT.Sign, 0.5, -1.0)
+            if k in SK[t][:-1]: mm([x for u in range(9) if SK[t][u] == k for x in sums[u]])
+            if k == SK[t][-1]: act(R("SG"), R("B2", 0, 256), ACT.Sign, 0.5, -1.0)
         chain[0] = False
+        if t == 0:
+            for u in range(len(FT), 8): flags(1, FB[u - len(FT)], 4 * u, 4 * u + 4, FL8[u - len(FT)])
         for s in range(2):
             c = 128 * s; last = "B%d" % (5 + s); al = R("AL", c, c + 128)
-            for u in range(PR - 1): group(tal[s], [(R("IN128"), part(u, s)[2])], False, u == PR - 2)
-            if RS[s] & 1: act(R("RR", c, c + 128), tal[s], ACT.Identity, 1536.0 - 6144.0 / MOD, 1.0 / MOD)
-            else: ts(R("RR", c, c + 128), tal[s], 1.0 / MOD, ALU.mult, 1536.0 - 6144.0 / MOD, ALU.add)
-            if RS[s] & 2: act(R("AC", c, c + 128), tal[s], ACT.Copy)
-            else: cp(R("AC", c, c + 128), tal[s])
-            for u in range(ET, PR): group(R(last, 0, 128), [(part(u, s)[1], NID), (part(u, s)[3], ID)] + rnd, u == ET, False)
-            group(R(last, 0, 128), [(R("IM"), R("RR", c, c + 128)), (R("IM"), R("TM")), (R("IDF"), R("AC", c, c + 128))], False, False)
-            mm([(R(last, 0, 128), R("IK"), R("SG", c, c + 128), False, False)]
-               + [(R(last, r, 128, 16), R("FL", W * s + r, W * s + W, 16), R("G8B"), False, r == 15) for r in range(16)])
-            ts(al, R(last, 0, 128), 14336.0 + 8192.5, ALU.is_gt)
-            pre = R(tal[s][0], s, 129)
-            group(pre, [(R("AL", 0, 128), ONE)] * s + [(al, R("UU", s, 129))])
-            if s: act(R("A5", 15 + s + c, 144 + c), pre, ACT.Copy)
+            group(tal[s], [(part(PR - 1, s)[1], NID), (part(PR - 1, s)[3], ID), (R("IHS"), R("SG", c, c + 128))], False, False)
+            for u, v in CM if s else ((0, 128),):
+                mm([(R(tal[s][0], r, 128, 16) + (u, v), R("FL", W * s + 16 * u + r, W * s + 16 * v, 16), R("G8K"), False, r == 15)
+                    for r in range(16)])
+            es = ES[t][s]
+            if es[0]: act(al, tal[s], ACT.Sigmoid, -256 * 8.5 * SV + 128, 256.0)
+            else: ts(al, tal[s], 8.5 * SV - 0.5, ALU.is_gt)
+            pre = R(("B7", "B6")[s], s, 129)
+            if s: group(pre, [(R("AL", 0, 128), ONE)], True, False)
+            group(pre, [(al, R("UU", s, 129))], not s, True)
+            if es[1]: act(R("A5", 15 + s + c, 144 + c), pre, ACT.Copy)
             else: cp(R("A5", 15 + s + c, 144 + c), pre)
-            starts(R("B%d" % (2 * s), 0, 128), R("B%d" % (2 * s + 1), 0, 128), "A5", 15 + c, c, 1030.0 + c, False)
-            group(R(last, 0, 8), [(R("L1", c, c + 128), R("G16", 8, 16)), (R("L2", c, c + 128), R("G4", 8, 16))])
-            cp(R("SC", 8 * s, 8 * s + 8), R(last, 0, 8))
+            starts(R(("B3", "B0")[s], 0, 128), R(("B5", "B1")[s], 0, 128), "A5", 15 + c, c, 1030.0 + c, es[2] and not s, s)
+            if t == 0:
+                lm = R(("B7", "B4")[s], 256, 384)
+                group(lm, [(ONE, R("DN")), (R("INK"), al)], True, False)
+                group(lm, [(R("A5", 16 + c, 144 + c), R("TRI")), (R("A5", 15 + c, 143 + c), R("TRU"))], False, True)
+                if es[3]: act(R("LM", c, c + 128), lm, ACT.Sigmoid, -256 * 8191.5, -256.0)
+                else: ts(R("LM", c, c + 128), lm, -8191.5, ALU.is_lt)
+                group(R("B2", 0, 8), [(R("NC", 16 * c + 128 * r, 16 * c + 128 * r + 128), R("LM", c + r, c + 128, 16)) for r in range(16)], s == 0, False)
+            group(R(last, 0, 8), [(R("L1", c, c + 128), R("G1", 8, 16)), (R("L2", c, c + 128), R("G4", 8, 16))])
+            ts(R("SC", 8 * s, 8 * s + 8), R(last, 0, 8), 2048.0 * s, ALU.add)
             scatter(R("WS"), R("SC", 8 * s, 8 * s + 8), R("CIB", c, c + 128))
         group(R("B3", 0, 256), [(R("TRI"), R("A5", 16, 272)), (R("TRU"), R("A5", 15, 271))])
         act(R("W35", 0, 256), R("B3", 0, 256), ACT.Copy)
         group(R("B7", 0, 1), [(R("BLK"), R("A5", 271, 272))])
-        ts(R("TK"), R("KEY"), R("B7", 0, 1), ALU.subtract, 0.0, ALU.max)
+        if t == 0: ts(R("KP"), R("KEY"), R("B7", 0, 1), ALU.is_gt)
+        if TKS[t]:
+            act(R("T5", 1, 2), R("B7", 0, 1), ACT.Identity, None, -1.0); act(R("TK"), R("KEY"), ACT.Relu, R("T5", 1, 2))
+        else: ts(R("TK"), R("KEY"), R("B7", 0, 1), ALU.subtract, 0.0, ALU.max)
         if t == 0:
-            ts(R("KP"), R("KEY"), R("B7", 0, 1), ALU.is_gt)
-            ts(R("LG"), R("G80"), R("B7", 0, 1), ALU.min, R("T5", 0, 1), ALU.min)
             group(R("B0", 0, 128), [(R("KP"), ID)]); act(R("KT"), R("B0", 0, 128), ACT.Copy)
-            group(R("B1", 0, 104), [(ONE, R("LG"))]); tt(R("MC"), R("B1", 0, 104), R("HP"), ALU.is_gt)
+            group(R("B2", 0, 8), [(R("NK", 128 * r, 128 * r + 128), R("KT", r, 128, 16)) for r in range(16)], False, True)
 
         def sources(bank):
             group(R(bank, 0, 128), [(ID, R("KEY")), (R("INK"), R("TK"))])
             tt(R("TT"), R(bank, 0, 128), R("PL"), ALU.max)
             ts(R("FO"), R("TT"), float(ZS - X1 - 1), ALU.add)
-        if t == 1: sources("B7")
-        marks("WS", HC[0], HC[1]); blocks("B4", HC[0], HC[1])
-        marks("WS", HC[1], HC[-1]); blocks("B5", HC[1], HC[-1])
-        for u in range(len(HC) - 1):
-            within("B%d" % (4 + u % 3), R("W35"), HC[u], HC[u + 1], SS[t][u], "B%d" % (2 + u % 2))
-            a, h, b = HC[u], HC[u] + CV[t][u], HC[u + 1]
+        sources("B7")
+        hb, hc = HB[t], HC[t]
+        for u in range(len(hb) - 1):
+            marks("WS", hb[u], hb[u + 1])
+            if hb[u + 1] - hb[u] > 16: blocks("B%d" % (4 + u), hb[u], hb[u + 1])
+            else: pick(hb[u])
+        for u in range(len(hc) - 1):
+            within("B%d" % (4 + u % 3), R("W35"), hc[u], hc[u + 1], SS[t][u], "B%d" % (u % 2))
+            a, h, b = hc[u], min(hc[u] + CV[t][u], hc[u + 1]), hc[u + 1]
             if h > a: ts(R(XR, ZS + 16 * a, ZS + 16 * h), ind(R("Z"), R("SP", a, h)), 0.0, ALU.max)
             if b > h: act(R(XR, ZS + 16 * h, ZS + 16 * b), ind(R("Z"), R("SP", h, b)), ACT.Relu)
-        if t == 0:
-            sources("B6")
-            for k, (u0, u1) in enumerate(NP):
-                flags(1, "B%d" % (k % 2), u0, u1, k in NV)
-                group(R("B7", 0, 8), [(R("NC", 128 * u, 128 * u + 128), R("MC", 8 * u, 8 * u + 8)) for u in range(u0, u1)], k == 0, u1 == 13)
-                if k == 0:
-                    for h in (0, 8): group(R("B7", 0, 8), [(R("NK", 128 * r, 128 * r + 128), R("KT", r, 128, 16)) for r in range(h, h + 8)], False, False)
-        for k, (u0, u1) in enumerate(FP):
+        for k, (u0, u1) in enumerate(FP[t]):
             src = ind(R(XR, X1, ZS + min(128 * u1, NH)), R("FO", 8 * u0, 8 * u1))
             if t == 0:
                 o = R("XB", X1 + 128 * u0, X1 + 128 * u1)
@@ -548,26 +623,81 @@ def arrange(ops, hard):
     pri = [0.0] * n
     for i in range(n - 1, -1, -1):
         pri[i] = ops[i]["c"] + max([pri[x] + v for x, v in succ[i].items()] + [tail[i]])
-    best = passes(pri); free = [i for i in range(n) if not ops[i]["chain"]]
+    def waits(end):
+        ahead = {}; last = {}; out = []
+        for i in sorted(range(n), key=lambda i: end[i]):
+            ahead[i] = last.get(ops[i]["e"]); last[ops[i]["e"]] = i
+        i = max(range(n), key=lambda i: end[i] + tail[i])
+        while i is not None:
+            s = end[i] - ops[i]["c"]; by = [j for j, v in deps[i].items() if end[j] + v > s - 1e-6]
+            if by: i = by[draw(len(by))]
+            elif s > 1e-6:
+                if not (ops[i]["chain"] and ops[ahead[i]]["chain"]) and ahead[i] not in deps[i]: out.append((i, ahead[i]))
+                i = ahead[i]
+            else: i = None
+        return out
+    cases = []
+    for gat, far, late in CASES:
+        c = [o["c"] + o["n"] * (gat - GAT) for o in ops]
+        cases.append((c, [[(j, (v - ops[j]["lat"]) * far + ops[j]["lat"] * late) for j, v in deps[i].items()] for i in range(n)]))
+
+    def worth(end):
+        order = sorted(range(n), key=lambda i: (end[i] - ops[i]["c"], end[i], i)); out = max(end[i] + tail[i] for i in range(n))
+        for c, before in cases:
+            free = {}; e2 = [0.0] * n
+            for i in order:
+                s = free.get(ops[i]["e"], 0.0)
+                for j, v in before[i]:
+                    if e2[j] + v > s: s = e2[j] + v
+                e2[i] = free[ops[i]["e"]] = s + c[i]
+            out += max(e2[i] + tail[i] for i in range(n))
+        return out / (1 + len(cases))
+    total, end, back = passes(pri); total = worth(end); best = (total, end); held = waits(end)
     for k in range(TRIES):
-        key = list(best[2]); c = free[draw(len(free))]; near = [i for i in free if abs(best[1][i] - best[1][c]) < 3000]
-        for u in range(4): key[near[draw(len(near))]] += draw(2500)
-        for i in range(n - 1, -1, -1):
-            for x in succ[i]:
-                if key[i] <= key[x]: key[i] = key[x] + 1e-3
-        r = passes(key)
-        if r[0] <= best[0]: best = r
-    end = best[1]
+        key = [ops[i]["c"] - end[i] for i in range(n)]
+        for u in range(1 + draw(2)):
+            i, j = held[draw(len(held))]
+            if draw(3) == 0:
+                near = [x for x in range(n) if not ops[x]["chain"] and abs(end[x] - end[i]) < 2000]
+                for v in range(3): key[near[draw(len(near))]] += draw(2000)
+            elif draw(2): key[i] = max(key[i], key[j] + 1 + draw(600))
+            else:
+                key[j] = min(key[j], key[i] - 1 - draw(600))
+                for x in range(j, n):
+                    for y in deps[x]:
+                        if key[x] >= key[y]: key[x] = key[y] - 1e-3
+        for x in range(n - 1, -1, -1):
+            for y in succ[x]:
+                if key[x] <= key[y]: key[x] = key[y] + 1e-3
+        if draw(4): e2 = lay([(-key[x], x) for x in range(n)], deps, zero)
+        else: e2 = passes(key)[1]
+        r = worth(e2)
+        if r <= total + SLACK * (1 - k / TRIES):
+            total, end = r, e2; held = waits(end)
+            if r < best[0]: best = (r, e2)
+    end = best[1]; PLAN["worth"] = best[0]
     return sorted(range(n), key=lambda i: (end[i] - ops[i]["c"], end[i], i))
+
+
+def order_all(ops):
+    of = [i for i, o in enumerate(ops) if o["chain"] and o["w"][0][0] == "OF"]; n = len(of) // 2
+    cuts = [0, of[3], of[n - 4], of[n + 3], of[2 * n - 4], len(ops)]; order = []
+    for k in range(5):
+        a, b = cuts[k], cuts[k + 1]
+        if k % 2: order += range(a, b)
+        else:
+            part = [dict(o, after=None if o["after"] is None or o["after"] < a else o["after"] - a) for o in ops[a:b]]
+            order += [a + i for i in arrange(part, depend(part))]
+    return order
 
 
 def rank_program(g, core, T, topo):
     if T.rank_of(core) is None:
         return
     ops = build(g, core, T, topo)
-    if not PLAN:
+    if "deps" not in PLAN:
         PLAN["deps"] = depend(ops)
-        PLAN["order"] = arrange(ops, PLAN["deps"])
+        PLAN["order"] = order_all(ops)
     deps = PLAN["deps"]
     queue = {"V": g.vector, "S": g.scalar, "P": g.tensor, "G": g, "Y": g.sync}
     count = {}; known = {e: {} for e in queue}; token = {}; clock = {}

from concourse.bass import DstId, RemoteDMATransfer
from concourse.mybir import AluOpType, AxisListType, ActivationFunctionType

ALU, ACT = AluOpType, ActivationFunctionType
W, K, CAP, MP, PR, NR = 2048, 4096, 256, 1024, 8, 8
XS = (4, 3)
NH = 1648
X1, ZS = W, 2 * W + 16
MV0 = 84
M1 = 26
MF, M1F = 76, 30
MK_ = {(0, 0): (92, 30), (0, 15): (76, 20), (1, 14): (80, 20), (1, 15): (80, 30)}
TS = {}
ES = (((0, 0, 0, 0), (0, 1, 0, 0)),) * 2
PV = ((0, 0), (0, 0))
GV = (0, 0)
CM = ((0, 128),)
FT = (7, 8, 9, 10, 11, 12)
FB = ("B2", "B3", "B2")
FL8 = (0, 0, 0)
F0, O0, F2 = (1, 0, 0, 0), (1, 0, 2, 3), (1, 1, 1, 0)
TKS = (0, 0)
SK = ((2, 2, 3, 4, 5, 2, 3, 4, 5, 6), (3, 4, 5, 6, 7, 8, 9, 10, 11, 12))
NS = 1024
CR2, BIG, SV = 1.5 * 2.0 ** 34, 30000.0, 65536.0
LS, AS_ = True, (1, 0)
AN = 160
HB, HC = ((0, 32, 103),) * 2, ((0, 32, 64, 103),) * 2
FP = (((0, 4), (4, 8), (8, 12), (12, 14), (14, 16)),) * 2
FV = ((1, 4), (0, 2, 4))
ZC = ("SVVSSVSS", "SVSSS")
ZB = (("B4", "B7", "B0", "B1", "B3", "B3", "B1", "B4"), ("B2", "B3", "B2", "B3", "B2"))
ZV = ((0, 0), (256, 128))
CV = ((16, 16, 16), (16, 0, 16))
PS, SS = (0, 0), ((16, 16, 0), (16, 16, 0))

SCRATCH = {}
DIAG = {"NID": -1.0, "I5": 5.0, "IN5": -5.0, "I113": 113.0, "IN113": -113.0, "IC": CR2, "INC": -CR2, "I19": 19.0,
        "IN39": -2.0 ** 39, "I8S": 8.0 * SV, "IHS": SV / 2, "IN16": -16.0, "I17": 17.0, "IK": 8192.0, "INK": -8192.0}
for _d, _l in (
    ("bfloat16", [("XT", W), ("XA", ZS + NH + 16), ("NC", K), ("NK", W), ("KP", 128), ("KT", 128), ("LM", 256), ("CBS", 144), ("G82", 16), ("C16", 16), ("XB", ZS + NH), ("Z", K + 16), ("FL", K), ("GS", 2 * NS), ("PRS", 1024), ("GN", CAP), ("MN", 128), ("DM", CAP),
                  ("G0", CAP), ("WN", 4704), ("GE0", 768), ("GE1", 768), ("QB", 128), ("NZ", W), ("NZ2", 1024), ("BLK", 128), ("BP", 128), ("BN", 128), ("ID", 128),
                  ("TRI", 128), ("TRU", 128), ("UU", 146), ("SW1", 144), ("SW16", 144), ("SW4", 144), ("SB", 128), ("G8B", 8), ("G8K", 8), ("ICX", 128),
                  ("CB", 128), ("ONE", 128), ("TM255", 128), ("FS", 384), ("AS", 480), ("SF", NH), ("BL", NH), ("SG", 256),
                  ("AL", 256), ("A5", 272), ("MK", 128), ("CIB", 256), ("WP", 4704), ("WS", 9248), ("KM", 32), ("QS", 32), ("US", 32)]
     + [(n, 128) for n in DIAG]),
    ("float32", [("QF", 16), ("PC", 8), ("CI", 146), ("CG", 128), ("CR", 128), ("CQ", 144), ("E32", 32), ("KD", 32), ("BLKF", 128), ("G16", 24), ("COL", 16),
                 ("TF", 160), ("PL", 128), ("W3", 272), ("QT", 512), ("W35", 264), ("T5", 4), ("TT", 128)]),
    ("float16", [("SH", NH), ("QH", NH), ("LD0", 64), ("LD1", 64), ("DN", 128), ("I785", 128), ("J50", 128), ("J51", 128), ("AP", 256), ("ST", 8 * 256),
                 ("FF", 8 * 256), ("JB", 128), ("JS", 2), ("G4", 24), ("G1", 24), ("L1", 256), ("L2", 256), ("KEY", 128), ("TK", 128)]),
    ("int32", [("QI", 16), ("PI", 8), ("TI", 256), ("TJ", 256)]),
    ("uint16", [("SO", 128), ("SP", 128), ("PM0", 16), ("PM1", 16), ("SC", 20), ("OF", 256), ("FO", 128)]),
):
    for _n, _c in _l: SCRATCH[_n] = ("sbuf", [128, _c], _d)
for _b in range(8):
    SCRATCH["B%d" % _b] = ("psum", [128, 512], "float32")
SEMAPHORES = ["sV", "sS", "sP", "sG", "lq", "lx0", "lx1", "lx2", "lx3", "ca0", "ca1", "cl0", "cl1", "ga0", "ga1", "gl0", "gl1",
              "y0", "y1", "y2", "y3", "y4", "y5", "y6", "y7", "xc0", "xc1", "ge0", "ge1"]
TWO = ("bfloat16", "float16", "uint16")
CYC, PEC, GAT, SCA, FIXV, FIXS, HOP, SELF, GL = 1.0, 0.5, 1.56, 3.8, 60.0, 90.0, 75.0, 50.0, 2200.0
LC, LG = (1500.0, 2500.0), 900.0
CASES = ()
TRIES, SLACK = 12000, 100.0
PLAN = {}


def R(name, a=0, b=None, s=1):
    return (name, a, SCRATCH[name][1][1] if b is None else b, s)


def width(r):
    if r[0] == "ind": return 16 * width(r[2])
    return (r[2] - r[1] + r[3] - 1) // r[3]


def build(g, core, T, topo):
    rank = T.rank_of(core)
    ops = []; chain = [False]; after = [None]

    def ap(r):
        if not isinstance(r, tuple): return r
        if r[0] == "ind": return ap(r[1]).indirect(ap(r[2]))
        if len(r) > 4: return T[r[0]][r[4]:r[5], r[1]:r[2]:r[3]]
        if r[3] == 1: return T[r[0]][:, r[1]:r[2]]
        return T[r[0]][:, r[1]:r[2]:r[3]]

    def regs(rs):
        out = []
        for r in rs:
            if isinstance(r, tuple):
                if r[0] == "ind": out += [r[1], r[2]]
                else: out.append(r)
        return out

    def add(eng, fn, reads, writes, cost, tok=None, lat=0.0):
        ops.append({"e": eng, "f": fn, "r": regs(reads), "w": regs(writes), "c": cost, "tok": tok, "lat": lat,
                    "n": sum(width(r) for r in reads if isinstance(r, tuple) and r[0] == "ind"),
                    "chain": chain[0], "after": after[0]})

    def vcost(out, ins, two=False):
        n = width(out)
        if ins[0][0] == "ind": return FIXV + n * GAT * CYC
        if two: k = 1.0 if any(SCRATCH[r[0]][0] == "psum" for r in ins) else 2.0
        else: k = 0.5 if all(SCRATCH[r[0]][2] in TWO for r in [out] + ins) else 1.0
        return FIXV + max(30.0, n * k) * CYC

    def ts(out, in0, s1, op0, s2=None, op1=None):
        if op1 is None: fn = lambda: [g.vector.tensor_scalar(ap(out), ap(in0), ap(s1), None, op0)]
        else: fn = lambda: [g.vector.tensor_scalar(ap(out), ap(in0), ap(s1), ap(s2), op0, op1)]
        add("V", fn, [in0, s1, s2], [out], vcost(out, [in0]))

    def tt(out, in0, in1, op):
        add("V", lambda: [g.vector.tensor_tensor(ap(out), ap(in0), ap(in1), op)], [in0, in1], [out], vcost(out, [in0, in1], True))

    def cp(out, in_):
        add("V", lambda: [g.vector.tensor_copy(ap(out), ap(in_))], [in_], [out], vcost(out, [in_]))

    def scatter(win, off, in_):
        add("V", lambda: [g.vector.tensor_copy(ap(ind(win, off)), ap(in_))], [in_, off], [win], FIXV + width(in_) * SCA * CYC)

    def red(out, in_, op):
        add("V", lambda: [g.vector.tensor_reduce(ap(out), ap(in_), AxisListType.X, op)], [in_], [out], FIXV + max(30, width(in_)) * CYC)

    def scan(out, d0, d1, init, op0, op1):
        add("V", lambda: [g.vector.tensor_tensor_scan(ap(out), ap(d0), ap(d1), ap(init), op0, op1)], [d0, d1, init], [out], vcost(out, [d0, d1]))

    def fill(out, v):
        add("V", lambda: [g.vector.memset(ap(out), v)], [], [out], vcost(out, [out]))

    def act(out, in_, func, bias=None, scale=None):
        def fn():
            kw = {}
            if bias is not None: kw["bias"] = ap(bias)
            if scale is not None: kw["scale"] = ap(scale)
            return [g.scalar.activation(ap(out), ap(in_), func, **kw)]
        add("S", fn, [in_, bias, scale], [out], FIXS + width(out) * (GAT if in_[0] == "ind" else 1.0) * CYC)

    def mm(items):
        cost = 20.0
        for o, l, r, a, b in items:
            cost += max(min(64, width(l)), width(r)) * PEC * (4 if SCRATCH[l[0]][2] == "float32" else 1)
        add("P", lambda: [g.tensor.matmul(ap(o), ap(l), ap(r), a, b) for o, l, r, a, b in items],
            [x[1] for x in items] + [x[2] for x in items], [x[0] for x in items], cost)

    def group(out, pairs, start=True, stop=True):
        mm([(out, l, r, start and n == 0, stop and n == len(pairs) - 1) for n, (l, r) in enumerate(pairs)])

    def iota(out, pattern, base, cm):
        small = SCRATCH[out[0]][2] != "int32"

        def fn():
            if small: return [g.iota(ap(out), pattern, base, cm, allow_small_or_imprecise_dtypes=True)]
            return [g.iota(ap(out), pattern, base, cm)]
        add("G", fn, [], [out], 150 + 2 * width(out) * CYC)

    def ind(win, off):
        return ("ind", win, off)

    def sel(r, nm="SW1"):
        return R(nm, 15 - r, 143 - r)

    ID, NID, ONE = R("ID"), R("NID"), R("ONE")
    rnd = [(R("IC"), ONE), (R("INC"), ONE)]

    add("Y", lambda: [g.sync.dma_start(ap(R("QI")), T.q[:]).then_inc(T.sem.lq, 16)], [], [R("QI")], 60, ("lq", 16), 1800)
    for k in range(4):
        q = g.sync if k % 2 == 0 else g.scalar
        add("Y" if k % 2 == 0 else "S",
            lambda q=q, k=k: [q.dma_start(ap(R("XT", 512 * k, 512 * k + 512)), T.x[:, 512 * k:512 * k + 512]).then_inc(T.sem["lx%d" % k], 16)],
            [], [R("XT", 512 * k, 512 * k + 512)], 60, ("lx%d" % k, 16), 2300 + 200 * k)

    pc, gc16, rc, gcol, r80, bjc, p4k, g43 = (R("PC", k, k + 1) for k in range(8))
    iota(R("PI", 0, 1), [[0, 1]], 0, 1)
    iota(R("CI"), [[1, 146]], 0, 0)
    iota(R("CR"), [[0, 8], [1, 16]], 0, 0)
    iota(R("CG"), [[1, 8], [0, 16]], 0, 0)
    iota(R("CQ"), [[1, 36], [0, 4]], 0, 0)
    cp(pc, R("PI", 0, 1))
    ts(R("PI", 1, 2), R("PI", 0, 1), 4, ALU.arith_shift_right)
    cp(gcol, R("PI", 1, 2))
    ts(R("G16"), R("CI", 0, 24), -8.0, ALU.add, gcol, ALU.is_equal)
    cp(R("QF"), R("QI"))
    for k in range(8):
        if k < 5: ts(R("QB", 16 * k, 16 * k + 16), R("QI"), R("G16", 8 + k, 9 + k), ALU.mult)
        else: act(R("QB", 16 * k, 16 * k + 16), R("QF"), ACT.Identity, None, R("G16", 8 + k, 9 + k))
    fill(ONE, 1.0)
    ts(R("PI", 2, 3), R("PI", 0, 1), 15, ALU.bitwise_and)
    cp(rc, R("PI", 2, 3))
    ts(R("E32"), R("CR", 0, 32), rc, ALU.is_equal)
    cp(R("G8B"), R("G16", 8, 16)); ts(R("G4"), R("G16"), 4.0, ALU.mult); act(R("G1"), R("G16"), ACT.Copy)
    ts(gc16, gcol, 16.0, ALU.mult, 15.0, ALU.add)
    ts(g43, gcol, 4.0, ALU.mult, 3.0, ALU.add)
    ts(p4k, pc, 4096.0, ALU.add)
    ts(r80, gcol, 256.0 - 37 * 16 % 256, ALU.mult)
    ts(R("PI", 3, 4), R("PI", 0, 1), 2, ALU.arith_shift_right, 3, ALU.bitwise_and)
    ts(R("PI", 4, 5), R("PI", 0, 1), 3, ALU.bitwise_and)
    ts(R("COL", 4, 5), R("PI", 3, 4), 37.0, ALU.mult)
    ts(bjc, R("PI", 4, 5), 64.0, ALU.mult, R("COL", 4, 5), ALU.add)
    act(R("KM"), R("CR", 0, 32), ACT.Identity, 3.0 / 128, 1.0 / 16)
    iota(R("QS", 0, 16), [[0, 16]], 0, 0); act(R("QS", 16, 32), R("QF"), ACT.Identity, None, 1.0 / 128)
    ts(R("BLKF"), R("CG"), gcol, ALU.is_equal)
    act(R("BLK"), R("BLKF"), ACT.Copy)
    ts(ID, R("CI", 0, 128), pc, ALU.is_equal)
    for nm, v in DIAG.items(): act(R(nm), ID, ACT.Identity, None, v)
    act(R("I785"), ID, ACT.Identity, None, -785.5); act(R("G8K"), R("G16", 8, 16), ACT.Identity, None, 2048.0)
    act(R("BP"), R("BLK"), ACT.Identity, None, 2048.0); act(R("BN"), R("BLK"), ACT.Identity, None, -2048.0)
    ts(R("COL", 6, 7), pc, -256.0, ALU.mult, -128.0, ALU.add)
    act(R("UU"), R("CI"), ACT.Sigmoid, R("COL", 6, 7), 256.0)
    for nm, d, op in (("TRI", 1, ALU.is_ge), ("TRU", -1, ALU.is_gt)):
        add("G", lambda nm=nm, d=d, op=op: [g.affine_select(ap(R(nm)), ap(R("BLK")), [[d, 128]], op, 0.0, 0, -d)], [R("BLK")], [R(nm)], 200 + 256 * CYC)
    ts(R("SW1"), R("CI", 0, 144), gc16, ALU.is_equal)
    act(R("SW16"), R("SW1"), ACT.Identity, None, 1.0 / 16)
    ts(R("SW4"), R("CQ"), g43, ALU.is_equal)
    for a in (0, 8): act(R("G82", a, a + 8), R("G16", 8, 16), ACT.Copy)
    ts(R("MK"), R("CR"), rc, ALU.is_equal)
    ts(R("JB"), R("MK"), p4k, ALU.mult, -4096.0, ALU.add)
    act(R("MN"), R("MK"), ACT.Identity, -8192.0, 8192.0)
    for a in (0, 128): act(R("DM", a, a + 128), R("MK"), ACT.Identity, None, 256.0)
    ts(R("COL", 5, 6), rc, 4.0, ALU.mult, 4640.0, ALU.add)
    ts(R("JS", 0, 1), rc, 0.0, ALU.is_gt, R("COL", 5, 6), ALU.mult)
    act(R("TM255"), ONE, ACT.Identity, None, -255.0)
    cp(R("QH", 0, 128), R("CI", 0, 128))
    for a in (128, 256, 512, 1024):
        b = min(2 * a, NH); ts(R("QH", a, b), R("QH", 0, b - a), float(a), ALU.add)
    cp(R("CIB"), R("QH", 0, 256))

    def late_constants():
        for r in (R("XA", 2 * W, ZS), R("XB", 2 * W, ZS), R("Z", K, K + 16)): iota(r, [[0, 16]], 0, 0)
        for r in (R("W3", 128, 136), R("W3", 264, 272), R("W35", 256, 264)): iota(r, [[0, 8]], int(BIG), 0)
        iota(R("ICX"), [[0, 128]], 0, 0)
        for k in range(3):
            add("G", lambda k=k: [g.affine_select(ap(R("ICX")), ap(R("ICX")), [[0, 128]], ALU.not_equal, 255.0 * 2 ** (31 - 8 * k), -k, 1)],
                [R("ICX")], [R("ICX")], 200 + 256 * CYC)

    def round_constants(t):
        iota(R("TF", 128, 144), [[37 * 16, 16]], t, 37)
        ts(R("TI", 128, 144), R("TF", 128, 144), r80, ALU.add)
        ts(R("TJ", 128, 144), R("TI", 128, 144), 255, ALU.bitwise_and)
        cp(R("PM%d" % t), R("TJ", 128, 144))
        iota(R("TF", 0, 128), [[148, 128]], t, 0)
        ts(R("TI", 0, 128), R("TF", 0, 128), bjc, ALU.add)
        ts(R("TJ", 0, 128), R("TI", 0, 128), 255, ALU.bitwise_and)
        ts(R("J5%d" % t), R("TJ", 0, 128), 5.0, ALU.mult, 239.0, ALU.add)
        if t == 0:
            group(R("B5", 0, 128), [(R("TM255"), R("QB"))])
            for a in range(0, 512, 128): act(R("QT", a, a + 128), R("B5", 0, 128), ACT.Identity, None, -1.0)
            iota(R("TT"), [[16, 128]], 1 + X1 - ZS, 0)
            ts(R("PL"), R("TT"), rc, ALU.add)

    def starts(tb, jb, src, a, col, bias, scalar, less=False):
        group(jb, [(ID, R("JB"))], True, False)
        if scalar or less: group(tb, [(ID, R("MN")) if scalar else (R("BN"), R("MK"))], True, False)
        group(jb, [(R(src, a, a + 128), R("BP")), (R(src, a + 1, a + 129), R("BN"))], False, True)
        group(tb, [(R(src, a, a + 128), R("BLK"))], not (scalar or less), True)
        if scalar: act(R("L1", col, col + 128), tb, ACT.Relu)
        else: tt(R("L1", col, col + 128), tb, R("MK"), ALU.mult)
        act(R("L2", col, col + 128), jb, ACT.Relu, bias)

    def places(win, a, u, banks, scalar):
        c = 128 * u; o, e = R(banks[0], 128, 138), R(banks[0], 136, 137)
        starts(R(banks[0], 0, 128), R(banks[1], 0, 128), "AS", a, c, 520.0, scalar)
        mm([(o, R("L1", c, c + 128), R("G1", 8, 18), True, False), (o, R("L2", c, c + 128), R("G4", 8, 18), False, False),
            (e, sel(0), R("AS", a + 144, a + 145), False, False), (e, ID, R("JS", 0, 1), False, True)])
        cp(R("SC", 10 * u, 10 * u + 10), o)
        scatter(R(win), R("SC", 10 * u, 10 * u + 9), R("CIB", 0, 144))
        group(R(banks[2], 0, 128), [(R("TRI"), R("AS", a + 1, a + 129)), (R("TRU"), R("AS", a, a + 128))])
        act(R("W3", 136 * u, 136 * u + 128), R(banks[2], 0, 128), ACT.Copy)

    def marks(win, c0, c1, z=0):
        w = R(win, 16 * (c0 - z), 16 * (c1 - z))
        scan(R("BL", 16 * c0, 16 * c1), w, w, R("BL", 16 * c0 - 1, 16 * c0) if c0 > z else 0.0, ALU.max, ALU.max)

    def blocks(bank, c0, c1):
        group(R(bank, 0, c1 - c0), [(sel(r, "SW16"), R("BL", 16 * c0 + r, 16 * c1, 16)) for r in range(16)])
        cp(R("SO", c0, c1), R(bank, 0, c1 - c0)); act(R("SB", c0, c1), R(bank, 0, c1 - c0), ACT.Identity, None, -1.0)

    def pick(c0):
        scan(R("G0"), R("DM"), R("BL", 16 * c0, 16 * c0 + CAP), 0.0, ALU.add, ALU.min)
        cp(R("SO", c0, c0 + 16), R("G0", 15, CAP, 16)); act(R("SB", c0, c0 + 16), R("G0", 15, CAP, 16), ACT.Identity, None, -1.0)

    def within(bank, w3, c0, c1, ns, sub, z=0):
        h = (c1 - ns + 1) // 2 * 2 if ns else c1; ns = c1 - h
        if ns:
            act(R("SH", 16 * h, 16 * c1), ind(w3, R("SO", h, c1)), ACT.Copy)
            group(R(sub, 0, 16 * ns), [(ID, R("QH", 16 * h, 16 * c1)), (NID, R("SH", 16 * h, 16 * c1))])
            act(R("SF", 16 * h, 16 * c1), R(sub, 0, 16 * ns), ACT.Sigmoid, 128.0, 256.0)
        if h > c0: tt(R("SF", 16 * c0, 16 * h), ind(w3, R("SO", c0, h)), R("QH", 16 * (c0 - z), 16 * (h - z)), ALU.is_le)
        group(R(bank, 0, c1 - c0), [(R("IN16"), R("SB", c0, c1))] + [(sel(r), R("SF", 16 * c0 + r, 16 * c1, 16)) for r in range(16)])
        cp(R("SP", c0, c1), R(bank, 0, c1 - c0))

    def flags(t, bank, u0, u1, scalar, later=False):
        items = []; nm = ("NZ", "NC", "NK")[t]
        for u in range(u0, u1):
            o = R(bank, 128 * (u - u0), 128 * (u - u0) + 128); z = R("Z", W * (u // 16) + u % 16, W * (u // 16) + W, 16)
            if t == 0: items.append((o, R("XT", 128 * u, 128 * u + 128), R("QB"), True, True))
            elif t == 2: items.append((o, R("XT", u, W, 16), R("QB"), True, True))
            else: items += [(o, R("TM255"), R("QB"), True, False)] * (scalar > 0) + [(o, z, R("QB"), not scalar, True)]
        mm(items)
        nz, pb = R(nm, 128 * u0, 128 * u1), R(bank, 0, 128 * (u1 - u0))

        def flag():
            if scalar:
                sg = R("NZ2", 512 * (u0 // 4 % 2), 512 * (u0 // 4 % 2) + width(nz))
                act(sg, pb, ACT.Sign)
                if scalar == 2: ts(nz, sg, 0.0, ALU.not_equal)
                else: act(nz, sg, ACT.Square)
            elif t == 1: tt(nz, pb, R("QT", 0, width(nz)), ALU.not_equal)
            else: ts(nz, pb, 0.0, ALU.not_equal)
        if later: return flag
        flag()

    others = [r for r in range(NR) if r != rank]
    for k in range(4): flags(0, "B%d" % k, 4 * k, 4 * k + 4, F0[k])
    for k in range(4):
        group(R("B7", 0, 2), [(R("NZ", 128 * u, 128 * u + 128), R("ONE", 0, 2)) for u in range(4 * O0[k], 4 * O0[k] + 4)], k == 0, k == 3)
    for t in range(2):
        LD, GE, XR = "LD%d" % t, "GE%d" % t, ("XA", "XB")[t]
        mine, slots = (R(LD, 8 * rank, 8 * rank + 8), R(LD)) if t else (R(LD, 8 * rank, 8 * rank + 2), R(LD, 0, 64, 8))
        if t == 0: cp(mine, R("B7", 0, 2))
        else: tt(mine, R("B2", 0, 8), R("G16", 8, 16), ALU.mult)

        def send_counts(t=t, mine=mine):
            ids = []; m = None
            for r in others:
                rid, pid = topo.addr(T.cores[r], core); ids.append(DstId(rid=rid, pnc=pid))
                mk = topo.mask(core, T.cores[r]); m = mk if m is None else m & mk
            return [g.remote_dma_fused([RemoteDMATransfer(dst_ids=ids, dma_engine_mask=m, remote_sem=T.sem["ca%d" % t], src=ap(mine),
                                                          dsts=[ap(mine)] * len(ids))], local_sem=T.sem["cl%d" % t])]
        ne = len(topo.engines(core, T.cores[others[0]]))
        add("G", send_counts, [R(LD)], [R("COL", 8 + t, 9 + t)], 300, ("cl%d" % t, ne), GL)
        sent = len(ops) - 1
        add("A", None, [R("COL", 8 + t, 9 + t)], [R(LD)], 0, ("ca%d" % t, ne * len(others)), LC[t])
        if t == 0: round_constants(0)
        after[0] = sent
        if t == 0: round_constants(1)
        for nm, n in (("WN", CAP), ("WP", MP), ("WS", NH)): iota(R(nm, 0, n), [[0, n]], 0, 0)
        if t == 0:
            late_constants()
            for k in range(4): flags(2, "B%d" % k, 4 * k, 4 * k + 4, F2[k])
        after[0] = None
        if t == 0:
            for k in range(4): ts(R(XR, X1 + 512 * k, X1 + 512 * k + 512), R("XT", 512 * k, 512 * k + 512), -1.0, ALU.mult, 255.0, ALU.add)
        add("Y", lambda XR=XR, t=t: [g.sync.dma_start(ap(R(XR, 0, W)), ap(R(XR, X1, X1 + W))).then_inc(T.sem["xc%d" % t], 16)],
            [R(XR, X1, X1 + W)], [R(XR, 0, W)], 60, ("xc%d" % t, 16), 4000)
        AO = AN
        mn0, mn1, coef = R("COL", 0, 1), R("COL", 1, 2), R("COL", 2, 3)
        group(R("B4", 0, 32), [(ID, R("KM")), (ID, R("QS"))] + [(R("IC"), R("US"))] * t, True, False)
        red(R("COL", 3, 4), slots, ALU.add)
        ts(R("KD"), R("E32"), R("COL", 3, 4), ALU.mult)
        group(R("B4", 0, 32), [(R("BLKF"), R("KD"))], False, True)
        red(mn0, R("B4", 0, 16), ALU.min); red(mn1, R("B4", 16, 32), ALU.min)
        ts(coef, mn1, mn0, ALU.subtract, 128.0, ALU.mult)
        ts(R("C16"), R("G82"), coef, ALU.mult)
        if t == 0: ts(R("US"), R("B4", 0, 32), mn0, ALU.subtract, 1.0 / 32, ALU.is_lt)
        act(R("CB"), R("BLK"), ACT.Identity, None, coef); act(R("CBS"), R("SW4"), ACT.Identity, None, coef)
        if t == 0: mm([(R("B5", r, 128, 16), R("XT", r, W, 16), R("C16", 0, 8), True, True) for r in range(16)])
        else:
            mm([(R("B5", r, 128, 16), R(XR, X1 + r, X1 + W, 16), R("C16", 0, 8), r == 0, False) for r in range(16)])
            group(R("B5", 0, 128), [(R("TM255"), R("CB"))], False, True)
        win = R(XR, X1, ZS)
        ts(R("FS", 128, 256), R("B5", 0, 128), 0.0, ALU.is_gt if t else ALU.is_lt)
        act(R("FS", 0, 128), R("B5", 0, 128), ACT.Sigmoid, -128.0, -256.0 if t else 256.0)
        group(R("B6", 0, 146), [(R("FS", 128, 256), R("UU"))]); group(R("B7", 0, 146), [(R("FS", 0, 128), R("UU"))])
        cp(R("AS", AN, AN + 146), R("B6", 0, 146)); act(R("AS", 0, 146), R("B7", 0, 146), ACT.Copy)
        places("WN", AN, 1, ("B0", "B1", "B6"), False)
        marks("WN", 64, 80, 64)
        pick(64)
        within("B4", R("W3", 136, 272), 64, 80, 0, None, 64)
        u, v = GV
        if u: ts(R("G0", 0, 16 * u), ind(win, R("SP", 64, 64 + u)), -255.0, ALU.add)
        if u < 16: act(R("G0", 16 * u, CAP), ind(win, R("SP", 64 + u, 80)), ACT.Identity, -255.0)
        if v: cp(R("GN", 0, 16 * v), ind(R("G0"), R("PM%d" % t, 0, v)))
        if v < 16: act(R("GN", 16 * v, CAP), ind(R("G0"), R("PM%d" % t, v, 16)), ACT.Copy)
        partner = T.cores[rank ^ XS[t]]

        def send_guests(t=t, GE=GE, partner=partner):
            rid, pid = topo.addr(partner, core)
            return [g.remote_dma(ap(R(GE, 0, CAP)), ap(R("GN")), T.sem["ga%d" % t], T.sem["gl%d" % t], pid, rid, topo.mask(core, partner))]
        ne = len(topo.engines(core, partner))
        add("G", send_guests, [R("GN")], [R("COL", 10 + t, 11 + t)], 300, ("gl%d" % t, ne), GL)
        add("A", None, [R("COL", 10 + t, 11 + t)], [R(GE, 0, CAP)], 0, ("ga%d" % t, ne), LG)
        add("Y", lambda GE=GE, t=t: [g.sync.dma_start(ap(R(GE, a, a + CAP)), ap(R(GE, 0, CAP))).then_inc(T.sem["ge%d" % t], 16) for a in (CAP, 2 * CAP)],
            [R(GE, 0, CAP)], [R(GE, CAP, 3 * CAP)], 120, ("ge%d" % t, 32), 2500)
        places("WP", 0, 0, ("B2", "B3", "B7"), LS)
        for s in range(2):
            marks("WP", 32 * s, 32 * s + 32); blocks("B%d" % s, 32 * s, 32 * s + 32)
        for s in range(2):
            c = 128 * s; pbk = R("B%d" % (5 + s), 0, 128); ab = R("B7" if s else "B3", 0, 128); a = R("AP", c, c + 128)
            group(ab, [(R("SW4", 12 - 4 * q, 140 - 4 * q), R("BL", 512 * s + q, 512 * s + 512, 4)) for q in range(4)], True, False)
            within("B%d" % s, R("W3", 0, 136), 32 * s, 32 * s + 32, PS[s], "B2")
            u, v, w = 32 * s, 32 * s + PV[t][s], 32 * s + 32
            if v > u: cp(R("PRS", 16 * u, 16 * v), ind(win, R("SP", u, v)))
            if w > v: act(R("PRS", 16 * v, 16 * w), ind(win, R("SP", v, w)), ACT.Copy)
            group(ab, [(R("SW4", 12 - 4 * q, 140 - 4 * q), R("SF", 512 * s + q, 512 * s + 512, 4)) for q in range(4)], False, True)
            if AS_[s]: act(a, ab, ACT.Identity, -2048.0)
            else: ts(a, ab, -2048.0, ALU.add)
            group(pbk, [(R("I785"), ONE), (NID, R("J5%d" % t)), (R("IN16"), a)] + rnd + [(ID, R("J5%d" % t)), (R("I17"), a)])
        group(R("B2", 0, 128), [(R("TRI"), R("AS", AO + 1, AO + 129)), (R("TRU"), R("AS", AO, AO + 128)), (R("IK"), ONE),
                                (R("INK"), R("AS", AO + 1, AO + 129)), (R("IK"), R("AS", AO, AO + 128))])
        act(R("KEY"), R("B2", 0, 128), ACT.Copy)
        if t == 0:
            group(R("B2", 128, 129), [(R("BLK"), R("AS", AO + 144, AO + 145))]); act(R("T5", 0, 1), R("B2", 128, 129), ACT.Copy)
            act(R("DN"), NID, ACT.Identity, None, R("T5", 0, 1))
        for s in range(2):
            nv = ZV[t][s]; pv = R(("B4", "B7")[s], 0, nv)
            if nv:
                group(pv, [(ID, R("PRS", 512 * s, 512 * s + nv))])
                for kk in range(4):
                    h = min(nv, CAP - 64 * kk)
                    tt(R("Z", W * s + kk, W * s + 4 * h, 4), R(pv[0], 0, h), R(GE, 64 * kk, 64 * kk + h), ALU.add)
                    if h < nv: tt(R("Z", W * s + 4 * h + kk, W * s + 4 * nv, 4), R(pv[0], h, nv), R(GE, 0, nv - h), ALU.add)
        pieces = [(i, min(128, 512 * s + 512 - i)) for s in range(2) for i in range(512 * s + ZV[t][s], 512 * s + 512, 128)]
        for u, (i, m) in enumerate(pieces):
            bank = ZB[t][u]
            mm([(R(bank, kk, 4 * m, 4), ID, R("PRS", i, i + m), kk == 0, False) for kk in range(4)])
            items = []
            for kk in range(4):
                a = (i + 64 * kk) % CAP; h = min(m, CAP - a)
                items += [(R(bank, kk, 4 * h, 4), ID, R(GE, a, a + h), False, False)]
                if h < m: items += [(R(bank, 4 * h + kk, 4 * m, 4), ID, R(GE, 0, m - h), False, False)]
            mm(items[:-1] + [items[-1][:4] + (True,)])
            if ZC[t][u] == "V": ts(R("Z", 4 * i, 4 * (i + m)), R(bank, 0, 4 * m), 0.0, ALU.max)
            else: act(R("Z", 4 * i, 4 * (i + m)), R(bank, 0, 4 * m), ACT.Relu)
        xw = R(XR, 0, 2 * W)
        tal = (R("B7", 0, 128), R("B4", 0, 128))

        def part(n, s):
            c = 256 * n + 128 * s
            return R("B%d" % (5 + s), 0, 128), R("ST", c, c + 128), R("FF", c, c + 128), R("AP", 128 * s, 128 * s + 128)

        def counts(s):
            mm([(R("B3", 128 * s + r, 128 * s + 128, 16), R("FL", W * s + r, W * s + W, 16), R("G8B"), True, True) for r in range(16)])

        def relu(n, s):
            act(part(n, s)[2], R("B3", 128 * s, 128 * s + 128), ACT.Relu, -16.0, 129.0)

        def state(n, s):
            ts(part(n, s)[1], R("OF", 128 * s, 128 * s + 128), -2048.0, ALU.add)

        def tally(n, s):
            _, st, f, a = part(n, s)
            group(tal[s], [(R("I8S"), ONE)] * (n == 0) + [(st, NID), (a, ID), (R("I19"), f), (R("ICX"), ONE), (R("IN39"), ONE)], n == 0, False)

        def shares(k):
            MV, m1 = MK_.get((t, k), (MF, M1F) if t == 0 and k in FT else (MV0, M1))
            return MV, (0, m1, 128 - MV)

        def offsets(k):
            ts(R("OF", 128 * (k % 2), 128 * (k % 2) + 128), part(0, k % 2)[0], 3857.0, ALU.add)

        def gather(k, h):
            MV, cut = shares(k); s = k % 2; c = 128 * s + MV
            act(R("GS", NS * s + 16 * cut[h], NS * s + 16 * cut[h + 1]), ind(xw, R("OF", c + cut[h], c + cut[h + 1])), ACT.Copy)

        sums = [[(R("B2", 128 * v, 128 * v + 128), R("TM255"), R("CB"), v == 0, False) for v in range(2)]]
        sums += [[(R("B2", 128 * v, 128 * v + 128), R("PRS", 512 * v + u, 512 * v + 512, 4), R("CBS", 12 - 4 * u, 140 - 4 * u), False, False)
                  for v in range(2)] for u in range(4)]
        sums += [[(R("B2", 4 * u + kk, 256, 16), R(GE, u + 64 * kk, u + 64 * kk + 509, 4), R("C16"), False, u == 3 and kk == 3)
                  for kk in range(4)] for u in range(4)]
        chain[0] = True
        for k in range(2 * PR):
            n, s = k // 2, k % 2; pn, ps = (k - 1) // 2, (k - 1) % 2
            c, e = 128 * s, W * s
            fl = t == 0 and k in FT
            MV, cut = shares(k); cut = (0, min(cut[1], 32), cut[2])
            gs = [R("GS", NS * s + 16 * cut[h], NS * s + 16 * cut[h + 1]) for h in range(2)]
            zs = [(e + 16 * (MV + cut[h]), e + 16 * (MV + cut[h + 1])) for h in range(2)]
            bk = [R("B%d" % h, 0, 16 * (cut[h + 1] - cut[h])) for h in range(2)]
            offsets(k)
            if 0 < k < 2 * PR - 1: state(pn, ps)
            if n == PR - 1: state(n, s)
            mm([(bk[0], ID, R("Z", *zs[0]), True, False)])
            more = k > 0 and pn < PR - 1
            if more: counts(ps)
            if more: group(part(pn, ps)[0], [(R("I785"), ONE), (ID, part(pn, ps)[3]), (R("IN5"), part(pn, ps)[1])], True, False)
            mm([(bk[1], ID, R("Z", *zs[1]), True, False)])
            if fl: flag = flags(1, "B2", 4 * FT.index(k), 4 * FT.index(k) + 4, False, True)
            gather(k, 0)
            if more: relu(pn, ps)
            mm([(bk[0], NID, gs[0], False, True)])
            if more:
                pb, pst, pf, _ = part(pn, ps)
                group(pb, [(pf, R("IN113"))] + rnd + [(pf, R("I113")), (R("I5"), pst)], False, True)
            gather(k, 1)
            mm([(bk[1], NID, gs[1], False, True)])
            cuts = list(zip((0,) + TS.get((t, k), ()), TS.get((t, k), ()) + (MV,)))
            for u, v in cuts[1:] + cuts[:1] if k == 2 * PR - 1 else cuts:
                tt(R("FL", e + 16 * u, e + 16 * v), ind(xw, R("OF", c + u, c + v)), R("Z", e + 16 * u, e + 16 * v), ALU.is_lt)
            if fl: flag()
            for h in range(2):
                act(R("FL", *zs[h]), bk[h], ACT.Sigmoid, -128.0, 256.0)
            if more: tally(pn, ps)
            if k in SK[t][:-1]: mm([x for u in range(9) if SK[t][u] == k for x in sums[u]])
            if k == SK[t][-1]: act(R("SG"), R("B2", 0, 256), ACT.Sign, 0.5, -1.0)
        chain[0] = False
        if t == 0:
            for u in range(len(FT), 8): flags(1, FB[u - len(FT)], 4 * u, 4 * u + 4, FL8[u - len(FT)])
        for s in range(2):
            c = 128 * s; last = "B%d" % (5 + s); al = R("AL", c, c + 128)
            group(tal[s], [(part(PR - 1, s)[1], NID), (part(PR - 1, s)[3], ID), (R("IHS"), R("SG", c, c + 128))], False, False)
            for u, v in CM if s else ((0, 128),):
                mm([(R(tal[s][0], r, 128, 16) + (u, v), R("FL", W * s + 16 * u + r, W * s + 16 * v, 16), R("G8K"), False, r == 15)
                    for r in range(16)])
            es = ES[t][s]
            if es[0]: act(al, tal[s], ACT.Sigmoid, -256 * 8.5 * SV + 128, 256.0)
            else: ts(al, tal[s], 8.5 * SV - 0.5, ALU.is_gt)
            pre = R(("B7", "B6")[s], s, 129)
            if s: group(pre, [(R("AL", 0, 128), ONE)], True, False)
            group(pre, [(al, R("UU", s, 129))], not s, True)
            if es[1]: act(R("A5", 15 + s + c, 144 + c), pre, ACT.Copy)
            else: cp(R("A5", 15 + s + c, 144 + c), pre)
            starts(R(("B3", "B0")[s], 0, 128), R(("B5", "B1")[s], 0, 128), "A5", 15 + c, c, 1030.0 + c, es[2] and not s, s)
            if t == 0:
                lm = R(("B7", "B4")[s], 256, 384)
                group(lm, [(ONE, R("DN")), (R("INK"), al)], True, False)
                group(lm, [(R("A5", 16 + c, 144 + c), R("TRI")), (R("A5", 15 + c, 143 + c), R("TRU"))], False, True)
                if es[3]: act(R("LM", c, c + 128), lm, ACT.Sigmoid, -256 * 8191.5, -256.0)
                else: ts(R("LM", c, c + 128), lm, -8191.5, ALU.is_lt)
                group(R("B2", 0, 8), [(R("NC", 16 * c + 128 * r, 16 * c + 128 * r + 128), R("LM", c + r, c + 128, 16)) for r in range(16)], s == 0, False)
            group(R(last, 0, 8), [(R("L1", c, c + 128), R("G1", 8, 16)), (R("L2", c, c + 128), R("G4", 8, 16))])
            ts(R("SC", 8 * s, 8 * s + 8), R(last, 0, 8), 2048.0 * s, ALU.add)
            scatter(R("WS"), R("SC", 8 * s, 8 * s + 8), R("CIB", c, c + 128))
        group(R("B3", 0, 256), [(R("TRI"), R("A5", 16, 272)), (R("TRU"), R("A5", 15, 271))])
        act(R("W35", 0, 256), R("B3", 0, 256), ACT.Copy)
        group(R("B7", 0, 1), [(R("BLK"), R("A5", 271, 272))])
        if t == 0: ts(R("KP"), R("KEY"), R("B7", 0, 1), ALU.is_gt)
        if TKS[t]:
            act(R("T5", 1, 2), R("B7", 0, 1), ACT.Identity, None, -1.0); act(R("TK"), R("KEY"), ACT.Relu, R("T5", 1, 2))
        else: ts(R("TK"), R("KEY"), R("B7", 0, 1), ALU.subtract, 0.0, ALU.max)
        if t == 0:
            group(R("B0", 0, 128), [(R("KP"), ID)]); act(R("KT"), R("B0", 0, 128), ACT.Copy)
            group(R("B2", 0, 8), [(R("NK", 128 * r, 128 * r + 128), R("KT", r, 128, 16)) for r in range(16)], False, True)

        def sources(bank):
            group(R(bank, 0, 128), [(ID, R("KEY")), (R("INK"), R("TK"))])
            tt(R("TT"), R(bank, 0, 128), R("PL"), ALU.max)
            ts(R("FO"), R("TT"), float(ZS - X1 - 1), ALU.add)
        sources("B7")
        hb, hc = HB[t], HC[t]
        for u in range(len(hb) - 1):
            marks("WS", hb[u], hb[u + 1])
            if hb[u + 1] - hb[u] > 16: blocks("B%d" % (4 + u), hb[u], hb[u + 1])
            else: pick(hb[u])
        for u in range(len(hc) - 1):
            within("B%d" % (4 + u % 3), R("W35"), hc[u], hc[u + 1], SS[t][u], "B%d" % (u % 2))
            a, h, b = hc[u], min(hc[u] + CV[t][u], hc[u + 1]), hc[u + 1]
            if h > a: ts(R(XR, ZS + 16 * a, ZS + 16 * h), ind(R("Z"), R("SP", a, h)), 0.0, ALU.max)
            if b > h: act(R(XR, ZS + 16 * h, ZS + 16 * b), ind(R("Z"), R("SP", h, b)), ACT.Relu)
        for k, (u0, u1) in enumerate(FP[t]):
            src = ind(R(XR, X1, ZS + min(128 * u1, NH)), R("FO", 8 * u0, 8 * u1))
            if t == 0:
                o = R("XB", X1 + 128 * u0, X1 + 128 * u1)
                if k in FV[t]: cp(o, src)
                else: act(o, src, ACT.Copy)
            else:
                o = R("XT", 128 * u0, 128 * u1)
                if k in FV[t]: ts(o, src, -1.0, ALU.mult, 255.0, ALU.add)
                else: act(o, src, ACT.Identity, 255.0, -1.0)
                add("Y", lambda k=k, o=o: [g.sync.dma_start(T.y[:, o[1]:o[2]], ap(o)).then_inc(T.sem["y%d" % k], 16)],
                    [o], [], 60, ("y%d" % k, 16), 2000)
    return ops


def depend(ops):
    hist = {}; before = {}; deps = []
    for i, o in enumerate(ops):
        d = set()
        for kind, rs in (("r", o["r"]), ("w", o["w"])):
            for r in rs:
                psum = SCRATCH[r[0]][0] == "psum"
                if psum and hist.get(r[0]) and ops[hist[r[0]][-1][0]]["e"] == o["e"]: d.update(before.get(r[0], ()))
                for j, kj, a, b, step in hist.get(r[0], ()):
                    clash = (kind == "w" or kj == "w") and a < r[2] and r[1] < b and not (step == r[3] == 4 and (a - r[1]) % 4)
                    if clash or (psum and (ops[j]["e"] != o["e"] or o["e"] == "P")): d.add(j)
        for kind, rs in (("r", o["r"]), ("w", o["w"])):
            for r in rs:
                h = hist.setdefault(r[0], [])
                if SCRATCH[r[0]][0] == "psum":
                    if h and ops[h[-1][0]]["e"] != o["e"]:
                        before[r[0]] = [x[0] for x in h]; del h[:]
                elif kind == "w" and r[3] == 1: h[:] = [x for x in h if not (r[1] <= x[2] and x[3] <= r[2])]
                h.append((i, kind, r[1], r[2], r[3]))
        d.discard(i)
        deps.append(d)
    return deps


def arrange(ops, hard):
    n = len(ops); deps = [{} for _ in ops]; succ = [{} for _ in ops]; prev = {}
    for i, o in enumerate(ops):
        for j in hard[i]:
            deps[i][j] = ops[j]["lat"] + (HOP if ops[j]["e"] != o["e"] else 0.0 if o["e"] == "P" else SELF)
        if o["after"] is not None: deps[i].setdefault(o["after"], 0.0)
        if o["chain"]:
            if o["e"] in prev: deps[i].setdefault(prev[o["e"]], 0.0)
            prev[o["e"]] = i
        for j, v in deps[i].items(): succ[j][i] = v

    def lay(keys, before, first):
        busy = {}; end = [0.0] * n
        for i in sorted(range(n), key=lambda i: keys[i]):
            s = max([end[j] + v for j, v in before[i].items()] + [first[i]]); c = ops[i]["c"]
            b = busy.setdefault(ops[i]["e"], []); x, hi = 0, len(b)
            while x < hi:
                if b[(x + hi) // 2][0] <= s: x = (x + hi) // 2 + 1
                else: hi = (x + hi) // 2
            if x and b[x - 1][1] > s: s = b[x - 1][1]
            while x < len(b) and s + c > b[x][0]:
                s = b[x][1]; x += 1
            b.insert(x, (s, s + c)); end[i] = s + c
        return end
    zero = [0.0] * n; tail = [o["lat"] for o in ops]; seed = [1]

    def passes(key):
        end = lay([(-key[i], i) for i in range(n)], deps, zero)
        back = lay([(-end[i], -i) for i in range(n)], succ, tail)
        end = lay([(-back[i], i) for i in range(n)], deps, zero)
        return max(end[i] + tail[i] for i in range(n)), end, back

    def draw(m):
        seed[0] = (seed[0] * 1103515245 + 12345) % 2 ** 31
        return (seed[0] >> 8) % m
    pri = [0.0] * n
    for i in range(n - 1, -1, -1):
        pri[i] = ops[i]["c"] + max([pri[x] + v for x, v in succ[i].items()] + [tail[i]])
    def waits(end):
        ahead = {}; last = {}; out = []
        for i in sorted(range(n), key=lambda i: end[i]):
            ahead[i] = last.get(ops[i]["e"]); last[ops[i]["e"]] = i
        i = max(range(n), key=lambda i: end[i] + tail[i])
        while i is not None:
            s = end[i] - ops[i]["c"]; by = [j for j, v in deps[i].items() if end[j] + v > s - 1e-6]
            if by: i = by[draw(len(by))]
            elif s > 1e-6:
                if not (ops[i]["chain"] and ops[ahead[i]]["chain"]) and ahead[i] not in deps[i]: out.append((i, ahead[i]))
                i = ahead[i]
            else: i = None
        return out
    cases = []
    for gat, far, late in CASES:
        c = [o["c"] + o["n"] * (gat - GAT) for o in ops]
        cases.append((c, [[(j, (v - ops[j]["lat"]) * far + ops[j]["lat"] * late) for j, v in deps[i].items()] for i in range(n)]))

    def worth(end):
        order = sorted(range(n), key=lambda i: (end[i] - ops[i]["c"], end[i], i)); out = max(end[i] + tail[i] for i in range(n))
        for c, before in cases:
            free = {}; e2 = [0.0] * n
            for i in order:
                s = free.get(ops[i]["e"], 0.0)
                for j, v in before[i]:
                    if e2[j] + v > s: s = e2[j] + v
                e2[i] = free[ops[i]["e"]] = s + c[i]
            out += max(e2[i] + tail[i] for i in range(n))
        return out / (1 + len(cases))
    total, end, back = passes(pri); total = worth(end); best = (total, end); held = waits(end)
    for k in range(TRIES):
        key = [ops[i]["c"] - end[i] for i in range(n)]
        for u in range(1 + draw(2)):
            i, j = held[draw(len(held))]
            if draw(3) == 0:
                near = [x for x in range(n) if not ops[x]["chain"] and abs(end[x] - end[i]) < 2000]
                for v in range(3): key[near[draw(len(near))]] += draw(2000)
            elif draw(2): key[i] = max(key[i], key[j] + 1 + draw(600))
            else:
                key[j] = min(key[j], key[i] - 1 - draw(600))
                for x in range(j, n):
                    for y in deps[x]:
                        if key[x] >= key[y]: key[x] = key[y] - 1e-3
        for x in range(n - 1, -1, -1):
            for y in succ[x]:
                if key[x] <= key[y]: key[x] = key[y] + 1e-3
        if draw(4): e2 = lay([(-key[x], x) for x in range(n)], deps, zero)
        else: e2 = passes(key)[1]
        r = worth(e2)
        if r <= total + SLACK * (1 - k / TRIES):
            total, end = r, e2; held = waits(end)
            if r < best[0]: best = (r, e2)
    end = best[1]; PLAN["worth"] = best[0]
    return sorted(range(n), key=lambda i: (end[i] - ops[i]["c"], end[i], i))


def order_all(ops):
    of = [i for i, o in enumerate(ops) if o["chain"] and o["w"][0][0] == "OF"]; n = len(of) // 2
    cuts = [0, of[3], of[n - 4], of[n + 3], of[2 * n - 4], len(ops)]; order = []
    for k in range(5):
        a, b = cuts[k], cuts[k + 1]
        if k % 2: order += range(a, b)
        else:
            part = [dict(o, after=None if o["after"] is None or o["after"] < a else o["after"] - a) for o in ops[a:b]]
            order += [a + i for i in arrange(part, depend(part))]
    return order


def rank_program(g, core, T, topo):
    if T.rank_of(core) is None:
        return
    ops = build(g, core, T, topo)
    if "deps" not in PLAN:
        PLAN["deps"] = depend(ops)
        PLAN["order"] = order_all(ops)
    deps = PLAN["deps"]
    queue = {"V": g.vector, "S": g.scalar, "P": g.tensor, "G": g, "Y": g.sync}
    count = {}; known = {e: {} for e in queue}; token = {}; clock = {}
    for i in PLAN["order"]:
        o = ops[i]; e = o["e"]
        if e == "A":
            token[i] = o["tok"]; clock[i] = {}; count[o["tok"][0]] = o["tok"][1]
            continue
        kn = known[e]
        for j in sorted((j for j in deps[i] if not (e == "P" and ops[j]["e"] == "P")), key=lambda j: -token[j][1]):
            s, v = token[j]
            if kn.get(s, 0) < v:
                queue[e].wait_ge(T.sem[s], v); kn[s] = v
            for s2, v2 in clock[j].items():
                if kn.get(s2, 0) < v2: kn[s2] = v2
        ins = o["f"]()
        if o["tok"] is None:
            s = "s" + e
            for x in ins:
                x.then_inc(T.sem[s], 1); count[s] = count.get(s, 0) + 1
            token[i] = (s, count[s])
        else:
            token[i] = o["tok"]; count[o["tok"][0]] = o["tok"][1]
        clock[i] = dict(kn)
    for s, v in count.items():
        g.wait_ge(T.sem[s], v)
